import numpy as np
import ml_dtypes


def mxq(x, axis, fmt="e4m3"):
    dtype, down = {"e4m3": (ml_dtypes.float8_e4m3fn, 7), "e5m2": (ml_dtypes.float8_e5m2, 14)}[fmt]
    v = np.moveaxis(np.asarray(x, np.float32).astype(ml_dtypes.bfloat16).astype(np.float64), axis, -1)
    blocks = v.reshape(v.shape[:-1] + (-1, 32))
    amax = np.abs(blocks).max(-1, keepdims=True)
    byte = np.maximum(np.where(amax > 0, np.frexp(amax)[1] - 1 + 127, 0) - down, 1)
    scale = np.exp2(byte - 127.0)
    codes = (blocks / scale).astype(np.float32).astype(dtype).astype(np.float64)
    return np.moveaxis((codes * scale).reshape(v.shape), -1, axis)


WIDE = False


def mx_kscale(k):
    if not WIDE:
        return np.ones(k)
    levels = np.array([10, -10, 5, -5, 0])
    if k % 512:
        return np.exp2(np.random.permutation(np.resize(levels, k // 32))).repeat(32)
    a = np.empty((k // 512, 16))
    for p in range(k // 512):
        a[p, :8] = np.random.permutation(np.resize(levels, 8))
        for g in range(8):
            far = levels[np.abs(levels - a[p, g]) >= 10]
            a[p, g + 8] = far[np.random.randint(len(far))]
    return np.exp2(a.ravel()).repeat(32)


def f64(x):
    return np.asarray(x).astype(np.float64)


def striped(idx):
    return np.tile(idx.reshape(-1, 16).T, (8, 1)).astype(np.uint16)


def unstriped(offs):
    return offs[:16].T.reshape(-1).astype(np.int64)


E2M1 = np.array([0.0, 0.5, 1.0, 1.5, 2.0, 3.0, 4.0, 6.0, -0.0, -0.5, -1.0, -1.5, -2.0, -3.0, -4.0, -6.0])


def pack_weight(w, fmt):
    k, n = w.shape
    w = f64(np.asarray(w, np.float32).astype(ml_dtypes.bfloat16)).reshape(k // 32, 32, n)
    amax = np.abs(w).max(1)
    if fmt == "e4m3":
        byte = np.frexp(amax)[1] - 1 + 127 - 7
    else:
        mant, ex = np.frexp(amax / 6.0)
        byte = np.where(mant > 0.5, ex, ex - 1) + 127
    byte = np.clip(np.where(amax > 0, byte, 1), 1, 254)
    scaled = (w * np.exp2(127.0 - byte)[:, None, :]).reshape(k, n).astype(np.float32)
    by_word = np.ascontiguousarray(scaled.reshape(k // 512, 128, 4, n).transpose(0, 1, 3, 2))
    if fmt == "e4m3":
        words = by_word.astype(ml_dtypes.float8_e4m3fn).view(np.uint8)
    else:
        c = by_word.astype(ml_dtypes.float4_e2m1fn).view(np.uint8) & 0xF
        words = (c[..., 0::2] | (c[..., 1::2] << 4)).reshape(k // 512, 128, 2 * n)
    return np.ascontiguousarray(words), np.ascontiguousarray(byte.astype(np.uint8).reshape(k // 512, 16, n))


def unpack_weight(words, scales, fmt):
    g, _, n = scales.shape
    words = np.ascontiguousarray(words).reshape(g, 128, n, -1)
    if fmt == "e4m3":
        vals = words.view(ml_dtypes.float8_e4m3fn).astype(np.float64)
    else:
        nib = np.empty((g, 128, n, 4), np.uint8)
        nib[..., 0::2] = words & 0xF
        nib[..., 1::2] = words >> 4
        vals = E2M1[nib]
    vals = vals * np.repeat(np.exp2(scales.astype(np.float64) - 127.0), 8, axis=1)[..., None]
    return vals.transpose(0, 1, 3, 2).reshape(g * 512, n)


def gelu(v):
    return 0.5 * v * (1.0 + np.tanh(np.sqrt(2.0 / np.pi) * (v + 0.044715 * v**3)))


def bf(x):
    return np.asarray(x, np.float32).astype(ml_dtypes.bfloat16)


def planes(Y):
    n, m = Y.shape
    b = f64(bf(Y)).reshape(n // 32, 32, m)
    amax = np.abs(b).max(1)
    byte = np.clip(np.where(amax > 0, np.frexp(amax)[1] - 1 + 127 - 7, 1), 1, 254)
    codes = (b * np.exp2(127.0 - byte)[:, None, :]).reshape(n, m).astype(np.float32).astype(ml_dtypes.float8_e4m3fn).view(np.uint8)
    words = codes.reshape(n // 512, 128, 4, m).transpose(0, 1, 3, 2)
    return np.ascontiguousarray(words), np.ascontiguousarray(byte.astype(np.uint8).reshape(n // 512, 16, m))


K, T, S, H, N = 512, 4096, 1024, 1024, 512

def setup_inputs():
    n = np.random.standard_normal
    s = mx_kscale(K)[:, None]
    u = mx_kscale(H)[:, None]
    tab_words, tab_scales = pack_weight(n((K, T)) * s, "e4m3")
    wp_words, wp_scales = pack_weight(0.35 * n((K, H)) / (s * np.sqrt(K)), "e2m1")
    w4_words, w4_scales = pack_weight(0.8 * n((K, N)) / (s * np.sqrt(K)), "e4m3")
    return {
        "tab_words": tab_words, "tab_scales": tab_scales,
        "offs": striped(np.random.permutation(T)[:S]),
        "wp_words": wp_words, "wp_scales": wp_scales,
        "phi": np.random.uniform(-0.9, 0.9, H).astype(np.float32),
        "wa": (n((K, H)) * u.T / (s * np.sqrt(K))).astype(np.float32),
        "w3": (0.5 * n((H, N)) / (u * np.sqrt(H))).astype(np.float32),
        "amp": np.random.uniform(0.8, 2.0, N).astype(np.float32),
        "w4_words": w4_words, "w4_scales": w4_scales,
    }

def reference(tab_words, tab_scales, offs, wp_words, wp_scales, phi, wa, w3, amp, w4_words, w4_scales):
    v = unpack_weight(tab_words, tab_scales, "e4m3")[:, unstriped(offs)]
    wp = unpack_weight(wp_words, wp_scales, "e2m1")
    w4 = unpack_weight(w4_words, w4_scales, "e4m3")
    phase = (wp.T @ v) + f64(phi)[:, None]
    h = np.cos(phase) * (mxq(f64(wa), 0, "e4m3").T @ v)
    words, scales = planes(h)
    d = mxq(f64(w3), 0, "e4m3").T @ mxq(h, 0, "e4m3")
    e = w4.T @ v
    y = f64(amp)[:, None] * np.sin(d) + e
    return y, h, words, scales

@@ -1,0 +1,291 @@
+import math
+from contextlib import ExitStack
+
+import concourse.mybir as mybir
+
+K, T, S, H, N = 512, 4096, 1024, 1024, 512
+FLOPS = 2 * S * (2 * K * H + H * N + K * N)
+
+F32 = mybir.dt.float32
+BF16 = mybir.dt.bfloat16
+I32 = mybir.dt.int32
+U32 = mybir.dt.uint32
+U16 = mybir.dt.uint16
+U8 = mybir.dt.uint8
+FP8X4 = mybir.dt.float8_e4m3fn_x4
+FP4X4 = mybir.dt.float4_e2m1fn_x4
+ACT = mybir.ActivationFunctionType
+ALU = mybir.AluOpType
+
+P = 128
+PACK = 4
+PASS = P * PACK
+GROUPS = H // PASS
+BANK = 512
+LOOKUP = 512
+CHUNKS = [(0, 512), (512, 256), (768, 256)]
+
+
+def tile_list_readout_phase_calibration_kernel(
+    tc, tab_words, tab_scales, offs, wp_words, wp_scales, phi, wa, w3, amp, w4_words, w4_scales,
+    out_0, out_1, out_2, out_3,
+):
+    nc = tc.nc
+    with ExitStack() as ctx:
+        keep = ctx.enter_context(tc.tile_pool(name="keep", bufs=1))
+        psum = ctx.enter_context(tc.psum_pool(name="psum", bufs=2))
+        ring = ctx.enter_context(tc.tile_pool(name="ring", bufs=4))
+
+        def sb(name, shape, dtype, tag=None):
+            return keep.tile(shape, dtype, name=name, tag=tag or name, align_bytes=64)
+
+        offsets = keep.tile([P, S // 16], U16, name="offsets")
+        nc.sync.dma_start(offsets[:], offs)
+
+        def load_scale_rows(queues, fill, name, src, width):
+            plane = sb(name, [P, width], U8)
+            fill.memset(plane[:].bitcast(I32), 0)
+            for r in range(4):
+                queues[r].dma_start(plane[r:P:32, :].bitcast(I32), src[0, r:16:4, :].bitcast(I32))
+            return plane
+
+        tab_plane = load_scale_rows([nc.scalar] * 4, nc.vector, "tab_plane", tab_scales, T)
+        wp_plane_raw = load_scale_rows([nc.gpsimd] * 2 + [nc.scalar] * 2, nc.gpsimd, "wp_plane_raw", wp_scales, H)
+
+        phi_sb = sb("phi_sb", [P, GROUPS, PACK], F32)
+        nc.gpsimd.dma_start(phi_sb[:], phi.rearrange("(g p t) -> p g t", g=GROUPS, t=PACK))
+
+        wp_raw = sb("wp_raw", [P, 2 * H], U8)
+        nc.sync.dma_start(wp_raw[:].bitcast(I32), wp_words[0].bitcast(I32))
+        tab = sb("tab", [P, T], U32)
+        nc.sync.dma_start(tab[:].bitcast(I32), tab_words[0].rearrange("p t i -> p (t i)").bitcast(I32))
+
+        wa_raw = {}
+
+        def load_wa(g, tag):
+            wa_raw[g] = sb("wa_raw%d" % g, [P, PACK, PASS], F32, tag=tag)
+            nc.sync.dma_start(wa_raw[g][:], wa[:, g * PASS:(g + 1) * PASS].rearrange("(p j) c -> p j c", j=PACK))
+
+        w4_plane = load_scale_rows([nc.gpsimd] * 4, nc.gpsimd, "w4_plane", w4_scales, N)
+
+        warm = sb("warm", [P, 1], F32)
+        nc.scalar.activation(warm[:], phi_sb[:, 0, 0:1], ACT.Sin)
+
+        wp_codes = sb("wp_codes", [P, 2 * H], U8)
+        nc.vector.tensor_copy(
+            wp_codes[:].rearrange("p (g t m b) -> p g m t b", g=GROUPS, t=PACK, b=2),
+            wp_raw[:].rearrange("p (g m t b) -> p g m t b", g=GROUPS, t=PACK, b=2),
+        )
+        load_wa(0, "wp_raw")
+        wp_plane = sb("wp_plane", [P, H], U8)
+        nc.vector.tensor_copy(
+            wp_plane[:].rearrange("p (g t m) -> p g m t", g=GROUPS, t=PACK),
+            wp_plane_raw[:].rearrange("p (g m t) -> p g m t", g=GROUPS, t=PACK),
+        )
+        load_wa(1, "wp_plane_raw")
+        v_planes, v_codes = {}, {}
+
+        def look_up(u):
+            cols = offsets[:, u * LOOKUP // 16:(u + 1) * LOOKUP // 16]
+            v_planes[u] = sb("v_plane%d" % u, [P, LOOKUP], U8, tag=(None, "wp_raw")[u])
+            nc.vector.tensor_copy(v_planes[u][:], tab_plane[:].indirect(cols))
+            v_codes[u] = sb("v_codes%d" % u, [P, LOOKUP], U32)
+            nc.vector.tensor_copy(v_codes[u][:], tab[:].indirect(cols))
+
+        look_up(0)
+        w3_raw = {}
+
+        def load_w3(g, tag):
+            w3_raw[g] = sb("w3_raw%d" % g, [P, PACK, N], F32, tag=tag)
+            nc.sync.dma_start(w3_raw[g][:], w3[g * PASS:(g + 1) * PASS, :].rearrange("(p j) n -> p j n", j=PACK))
+
+
+        def shots(j0, width):
+            u, c0 = divmod(j0, LOOKUP)
+            return v_codes[u][:, c0:c0 + width].bitcast(FP8X4), v_planes[u][:, c0:c0 + width]
+
+        wa_codes, wa_planes, w3_codes, w3_planes = {}, {}, {}, {}
+        staged = {}
+
+        def cast_wa(g):
+            rounded = sb("wa_bf%d" % g, [P, PASS * PACK], BF16)
+            nc.vector.tensor_copy(
+                rounded[:].rearrange("p (t m j) -> p m j t", t=PACK, j=PACK),
+                wa_raw[g][:].rearrange("p j (m t) -> p m j t", t=PACK),
+            )
+            staged["wa", g] = rounded
+
+        def cast_w3(g):
+            rounded = sb("w3_bf%d" % g, [P, N * PACK], BF16)
+            nc.scalar.copy(
+                rounded[:].rearrange("p (c i j) -> p c j i", i=4, j=PACK),
+                w3_raw[g][:].rearrange("p j (c i) -> p c j i", i=4),
+            )
+            staged["w3", g] = rounded
+
+        def quantise_weight(name, g, codes, planes):
+            codes[g] = sb("%s_codes%d" % (name, g), [P, PASS], U32)
+            planes[g] = sb("%s_plane%d" % (name, g), [P, PASS], U8)
+            nc.vector.quantize_mx(out=codes[g][:].bitcast(FP8X4), scales=planes[g][:], in_=staged[name, g][:])
+
+        h_plane = sb("h_plane", [P, GROUPS * S], U8)
+        h_codes = {}
+        cosines, h_tiles = {}, {}
+
+        def phase_bank(c, g, b):
+            j0, width = CHUNKS[c]
+            per = BANK // width
+            rhs, rhs_scale = shots(j0, width)
+            bank = psum.tile([P, BANK], F32, name="phase", tag="phase")
+            mag = ring.tile([P, BANK], F32, name="mag")
+            for s in range(per):
+                t = b * per + s
+                col = g * PASS + t * P
+                nc.tensor.matmul_mx(
+                    out=bank[:, s * width:(s + 1) * width],
+                    lhsT=wp_codes[:, 2 * col:2 * (col + P)].bitcast(FP4X4), lhsT_scale=wp_plane[:, col:col + P],
+                    rhs=rhs, rhs_scale=rhs_scale, start=True, stop=True,
+                )
+            for s in range(per):
+                t = b * per + s
+                nc.scalar.activation(
+                    mag[:, s * width:(s + 1) * width], bank[:, s * width:(s + 1) * width], ACT.Abs,
+                    bias=phi_sb[:, g, t:t + 1],
+                )
+            cosines[c, g, b] = mag
+
+        def cosine(c, g, b):
+            cos = ring.tile([P, BANK], F32, name="cos", bufs=8)
+            nc.scalar.activation(cos[:], cosines[c, g, b][:], ACT.Sin, bias=math.pi / 2, scale=-1.0)
+            cosines[c, g, b] = cos
+
+        def feature_bank(c, g, b):
+            j0, width = CHUNKS[c]
+            per = BANK // width
+            rhs, rhs_scale = shots(j0, width)
+            if b == 0:
+                h_tiles[c, g] = sb("h%d_%d" % (c, g), [P, PACK * width], F32)
+            bank = psum.tile([P, BANK], F32, name="ampl", tag="ampl")
+            for s in range(per):
+                t = b * per + s
+                nc.tensor.matmul_mx(
+                    out=bank[:, s * width:(s + 1) * width],
+                    lhsT=wa_codes[g][:, t * P:(t + 1) * P].bitcast(FP8X4), lhsT_scale=wa_planes[g][:, t * P:(t + 1) * P],
+                    rhs=rhs, rhs_scale=rhs_scale, start=True, stop=True,
+                )
+            h = h_tiles[c, g]
+            nc.vector.tensor_tensor(h[:, b * BANK:(b + 1) * BANK], cosines[c, g, b][:], bank[:], ALU.mult)
+            if b % 2 == 1:
+                t0, t1 = (b - 1) * per, (b + 1) * per
+                rows = out_1[g * PASS:(g + 1) * PASS, j0:j0 + width].rearrange("(p t) j -> p t j", t=PACK)
+                nc.sync.dma_start(
+                    rows[:, t0:t1, :],
+                    h[:, t0 * width:t1 * width].rearrange("p (t j) -> p t j", j=width),
+                )
+
+        def cast_h(c, g):
+            width = CHUNKS[c][1]
+            rounded = sb("h_bf%d_%d" % (c, g), [P, PACK * width], BF16)
+            nc.vector.tensor_copy(
+                rounded[:].rearrange("p (c i t) -> p c t i", i=4, t=PACK),
+                h_tiles[c, g][:].rearrange("p (t c i) -> p c t i", i=4, t=PACK),
+            )
+            staged["h", c, g] = rounded
+
+        def quantise_h(c, g):
+            j0, width = CHUNKS[c]
+            codes = sb("h_codes%d_%d" % (c, g), [P, width], U32)
+            nc.vector.quantize_mx(
+                out=codes[:].bitcast(FP8X4), scales=h_plane[:, g * S + j0:g * S + j0 + width], in_=staged["h", c, g][:]
+            )
+            h_codes[c, g] = codes
+            nc.sync.dma_start(
+                out_2[g].rearrange("p m t -> p (m t)").bitcast(I32)[:, j0:j0 + width], codes[:].bitcast(I32)
+            )
+
+        tail = {}
+
+        def load_readout():
+            tail["w4"] = sb("w4_codes", [P, N], U32, tag="tab_plane")
+            nc.sync.dma_start(tail["w4"][:].bitcast(I32), w4_words[0].rearrange("p c i -> p (c i)").bitcast(I32))
+            tail["amp"] = sb("amp_sb", [P, N // P], F32, tag="tab")
+            with nc.allow_non_contiguous_dma(reason="one value of amp to a partition"):
+                nc.sync.dma_start(tail["amp"][:], amp.rearrange("(i p) -> p i", p=P))
+
+        def result_bank(c, b):
+            j0, width = CHUNKS[c]
+            per = BANK // width
+            rhs, rhs_scale = shots(j0, width)
+            resp = psum.tile([P, BANK], F32, name="resp", tag="resp")
+            lin = psum.tile([P, BANK], F32, name="lin", tag="lin")
+            for s in range(per):
+                n0 = (b * per + s) * P
+                nc.tensor.matmul_mx(
+                    out=lin[:, s * width:(s + 1) * width],
+                    lhsT=tail["w4"][:, n0:n0 + P].bitcast(FP8X4), lhsT_scale=w4_plane[:, n0:n0 + P],
+                    rhs=rhs, rhs_scale=rhs_scale, start=True, stop=True,
+                )
+            for s in range(per):
+                n0 = (b * per + s) * P
+                for g in range(GROUPS):
+                    nc.tensor.matmul_mx(
+                        out=resp[:, s * width:(s + 1) * width],
+                        lhsT=w3_codes[g][:, n0:n0 + P].bitcast(FP8X4), lhsT_scale=w3_planes[g][:, n0:n0 + P],
+                        rhs=h_codes[c, g][:].bitcast(FP8X4), rhs_scale=h_plane[:, g * S + j0:g * S + j0 + width],
+                        start=(g == 0), stop=(g == GROUPS - 1),
+                    )
+            sine = ring.tile([P, BANK], F32, name="sine")
+            nc.scalar.activation(sine[:], resp[:], ACT.Sin)
+            y = sb("y%d_%d" % (c, b), [P, BANK], F32)
+            for s in range(per):
+                i = b * per + s
+                cols = slice(s * width, (s + 1) * width)
+                nc.vector.scalar_tensor_tensor(
+                    y[:, cols], sine[:, cols], tail["amp"][:, i:i + 1], lin[:, cols], ALU.mult, ALU.add
+                )
+            rows = out_0[b * per * P:(b + 1) * per * P, j0:j0 + width].rearrange("(s p) j -> p s j", p=P)
+            nc.sync.dma_start(rows, y[:].rearrange("p (s j) -> p s j", j=width))
+
+        def banks(c):
+            return PACK * CHUNKS[c][1] // BANK
+
+        steps = [(c, g, b) for c in range(len(CHUNKS)) for g in range(GROUPS) for b in range(banks(c))]
+        cast_wa(0)
+        quantise_weight("wa", 0, wa_codes, wa_planes)
+        load_w3(0, "wa_bf0")
+        later = {}
+        phase_bank(*steps[0])
+        for n, (c, g, b) in enumerate(steps):
+            if n + 1 < len(steps):
+                phase_bank(*steps[n + 1])
+            cosine(c, g, b)
+            feature_bank(c, g, b)
+            if (c, g, b) == (0, 0, 1):
+                cast_wa(1)
+                load_w3(1, "wp_plane_raw")
+            if (c, g, b) == (0, 0, 2):
+                quantise_weight("wa", 1, wa_codes, wa_planes)
+            if (c, g, b) == (0, 1, 0):
+                look_up(1)
+                load_readout()
+            if c == 0 and g == 1 and b < GROUPS:
+                cast_w3(b)
+            if c == 0 and g == 1 and b >= GROUPS:
+                quantise_weight("w3", b - GROUPS, w3_codes, w3_planes)
+            for job, args in later.get(n, []):
+                job(*args)
+            if b == banks(c) - 1:
+                cast_h(c, g)
+                later.setdefault(n + 1, []).append((quantise_h, (c, g)))
+                if g == GROUPS - 1:
+                    for rb in range(banks(c)):
+                        later.setdefault(n + 1 + rb, []).append((result_bank, (c, rb)))
+        for n in range(len(steps), len(steps) + PACK):
+            for job, args in later.get(n, []):
+                job(*args)
+
+        for r in range(4):
+            nc.sync.dma_start(
+                out_3[:, r:16:4, :].rearrange("g q m -> q g m").bitcast(I32),
+                h_plane[r:P:32, :].rearrange("q (g m) -> q g m", g=GROUPS).bitcast(I32),
+            )

@@ -73,21 +73,21 @@ def tile_list_readout_phase_calibration_kernel(
 
         wp_codes = sb("wp_codes", [P, 2 * H], U8)
         nc.vector.tensor_copy(
-            wp_codes[:].rearrange("p (g t m b) -> p g m t b", g=GROUPS, t=PACK, b=2),
-            wp_raw[:].rearrange("p (g m t b) -> p g m t b", g=GROUPS, t=PACK, b=2),
+            wp_codes[:].rearrange("p (g t m b) -> p g t m b", g=GROUPS, t=PACK, b=2),
+            wp_raw[:].rearrange("p (g m t b) -> p g t m b", g=GROUPS, t=PACK, b=2),
         )
         load_wa(0, "wp_raw")
         wp_plane = sb("wp_plane", [P, H], U8)
         nc.vector.tensor_copy(
-            wp_plane[:].rearrange("p (g t m) -> p g m t", g=GROUPS, t=PACK),
-            wp_plane_raw[:].rearrange("p (g m t) -> p g m t", g=GROUPS, t=PACK),
+            wp_plane[:].rearrange("p (g t m) -> p g t m", g=GROUPS, t=PACK),
+            wp_plane_raw[:].rearrange("p (g m t) -> p g t m", g=GROUPS, t=PACK),
         )
         load_wa(1, "wp_plane_raw")
         v_planes, v_codes = {}, {}
 
         def look_up(u):
             cols = offsets[:, u * LOOKUP // 16:(u + 1) * LOOKUP // 16]
-            v_planes[u] = sb("v_plane%d" % u, [P, LOOKUP], U8, tag=(None, "wp_raw")[u])
+            v_planes[u] = sb("v_plane%d" % u, [P, LOOKUP], U8)
             nc.vector.tensor_copy(v_planes[u][:], tab_plane[:].indirect(cols))
             v_codes[u] = sb("v_codes%d" % u, [P, LOOKUP], U32)
             nc.vector.tensor_copy(v_codes[u][:], tab[:].indirect(cols))
@@ -110,8 +110,8 @@ def tile_list_readout_phase_calibration_kernel(
         def cast_wa(g):
             rounded = sb("wa_bf%d" % g, [P, PASS * PACK], BF16)
             nc.vector.tensor_copy(
-                rounded[:].rearrange("p (t m j) -> p m j t", t=PACK, j=PACK),
-                wa_raw[g][:].rearrange("p j (m t) -> p m j t", t=PACK),
+                rounded[:].rearrange("p (t m j) -> p m t j", t=PACK, j=PACK),
+                wa_raw[g][:].rearrange("p j (m t) -> p m t j", t=PACK),
             )
             staged["wa", g] = rounded
 

@@ -2,6 +2,7 @@ import math
 from contextlib import ExitStack
 
 import concourse.mybir as mybir
+from concourse.masks import make_identity
 
 K, T, S, H, N = 512, 4096, 1024, 1024, 512
 FLOPS = 2 * S * (2 * K * H + H * N + K * N)
@@ -42,63 +43,85 @@ def tile_list_readout_phase_calibration_kernel(
         offsets = keep.tile([P, S // 16], U16, name="offsets")
         nc.sync.dma_start(offsets[:], offs)
 
-        def load_scale_rows(queues, fill, name, src, width):
-            plane = sb(name, [P, width], U8)
-            fill.memset(plane[:].bitcast(I32), 0)
-            for r in range(4):
-                queues[r].dma_start(plane[r:P:32, :].bitcast(I32), src[0, r:16:4, :].bitcast(I32))
-            return plane
+        def load_scale_rows(queue, fill, rows, src):
+            fill.memset(rows.bitcast(I32), 0)
+            queue.dma_start(rows[0:P:8, :].bitcast(I32), src[0].bitcast(I32))
 
-        tab_plane = load_scale_rows([nc.scalar] * 4, nc.vector, "tab_plane", tab_scales, T)
-        wp_plane_raw = load_scale_rows([nc.gpsimd] * 2 + [nc.scalar] * 2, nc.gpsimd, "wp_plane_raw", wp_scales, H)
-
-        phi_sb = sb("phi_sb", [P, GROUPS, PACK], F32)
-        nc.gpsimd.dma_start(phi_sb[:], phi.rearrange("(g p t) -> p g t", g=GROUPS, t=PACK))
+        def seat_scale_rows(plane):
+            for r in range(1, 4):
+                nc.sync.dma_start(plane[r:P:32, :].bitcast(I32), plane[8 * r:P:32, :].bitcast(I32))
 
         wp_raw = sb("wp_raw", [P, 2 * H], U8)
         nc.sync.dma_start(wp_raw[:].bitcast(I32), wp_words[0].bitcast(I32))
+        wp_rows = sb("wp_rows", [P, H], U8)
+        load_scale_rows(nc.sync, nc.gpsimd, wp_rows[:], wp_scales)
+        tab_rows = sb("tab_rows", [P, T], U8)
+        load_scale_rows(nc.sync, nc.vector, tab_rows[:], tab_scales)
         tab = sb("tab", [P, T], U32)
         nc.sync.dma_start(tab[:].bitcast(I32), tab_words[0].rearrange("p t i -> p (t i)").bitcast(I32))
 
-        wa_raw = {}
-
-        def load_wa(g, tag):
-            wa_raw[g] = sb("wa_raw%d" % g, [P, PACK, PASS], F32, tag=tag)
-            nc.sync.dma_start(wa_raw[g][:], wa[:, g * PASS:(g + 1) * PASS].rearrange("(p j) c -> p j c", j=PACK))
-
-        w4_plane = load_scale_rows([nc.gpsimd] * 4, nc.gpsimd, "w4_plane", w4_scales, N)
+        vectors = sb("vectors", [P, PASS], F32)
+        nc.gpsimd.memset(vectors[:], 0.0)
+        nc.scalar.dma_start(vectors[0:GROUPS, :], phi.rearrange("(g c) -> g c", g=GROUPS))
+        nc.scalar.dma_start(vectors[GROUPS:GROUPS + 1, :], amp.rearrange("(o n) -> o n", o=1))
+        first_planes = sb("first_planes", [P, LOOKUP + H], U8)
+        later_planes = sb("later_planes", [P, LOOKUP + N], U8)
+        wp_plane, w4_plane = first_planes[:, LOOKUP:], later_planes[:, LOOKUP:]
+        v_planes = [first_planes[:, :LOOKUP], later_planes[:, :LOOKUP]]
+        load_scale_rows(nc.scalar, nc.gpsimd, w4_plane, w4_scales)
+        identity = sb("identity", [P, P], F32)
+        make_identity(nc, identity[:])
 
         warm = sb("warm", [P, 1], F32)
-        nc.scalar.activation(warm[:], phi_sb[:, 0, 0:1], ACT.Sin)
+        nc.scalar.activation(warm[:], identity[:, 0:1], ACT.Sin)
 
+        phi_bank = psum.tile([P, PACK, P], F32, name="phi_bank", tag="resp")
+        amp_bank = psum.tile([P, N // P, P], F32, name="amp_bank", tag="lin")
+        for t in range(PACK):
+            nc.tensor.transpose(phi_bank[:, t, :], vectors[:, t:PASS:PACK], identity[:])
+        for i in range(N // P):
+            nc.tensor.transpose(amp_bank[:, i, :], vectors[:, i * P:(i + 1) * P], identity[:])
+        phi_sb = sb("phi_sb", [P, PACK, GROUPS], F32)
+        nc.scalar.copy(phi_sb[:], phi_bank[:, :, 0:GROUPS])
+        amp_sb = sb("amp_sb", [P, N // P, 1], F32)
+        nc.scalar.copy(amp_sb[:], amp_bank[:, :, GROUPS:GROUPS + 1])
+
+        def list_part(u):
+            return offsets[:, u * LOOKUP // 16:(u + 1) * LOOKUP // 16]
+
+        def look_up_scales(u):
+            picked = sb("v_rows%d" % u, [P, LOOKUP], U8)
+            nc.vector.tensor_copy(picked[:], tab_rows[:].indirect(list_part(u)))
+            nc.vector.tensor_copy(v_planes[u].bitcast(I32), picked[:].bitcast(I32))
+
+        look_up_scales(0)
+        nc.vector.tensor_copy(
+            wp_plane.rearrange("p (g t m) -> p g t m", g=GROUPS, t=PACK),
+            wp_rows[:].rearrange("p (g m t) -> p g t m", g=GROUPS, t=PACK),
+        )
+        seat_scale_rows(first_planes)
         wp_codes = sb("wp_codes", [P, 2 * H], U8)
         nc.vector.tensor_copy(
             wp_codes[:].rearrange("p (g t m b) -> p g t m b", g=GROUPS, t=PACK, b=2),
             wp_raw[:].rearrange("p (g m t b) -> p g t m b", g=GROUPS, t=PACK, b=2),
         )
-        load_wa(0, "wp_raw")
-        wp_plane = sb("wp_plane", [P, H], U8)
-        nc.vector.tensor_copy(
-            wp_plane[:].rearrange("p (g t m) -> p g t m", g=GROUPS, t=PACK),
-            wp_plane_raw[:].rearrange("p (g m t) -> p g t m", g=GROUPS, t=PACK),
-        )
-        load_wa(1, "wp_plane_raw")
-        v_planes, v_codes = {}, {}
-
-        def look_up(u):
-            cols = offsets[:, u * LOOKUP // 16:(u + 1) * LOOKUP // 16]
-            v_planes[u] = sb("v_plane%d" % u, [P, LOOKUP], U8)
-            nc.vector.tensor_copy(v_planes[u][:], tab_plane[:].indirect(cols))
-            v_codes[u] = sb("v_codes%d" % u, [P, LOOKUP], U32)
-            nc.vector.tensor_copy(v_codes[u][:], tab[:].indirect(cols))
-
-        look_up(0)
-        w3_raw = {}
-
-        def load_w3(g, tag):
-            w3_raw[g] = sb("w3_raw%d" % g, [P, PACK, N], F32, tag=tag)
-            nc.sync.dma_start(w3_raw[g][:], w3[g * PASS:(g + 1) * PASS, :].rearrange("(p j) n -> p j n", j=PACK))
-
+        wa_raw, w3_raw, v_codes = [], [], []
+        for g in range(GROUPS):
+            raw = sb("wa_raw%d" % g, [P, PACK, PASS], F32)
+            nc.sync.dma_start(raw[:], wa[:, g * PASS:(g + 1) * PASS].rearrange("(p j) c -> p j c", j=PACK))
+            wa_raw.append(raw)
+        look_up_scales(1)
+        seat_scale_rows(later_planes)
+        for g in range(GROUPS):
+            raw = sb("w3_raw%d" % g, [P, PACK, N], F32)
+            nc.sync.dma_start(raw[:], w3[g * PASS:(g + 1) * PASS, :].rearrange("(p j) n -> p j n", j=PACK))
+            w3_raw.append(raw)
+        w4_codes = sb("w4_codes", [P, N], U32)
+        nc.sync.dma_start(w4_codes[:].bitcast(I32), w4_words[0].rearrange("p c i -> p (c i)").bitcast(I32))
+        for u in range(S // LOOKUP):
+            picked = sb("v_codes%d" % u, [P, LOOKUP], U32)
+            nc.vector.tensor_copy(picked[:], tab[:].indirect(list_part(u)))
+            v_codes.append(picked)
 
         def shots(j0, width):
             u, c0 = divmod(j0, LOOKUP)
@@ -117,7 +140,8 @@ def tile_list_readout_phase_calibration_kernel(
 
         def cast_w3(g):
             rounded = sb("w3_bf%d" % g, [P, N * PACK], BF16)
-            nc.scalar.copy(
+            copy = nc.vector.tensor_copy if g == 0 else nc.scalar.copy
+            copy(
                 rounded[:].rearrange("p (c i j) -> p c j i", i=4, j=PACK),
                 w3_raw[g][:].rearrange("p j (c i) -> p c j i", i=4),
             )
@@ -150,7 +174,7 @@ def tile_list_readout_phase_calibration_kernel(
                 t = b * per + s
                 nc.scalar.activation(
                     mag[:, s * width:(s + 1) * width], bank[:, s * width:(s + 1) * width], ACT.Abs,
-                    bias=phi_sb[:, g, t:t + 1],
+                    bias=phi_sb[:, t, g:g + 1],
                 )
             cosines[c, g, b] = mag
 
@@ -203,15 +227,6 @@ def tile_list_readout_phase_calibration_kernel(
                 out_2[g].rearrange("p m t -> p (m t)").bitcast(I32)[:, j0:j0 + width], codes[:].bitcast(I32)
             )
 
-        tail = {}
-
-        def load_readout():
-            tail["w4"] = sb("w4_codes", [P, N], U32, tag="tab_plane")
-            nc.sync.dma_start(tail["w4"][:].bitcast(I32), w4_words[0].rearrange("p c i -> p (c i)").bitcast(I32))
-            tail["amp"] = sb("amp_sb", [P, N // P], F32, tag="tab")
-            with nc.allow_non_contiguous_dma(reason="one value of amp to a partition"):
-                nc.sync.dma_start(tail["amp"][:], amp.rearrange("(i p) -> p i", p=P))
-
         def result_bank(c, b):
             j0, width = CHUNKS[c]
             per = BANK // width
@@ -222,7 +237,7 @@ def tile_list_readout_phase_calibration_kernel(
                 n0 = (b * per + s) * P
                 nc.tensor.matmul_mx(
                     out=lin[:, s * width:(s + 1) * width],
-                    lhsT=tail["w4"][:, n0:n0 + P].bitcast(FP8X4), lhsT_scale=w4_plane[:, n0:n0 + P],
+                    lhsT=w4_codes[:, n0:n0 + P].bitcast(FP8X4), lhsT_scale=w4_plane[:, n0:n0 + P],
                     rhs=rhs, rhs_scale=rhs_scale, start=True, stop=True,
                 )
             for s in range(per):
@@ -241,7 +256,7 @@ def tile_list_readout_phase_calibration_kernel(
                 i = b * per + s
                 cols = slice(s * width, (s + 1) * width)
                 nc.vector.scalar_tensor_tensor(
-                    y[:, cols], sine[:, cols], tail["amp"][:, i:i + 1], lin[:, cols], ALU.mult, ALU.add
+                    y[:, cols], sine[:, cols], amp_sb[:, i, :], lin[:, cols], ALU.mult, ALU.add
                 )
             rows = out_0[b * per * P:(b + 1) * per * P, j0:j0 + width].rearrange("(s p) j -> p s j", p=P)
             nc.sync.dma_start(rows, y[:].rearrange("p (s j) -> p s j", j=width))
@@ -252,7 +267,6 @@ def tile_list_readout_phase_calibration_kernel(
         steps = [(c, g, b) for c in range(len(CHUNKS)) for g in range(GROUPS) for b in range(banks(c))]
         cast_wa(0)
         quantise_weight("wa", 0, wa_codes, wa_planes)
-        load_w3(0, "wa_bf0")
         later = {}
         phase_bank(*steps[0])
         for n, (c, g, b) in enumerate(steps):
@@ -262,12 +276,8 @@ def tile_list_readout_phase_calibration_kernel(
             feature_bank(c, g, b)
             if (c, g, b) == (0, 0, 1):
                 cast_wa(1)
-                load_w3(1, "wp_plane_raw")
             if (c, g, b) == (0, 0, 2):
                 quantise_weight("wa", 1, wa_codes, wa_planes)
-            if (c, g, b) == (0, 1, 0):
-                look_up(1)
-                load_readout()
             if c == 0 and g == 1 and b < GROUPS:
                 cast_w3(b)
             if c == 0 and g == 1 and b >= GROUPS:
@@ -279,7 +289,8 @@ def tile_list_readout_phase_calibration_kernel(
                 later.setdefault(n + 1, []).append((quantise_h, (c, g)))
                 if g == GROUPS - 1:
                     for rb in range(banks(c)):
-                        later.setdefault(n + 1 + rb, []).append((result_bank, (c, rb)))
+                        delay = 3 if c == 1 else 0
+                        later.setdefault(n + 1 + rb + delay, []).append((result_bank, (c, rb)))
         for n in range(len(steps), len(steps) + PACK):
             for job, args in later.get(n, []):
                 job(*args)

@@ -90,7 +90,7 @@ def tile_list_readout_phase_calibration_kernel(
             return offsets[:, u * LOOKUP // 16:(u + 1) * LOOKUP // 16]
 
         def look_up_scales(u):
-            picked = sb("v_rows%d" % u, [P, LOOKUP], U8)
+            picked = sb("v_rows%d" % u, [P, LOOKUP], U8, tag="v_rows")
             nc.vector.tensor_copy(picked[:], tab_rows[:].indirect(list_part(u)))
             nc.vector.tensor_copy(v_planes[u].bitcast(I32), picked[:].bitcast(I32))
 
@@ -102,13 +102,18 @@ def tile_list_readout_phase_calibration_kernel(
         seat_scale_rows(first_planes)
         wp_codes = sb("wp_codes", [P, 2 * H], U8)
         nc.vector.tensor_copy(
-            wp_codes[:].rearrange("p (g t m b) -> p g t m b", g=GROUPS, t=PACK, b=2),
-            wp_raw[:].rearrange("p (g m t b) -> p g t m b", g=GROUPS, t=PACK, b=2),
+            wp_codes[:].bitcast(U16).rearrange("p (g t m) -> p g t m", g=GROUPS, t=PACK),
+            wp_raw[:].bitcast(U16).rearrange("p (g m t) -> p g t m", g=GROUPS, t=PACK),
         )
         wa_raw, w3_raw, v_codes = [], [], []
         for g in range(GROUPS):
-            raw = sb("wa_raw%d" % g, [P, PACK, PASS], F32)
-            nc.sync.dma_start(raw[:], wa[:, g * PASS:(g + 1) * PASS].rearrange("(p j) c -> p j c", j=PACK))
+            raw = sb("wa_raw%d" % g, [P, PACK, PASS], F32, tag=("wp_rows", None)[g])
+            src = wa[:, g * PASS:(g + 1) * PASS].rearrange("(p j) c -> p j c", j=PACK)
+            if g == 0:
+                nc.scalar.dma_start(raw[:, :PACK // 2, :], src[:, :PACK // 2, :])
+                nc.sync.dma_start(raw[:, PACK // 2:, :], src[:, PACK // 2:, :])
+            else:
+                nc.sync.dma_start(raw[:], src)
             wa_raw.append(raw)
         look_up_scales(1)
         seat_scale_rows(later_planes)
@@ -210,7 +215,8 @@ def tile_list_readout_phase_calibration_kernel(
         def cast_h(c, g):
             width = CHUNKS[c][1]
             rounded = sb("h_bf%d_%d" % (c, g), [P, PACK * width], BF16)
-            nc.vector.tensor_copy(
+            copy = nc.scalar.copy if (c, g) == (len(CHUNKS) - 1, GROUPS - 1) else nc.vector.tensor_copy
+            copy(
                 rounded[:].rearrange("p (c i t) -> p c t i", i=4, t=PACK),
                 h_tiles[c, g][:].rearrange("p (t c i) -> p c t i", i=4, t=PACK),
             )
@@ -226,6 +232,12 @@ def tile_list_readout_phase_calibration_kernel(
             nc.sync.dma_start(
                 out_2[g].rearrange("p m t -> p (m t)").bitcast(I32)[:, j0:j0 + width], codes[:].bitcast(I32)
             )
+            if (c, g) == (len(CHUNKS) - 1, GROUPS - 1):
+                for r in range(4):
+                    nc.sync.dma_start(
+                        out_3[:, r:16:4, :].rearrange("g q m -> q g m").bitcast(I32),
+                        h_plane[r:P:32, :].rearrange("q (g m) -> q g m", g=GROUPS).bitcast(I32),
+                    )
 
         def result_bank(c, b):
             j0, width = CHUNKS[c]
@@ -258,8 +270,7 @@ def tile_list_readout_phase_calibration_kernel(
                 nc.vector.scalar_tensor_tensor(
                     y[:, cols], sine[:, cols], amp_sb[:, i, :], lin[:, cols], ALU.mult, ALU.add
                 )
-            rows = out_0[b * per * P:(b + 1) * per * P, j0:j0 + width].rearrange("(s p) j -> p s j", p=P)
-            nc.sync.dma_start(rows, y[:].rearrange("p (s j) -> p s j", j=width))
+                nc.sync.dma_start(out_0[i * P:(i + 1) * P, j0:j0 + width], y[:, cols])
 
         def banks(c):
             return PACK * CHUNKS[c][1] // BANK
@@ -285,18 +296,12 @@ def tile_list_readout_phase_calibration_kernel(
             for job, args in later.get(n, []):
                 job(*args)
             if b == banks(c) - 1:
-                cast_h(c, g)
-                later.setdefault(n + 1, []).append((quantise_h, (c, g)))
+                later.setdefault(n + 1, []).append((cast_h, (c, g)))
+                later.setdefault(n + 2, []).append((quantise_h, (c, g)))
                 if g == GROUPS - 1:
                     for rb in range(banks(c)):
                         delay = 3 if c == 1 else 0
-                        later.setdefault(n + 1 + rb + delay, []).append((result_bank, (c, rb)))
+                        later.setdefault(n + 2 + rb + delay, []).append((result_bank, (c, rb)))
         for n in range(len(steps), len(steps) + PACK):
             for job, args in later.get(n, []):
                 job(*args)
-
-        for r in range(4):
-            nc.sync.dma_start(
-                out_3[:, r:16:4, :].rearrange("g q m -> q g m").bitcast(I32),
-                h_plane[r:P:32, :].rearrange("q (g m) -> q g m", g=GROUPS).bitcast(I32),
-            )

@@ -2,7 +2,6 @@ import math
 from contextlib import ExitStack
 
 import concourse.mybir as mybir
-from concourse.masks import make_identity
 
 K, T, S, H, N = 512, 4096, 1024, 1024, 512
 FLOPS = 2 * S * (2 * K * H + H * N + K * N)
@@ -24,6 +23,7 @@ PASS = P * PACK
 GROUPS = H // PASS
 BANK = 512
 LOOKUP = 512
+TAB_FIRST = 640
 CHUNKS = [(0, 512), (512, 256), (768, 256)]
 
 
@@ -54,37 +54,25 @@ def tile_list_readout_phase_calibration_kernel(
         wp_raw = sb("wp_raw", [P, 2 * H], U8)
         nc.sync.dma_start(wp_raw[:].bitcast(I32), wp_words[0].bitcast(I32))
         wp_rows = sb("wp_rows", [P, H], U8)
-        load_scale_rows(nc.sync, nc.gpsimd, wp_rows[:], wp_scales)
+        load_scale_rows(nc.sync, nc.vector, wp_rows[:], wp_scales)
+        tab = sb("tab", [P, T], U32)
+        tab_src = tab_words[0].rearrange("p t i -> p (t i)").bitcast(I32)
+        nc.sync.dma_start(tab[:, :TAB_FIRST].bitcast(I32), tab_src[:, :TAB_FIRST])
         tab_rows = sb("tab_rows", [P, T], U8)
         load_scale_rows(nc.sync, nc.vector, tab_rows[:], tab_scales)
-        tab = sb("tab", [P, T], U32)
-        nc.sync.dma_start(tab[:].bitcast(I32), tab_words[0].rearrange("p t i -> p (t i)").bitcast(I32))
+        nc.sync.dma_start(tab[:, TAB_FIRST:].bitcast(I32), tab_src[:, TAB_FIRST:])
 
-        vectors = sb("vectors", [P, PASS], F32)
-        nc.gpsimd.memset(vectors[:], 0.0)
-        nc.scalar.dma_start(vectors[0:GROUPS, :], phi.rearrange("(g c) -> g c", g=GROUPS))
-        nc.scalar.dma_start(vectors[GROUPS:GROUPS + 1, :], amp.rearrange("(o n) -> o n", o=1))
+        phi_sb = sb("phi_sb", [P, GROUPS, 2 * PACK], F32)
+        nc.scalar.dma_start(phi_sb[:, :, :PACK], phi.rearrange("(g p t) -> p g t", g=GROUPS, t=PACK))
         first_planes = sb("first_planes", [P, LOOKUP + H], U8)
         later_planes = sb("later_planes", [P, LOOKUP + N], U8)
         wp_plane, w4_plane = first_planes[:, LOOKUP:], later_planes[:, LOOKUP:]
         v_planes = [first_planes[:, :LOOKUP], later_planes[:, :LOOKUP]]
-        load_scale_rows(nc.scalar, nc.gpsimd, w4_plane, w4_scales)
-        identity = sb("identity", [P, P], F32)
-        make_identity(nc, identity[:])
-
+        load_scale_rows(nc.scalar, nc.vector, w4_plane, w4_scales)
+        zero = sb("zero", [P, 1], F32)
+        nc.vector.memset(zero[:], 0.0)
         warm = sb("warm", [P, 1], F32)
-        nc.scalar.activation(warm[:], identity[:, 0:1], ACT.Sin)
-
-        phi_bank = psum.tile([P, PACK, P], F32, name="phi_bank", tag="resp")
-        amp_bank = psum.tile([P, N // P, P], F32, name="amp_bank", tag="lin")
-        for t in range(PACK):
-            nc.tensor.transpose(phi_bank[:, t, :], vectors[:, t:PASS:PACK], identity[:])
-        for i in range(N // P):
-            nc.tensor.transpose(amp_bank[:, i, :], vectors[:, i * P:(i + 1) * P], identity[:])
-        phi_sb = sb("phi_sb", [P, PACK, GROUPS], F32)
-        nc.scalar.copy(phi_sb[:], phi_bank[:, :, 0:GROUPS])
-        amp_sb = sb("amp_sb", [P, N // P, 1], F32)
-        nc.scalar.copy(amp_sb[:], amp_bank[:, :, GROUPS:GROUPS + 1])
+        nc.scalar.activation(warm[:], zero[:], ACT.Sin)
 
         def list_part(u):
             return offsets[:, u * LOOKUP // 16:(u + 1) * LOOKUP // 16]
@@ -106,14 +94,11 @@ def tile_list_readout_phase_calibration_kernel(
             wp_raw[:].bitcast(U16).rearrange("p (g m t) -> p g t m", g=GROUPS, t=PACK),
         )
         wa_raw, w3_raw, v_codes = [], [], []
-        for g in range(GROUPS):
-            raw = sb("wa_raw%d" % g, [P, PACK, PASS], F32, tag=("wp_rows", None)[g])
-            src = wa[:, g * PASS:(g + 1) * PASS].rearrange("(p j) c -> p j c", j=PACK)
-            if g == 0:
-                nc.scalar.dma_start(raw[:, :PACK // 2, :], src[:, :PACK // 2, :])
-                nc.sync.dma_start(raw[:, PACK // 2:, :], src[:, PACK // 2:, :])
-            else:
-                nc.sync.dma_start(raw[:], src)
+        wa_parts = [(0, 0, PASS // 2), (0, PASS // 2, PASS // 2), (1, 0, PASS)]
+        for n, (g, c0, width) in enumerate(wa_parts):
+            raw = sb("wa_raw%d" % n, [P, PACK, width], F32, tag="wp_rows" if n == 0 else None)
+            src = wa[:, g * PASS + c0:g * PASS + c0 + width].rearrange("(p j) c -> p j c", j=PACK)
+            (nc.scalar if n == 0 else nc.sync).dma_start(raw[:], src)
             wa_raw.append(raw)
         look_up_scales(1)
         seat_scale_rows(later_planes)
@@ -123,6 +108,9 @@ def tile_list_readout_phase_calibration_kernel(
             w3_raw.append(raw)
         w4_codes = sb("w4_codes", [P, N], U32)
         nc.sync.dma_start(w4_codes[:].bitcast(I32), w4_words[0].rearrange("p c i -> p (c i)").bitcast(I32))
+        amp_sb = sb("amp_sb", [P, N // P, 1], F32)
+        with nc.allow_non_contiguous_dma(reason="one value for each partition and row block"):
+            nc.sync.dma_start(amp_sb[:, :, 0], amp.rearrange("(i p) -> p i", p=P))
         for u in range(S // LOOKUP):
             picked = sb("v_codes%d" % u, [P, LOOKUP], U32)
             nc.vector.tensor_copy(picked[:], tab[:].indirect(list_part(u)))
@@ -137,10 +125,14 @@ def tile_list_readout_phase_calibration_kernel(
 
         def cast_wa(g):
             rounded = sb("wa_bf%d" % g, [P, PASS * PACK], BF16)
-            nc.vector.tensor_copy(
-                rounded[:].rearrange("p (t m j) -> p m t j", t=PACK, j=PACK),
-                wa_raw[g][:].rearrange("p j (m t) -> p m t j", t=PACK),
-            )
+            dealt = rounded[:].rearrange("p (t m j) -> p m t j", t=PACK, j=PACK)
+            for n, (part_g, c0, width) in enumerate(wa_parts):
+                if part_g == g:
+                    copy = nc.scalar.copy if n == 0 else nc.vector.tensor_copy
+                    copy(
+                        dealt[:, c0 // PACK:(c0 + width) // PACK],
+                        wa_raw[n][:].rearrange("p j (m t) -> p m t j", t=PACK),
+                    )
             staged["wa", g] = rounded
 
         def cast_w3(g):
@@ -179,7 +171,7 @@ def tile_list_readout_phase_calibration_kernel(
                 t = b * per + s
                 nc.scalar.activation(
                     mag[:, s * width:(s + 1) * width], bank[:, s * width:(s + 1) * width], ACT.Abs,
-                    bias=phi_sb[:, t, g:g + 1],
+                    bias=phi_sb[:, g, t:t + 1],
                 )
             cosines[c, g, b] = mag
 

@@ -24,7 +24,8 @@ GROUPS = H // PASS
 BANK = 512
 LOOKUP = 512
 TAB_FIRST = 640
-CHUNKS = [(0, 512), (512, 256), (768, 256)]
+UNITS = [(0, 0, 512), (1, 0, 512), (0, 512, 512), (1, 512, 256), (1, 768, 256)]
+SCALAR_SHARE = [0, 0, 128, 0, 96]
 
 
 def tile_list_readout_phase_calibration_kernel(
@@ -94,7 +95,7 @@ def tile_list_readout_phase_calibration_kernel(
             wp_raw[:].bitcast(U16).rearrange("p (g m t) -> p g t m", g=GROUPS, t=PACK),
         )
         wa_raw, w3_raw, v_codes = [], [], []
-        wa_parts = [(0, 0, PASS // 2), (0, PASS // 2, PASS // 2), (1, 0, PASS)]
+        wa_parts = [(g, c0, PASS // 2) for g in range(GROUPS) for c0 in (0, PASS // 2)]
         for n, (g, c0, width) in enumerate(wa_parts):
             raw = sb("wa_raw%d" % n, [P, PACK, width], F32, tag="wp_rows" if n == 0 else None)
             src = wa[:, g * PASS + c0:g * PASS + c0 + width].rearrange("(p j) c -> p j c", j=PACK)
@@ -123,25 +124,26 @@ def tile_list_readout_phase_calibration_kernel(
         wa_codes, wa_planes, w3_codes, w3_planes = {}, {}, {}, {}
         staged = {}
 
-        def cast_wa(g):
-            rounded = sb("wa_bf%d" % g, [P, PASS * PACK], BF16)
-            dealt = rounded[:].rearrange("p (t m j) -> p m t j", t=PACK, j=PACK)
-            for n, (part_g, c0, width) in enumerate(wa_parts):
-                if part_g == g:
-                    copy = nc.scalar.copy if n == 0 else nc.vector.tensor_copy
-                    copy(
-                        dealt[:, c0 // PACK:(c0 + width) // PACK],
-                        wa_raw[n][:].rearrange("p j (m t) -> p m t j", t=PACK),
-                    )
-            staged["wa", g] = rounded
+        def cast_wa(n):
+            g, c0, width = wa_parts[n]
+            if c0 == 0:
+                staged["wa", g] = sb("wa_bf%d" % g, [P, PASS * PACK], BF16)
+            dealt = staged["wa", g][:].rearrange("p (t m j) -> p m t j", t=PACK, j=PACK)
+            copy = nc.scalar.copy if n == 0 else nc.vector.tensor_copy
+            copy(
+                dealt[:, c0 // PACK:(c0 + width) // PACK],
+                wa_raw[n][:].rearrange("p j (m t) -> p m t j", t=PACK),
+            )
+
+        def interleave(copy, rounded, rows, c0, c1):
+            copy(
+                rounded[:, PACK * c0:PACK * c1].rearrange("p (c i t) -> p c t i", i=4, t=PACK),
+                rows[:, :, c0:c1].rearrange("p t (c i) -> p c t i", i=4),
+            )
 
         def cast_w3(g):
             rounded = sb("w3_bf%d" % g, [P, N * PACK], BF16)
-            copy = nc.vector.tensor_copy if g == 0 else nc.scalar.copy
-            copy(
-                rounded[:].rearrange("p (c i j) -> p c j i", i=4, j=PACK),
-                w3_raw[g][:].rearrange("p j (c i) -> p c j i", i=4),
-            )
+            interleave(nc.vector.tensor_copy if g == 0 else nc.scalar.copy, rounded, w3_raw[g], 0, N)
             staged["w3", g] = rounded
 
         def quantise_weight(name, g, codes, planes):
@@ -150,150 +152,152 @@ def tile_list_readout_phase_calibration_kernel(
             nc.vector.quantize_mx(out=codes[g][:].bitcast(FP8X4), scales=planes[g][:], in_=staged[name, g][:])
 
         h_plane = sb("h_plane", [P, GROUPS * S], U8)
-        h_codes = {}
-        cosines, h_tiles = {}, {}
+        h_codes = [sb("h_codes%d" % g, [P, S], U32) for g in range(GROUPS)]
+        h_tiles, folded, cosines, pending = {}, {}, {}, {}
 
-        def phase_bank(c, g, b):
-            j0, width = CHUNKS[c]
-            per = BANK // width
+        def slices(u, b):
+            per = BANK // UNITS[u][2]
+            return range(b * per, (b + 1) * per)
+
+        def phase_bank(u, b):
+            g, j0, width = UNITS[u]
             rhs, rhs_scale = shots(j0, width)
-            bank = psum.tile([P, BANK], F32, name="phase", tag="phase")
-            mag = ring.tile([P, BANK], F32, name="mag")
-            for s in range(per):
-                t = b * per + s
+            bank = psum.tile([P, BANK // width, width], F32, name="phase", tag="phase")
+            if b == 0:
+                folded[u] = ring.tile([P, PACK * BANK], F32, name="folded", bufs=2)
+            for s, t in enumerate(slices(u, b)):
                 col = g * PASS + t * P
                 nc.tensor.matmul_mx(
-                    out=bank[:, s * width:(s + 1) * width],
+                    out=bank[:, s, :],
                     lhsT=wp_codes[:, 2 * col:2 * (col + P)].bitcast(FP4X4), lhsT_scale=wp_plane[:, col:col + P],
                     rhs=rhs, rhs_scale=rhs_scale, start=True, stop=True,
                 )
-            for s in range(per):
-                t = b * per + s
+            for s, t in enumerate(slices(u, b)):
                 nc.scalar.activation(
-                    mag[:, s * width:(s + 1) * width], bank[:, s * width:(s + 1) * width], ACT.Abs,
-                    bias=phi_sb[:, g, t:t + 1],
+                    folded[u][:, t * width:(t + 1) * width], bank[:, s, :], ACT.Abs, bias=phi_sb[:, g, t:t + 1]
                 )
-            cosines[c, g, b] = mag
 
-        def cosine(c, g, b):
-            cos = ring.tile([P, BANK], F32, name="cos", bufs=8)
-            nc.scalar.activation(cos[:], cosines[c, g, b][:], ACT.Sin, bias=math.pi / 2, scale=-1.0)
-            cosines[c, g, b] = cos
+        def cosine(u, b0, b1):
+            if b0 == 0:
+                cosines[u] = ring.tile([P, PACK * BANK], F32, name="cos", bufs=3)
+            cols = slice(b0 * BANK, b1 * BANK)
+            nc.scalar.activation(cosines[u][:, cols], folded[u][:, cols], ACT.Sin, bias=math.pi / 2, scale=-1.0)
 
-        def feature_bank(c, g, b):
-            j0, width = CHUNKS[c]
-            per = BANK // width
+        def feature_bank(u, b):
+            g, j0, width = UNITS[u]
             rhs, rhs_scale = shots(j0, width)
             if b == 0:
-                h_tiles[c, g] = sb("h%d_%d" % (c, g), [P, PACK * width], F32)
-            bank = psum.tile([P, BANK], F32, name="ampl", tag="ampl")
-            for s in range(per):
-                t = b * per + s
+                h_tiles[u] = sb("h%d" % u, [P, PACK, width], F32)
+            bank = psum.tile([P, BANK // width, width], F32, name="ampl", tag="ampl")
+            for s, t in enumerate(slices(u, b)):
                 nc.tensor.matmul_mx(
-                    out=bank[:, s * width:(s + 1) * width],
+                    out=bank[:, s, :],
                     lhsT=wa_codes[g][:, t * P:(t + 1) * P].bitcast(FP8X4), lhsT_scale=wa_planes[g][:, t * P:(t + 1) * P],
                     rhs=rhs, rhs_scale=rhs_scale, start=True, stop=True,
                 )
-            h = h_tiles[c, g]
-            nc.vector.tensor_tensor(h[:, b * BANK:(b + 1) * BANK], cosines[c, g, b][:], bank[:], ALU.mult)
+            cols = slice(b * BANK, (b + 1) * BANK)
+            h = h_tiles[u]
+            nc.vector.tensor_tensor(
+                h[:].rearrange("p t j -> p (t j)")[:, cols], cosines[u][:, cols],
+                bank[:].rearrange("p s j -> p (s j)"), ALU.mult,
+            )
             if b % 2 == 1:
-                t0, t1 = (b - 1) * per, (b + 1) * per
+                t0, t1 = slices(u, b - 1).start, slices(u, b).stop
                 rows = out_1[g * PASS:(g + 1) * PASS, j0:j0 + width].rearrange("(p t) j -> p t j", t=PACK)
-                nc.sync.dma_start(
-                    rows[:, t0:t1, :],
-                    h[:, t0 * width:t1 * width].rearrange("p (t j) -> p t j", j=width),
-                )
+                nc.sync.dma_start(rows[:, t0:t1, :], h[:, t0:t1, :])
 
-        def cast_h(c, g):
-            width = CHUNKS[c][1]
-            rounded = sb("h_bf%d_%d" % (c, g), [P, PACK * width], BF16)
-            copy = nc.scalar.copy if (c, g) == (len(CHUNKS) - 1, GROUPS - 1) else nc.vector.tensor_copy
-            copy(
-                rounded[:].rearrange("p (c i t) -> p c t i", i=4, t=PACK),
-                h_tiles[c, g][:].rearrange("p (t c i) -> p c t i", i=4, t=PACK),
-            )
-            staged["h", c, g] = rounded
+        def cast_h(u):
+            width = UNITS[u][2]
+            rounded = sb("h_bf%d" % u, [P, PACK * width], BF16)
+            split = width - SCALAR_SHARE[u]
+            if split > 0:
+                interleave(nc.vector.tensor_copy, rounded, h_tiles[u], 0, split)
+            if split < width:
+                interleave(nc.scalar.copy, rounded, h_tiles[u], split, width)
+            staged["h", u] = rounded
 
-        def quantise_h(c, g):
-            j0, width = CHUNKS[c]
-            codes = sb("h_codes%d_%d" % (c, g), [P, width], U32)
+        def quantise_h(u):
+            g, j0, width = UNITS[u]
+            codes = h_codes[g][:, j0:j0 + width]
             nc.vector.quantize_mx(
-                out=codes[:].bitcast(FP8X4), scales=h_plane[:, g * S + j0:g * S + j0 + width], in_=staged["h", c, g][:]
+                out=codes.bitcast(FP8X4), scales=h_plane[:, g * S + j0:g * S + j0 + width], in_=staged["h", u][:]
             )
-            h_codes[c, g] = codes
-            nc.sync.dma_start(
-                out_2[g].rearrange("p m t -> p (m t)").bitcast(I32)[:, j0:j0 + width], codes[:].bitcast(I32)
-            )
-            if (c, g) == (len(CHUNKS) - 1, GROUPS - 1):
+            nc.sync.dma_start(out_2[g].rearrange("p m t -> p (m t)").bitcast(I32)[:, j0:j0 + width], codes.bitcast(I32))
+            if u == len(UNITS) - 1:
                 for r in range(4):
                     nc.sync.dma_start(
                         out_3[:, r:16:4, :].rearrange("g q m -> q g m").bitcast(I32),
                         h_plane[r:P:32, :].rearrange("q (g m) -> q g m", g=GROUPS).bitcast(I32),
                     )
 
-        def result_bank(c, b):
-            j0, width = CHUNKS[c]
-            per = BANK // width
+        def response(u, b):
+            g_last, j0, width = UNITS[u]
             rhs, rhs_scale = shots(j0, width)
-            resp = psum.tile([P, BANK], F32, name="resp", tag="resp")
-            lin = psum.tile([P, BANK], F32, name="lin", tag="lin")
-            for s in range(per):
-                n0 = (b * per + s) * P
-                nc.tensor.matmul_mx(
-                    out=lin[:, s * width:(s + 1) * width],
-                    lhsT=w4_codes[:, n0:n0 + P].bitcast(FP8X4), lhsT_scale=w4_plane[:, n0:n0 + P],
-                    rhs=rhs, rhs_scale=rhs_scale, start=True, stop=True,
-                )
-            for s in range(per):
-                n0 = (b * per + s) * P
+            freed = u == len(UNITS) - 1
+            resp = psum.tile([P, BANK // width, width], F32, name="resp", tag="phase" if freed else "resp")
+            lin = psum.tile([P, BANK // width, width], F32, name="lin", tag="ampl" if freed else "lin")
+            for s, i in enumerate(slices(u, b)):
                 for g in range(GROUPS):
                     nc.tensor.matmul_mx(
-                        out=resp[:, s * width:(s + 1) * width],
-                        lhsT=w3_codes[g][:, n0:n0 + P].bitcast(FP8X4), lhsT_scale=w3_planes[g][:, n0:n0 + P],
-                        rhs=h_codes[c, g][:].bitcast(FP8X4), rhs_scale=h_plane[:, g * S + j0:g * S + j0 + width],
+                        out=resp[:, s, :],
+                        lhsT=w3_codes[g][:, i * P:(i + 1) * P].bitcast(FP8X4),
+                        lhsT_scale=w3_planes[g][:, i * P:(i + 1) * P],
+                        rhs=h_codes[g][:, j0:j0 + width].bitcast(FP8X4),
+                        rhs_scale=h_plane[:, g * S + j0:g * S + j0 + width],
                         start=(g == 0), stop=(g == GROUPS - 1),
                     )
-            sine = ring.tile([P, BANK], F32, name="sine")
-            nc.scalar.activation(sine[:], resp[:], ACT.Sin)
-            y = sb("y%d_%d" % (c, b), [P, BANK], F32)
-            for s in range(per):
-                i = b * per + s
-                cols = slice(s * width, (s + 1) * width)
-                nc.vector.scalar_tensor_tensor(
-                    y[:, cols], sine[:, cols], amp_sb[:, i, :], lin[:, cols], ALU.mult, ALU.add
+            for s, i in enumerate(slices(u, b)):
+                nc.tensor.matmul_mx(
+                    out=lin[:, s, :],
+                    lhsT=w4_codes[:, i * P:(i + 1) * P].bitcast(FP8X4), lhsT_scale=w4_plane[:, i * P:(i + 1) * P],
+                    rhs=rhs, rhs_scale=rhs_scale, start=True, stop=True,
                 )
-                nc.sync.dma_start(out_0[i * P:(i + 1) * P, j0:j0 + width], y[:, cols])
+            sine = ring.tile([P, BANK // width, width], F32, name="sine", bufs=8)
+            nc.scalar.activation(sine[:].rearrange("p s j -> p (s j)"), resp[:].rearrange("p s j -> p (s j)"), ACT.Sin)
+            pending[u, b] = sine, lin
 
-        def banks(c):
-            return PACK * CHUNKS[c][1] // BANK
+        def result(u, b, tag=None):
+            g_last, j0, width = UNITS[u]
+            sine, lin = pending[u, b]
+            y = sb("y%d_%d" % (u, b), [P, BANK // width, width], F32, tag=tag)
+            for s, i in enumerate(slices(u, b)):
+                nc.vector.scalar_tensor_tensor(y[:, s, :], sine[:, s, :], amp_sb[:, i, :], lin[:, s, :], ALU.mult, ALU.add)
+                if (u, b) == steps[-1]:
+                    nc.sync.dma_start(out_0[i * P:(i + 1) * P, j0:j0 + width], y[:, s, :])
+            if (u, b) != steps[-1]:
+                n0, n1 = slices(u, b).start * P, slices(u, b).stop * P
+                nc.sync.dma_start(out_0[n0:n1, j0:j0 + width].rearrange("(s p) j -> p s j", p=P), y[:])
 
-        steps = [(c, g, b) for c in range(len(CHUNKS)) for g in range(GROUPS) for b in range(banks(c))]
+        steps = [(u, b) for u in range(len(UNITS)) for b in range(PACK * UNITS[u][2] // BANK)]
+        after = {
+            1: [(cast_wa, 3)],
+            2: [(quantise_weight, "wa", 1, wa_codes, wa_planes)],
+            4: [(cast_h, 0), (cast_w3, 0)],
+            5: [(quantise_h, 0), (cast_w3, 1)],
+            6: [(quantise_weight, "w3", 0, w3_codes, w3_planes)],
+            7: [(quantise_weight, "w3", 1, w3_codes, w3_planes)],
+            8: [(cast_h, 1)],
+            9: [(quantise_h, 1)],
+            10: [(response, 1, 0)],
+            11: [(response, 1, 1), (result, 1, 0)],
+            12: [(cast_h, 2), (result, 1, 1)],
+            13: [(quantise_h, 2), (response, 1, 2)],
+            14: [(cast_h, 3), (response, 1, 3), (result, 1, 2)],
+            15: [(quantise_h, 3), (cast_h, 4), (result, 1, 3), (response, 3, 0), (response, 3, 1), (quantise_h, 4)]
+            + [(result, 3, 0), (result, 3, 1), (response, 4, 0), (response, 4, 1), (result, 4, 0), (result, 4, 1)],
+        }
         cast_wa(0)
+        cast_wa(1)
         quantise_weight("wa", 0, wa_codes, wa_planes)
-        later = {}
+        cast_wa(2)
         phase_bank(*steps[0])
-        for n, (c, g, b) in enumerate(steps):
+        for n, (u, b) in enumerate(steps):
             if n + 1 < len(steps):
                 phase_bank(*steps[n + 1])
-            cosine(c, g, b)
-            feature_bank(c, g, b)
-            if (c, g, b) == (0, 0, 1):
-                cast_wa(1)
-            if (c, g, b) == (0, 0, 2):
-                quantise_weight("wa", 1, wa_codes, wa_planes)
-            if c == 0 and g == 1 and b < GROUPS:
-                cast_w3(b)
-            if c == 0 and g == 1 and b >= GROUPS:
-                quantise_weight("w3", b - GROUPS, w3_codes, w3_planes)
-            for job, args in later.get(n, []):
-                job(*args)
-            if b == banks(c) - 1:
-                later.setdefault(n + 1, []).append((cast_h, (c, g)))
-                later.setdefault(n + 2, []).append((quantise_h, (c, g)))
-                if g == GROUPS - 1:
-                    for rb in range(banks(c)):
-                        delay = 3 if c == 1 else 0
-                        later.setdefault(n + 2 + rb + delay, []).append((result_bank, (c, rb)))
-        for n in range(len(steps), len(steps) + PACK):
-            for job, args in later.get(n, []):
+            if n < PACK or n >= len(steps) - 2:
+                cosine(u, b, b + 1)
+            elif b % 2 == 0:
+                cosine(u, b, b + 2)
+            feature_bank(u, b)
+            for job, *args in after.get(n, []):
                 job(*args)

@@ -25,6 +25,7 @@ BANK = 512
 LOOKUP = 512
 TAB_FIRST = 640
 UNITS = [(0, 0, 512), (1, 0, 512), (0, 512, 512), (1, 512, 256), (1, 768, 256)]
+LAST = len(UNITS) - 1
 SCALAR_SHARE = [0, 0, 128, 0, 96]
 
 
@@ -44,8 +45,8 @@ def tile_list_readout_phase_calibration_kernel(
         offsets = keep.tile([P, S // 16], U16, name="offsets")
         nc.sync.dma_start(offsets[:], offs)
 
-        def load_scale_rows(queue, fill, rows, src):
-            fill.memset(rows.bitcast(I32), 0)
+        def load_scale_rows(queue, rows, src):
+            nc.vector.memset(rows.bitcast(I32), 0)
             queue.dma_start(rows[0:P:8, :].bitcast(I32), src[0].bitcast(I32))
 
         def seat_scale_rows(plane):
@@ -55,12 +56,12 @@ def tile_list_readout_phase_calibration_kernel(
         wp_raw = sb("wp_raw", [P, 2 * H], U8)
         nc.sync.dma_start(wp_raw[:].bitcast(I32), wp_words[0].bitcast(I32))
         wp_rows = sb("wp_rows", [P, H], U8)
-        load_scale_rows(nc.sync, nc.vector, wp_rows[:], wp_scales)
+        load_scale_rows(nc.sync, wp_rows[:], wp_scales)
         tab = sb("tab", [P, T], U32)
         tab_src = tab_words[0].rearrange("p t i -> p (t i)").bitcast(I32)
         nc.sync.dma_start(tab[:, :TAB_FIRST].bitcast(I32), tab_src[:, :TAB_FIRST])
         tab_rows = sb("tab_rows", [P, T], U8)
-        load_scale_rows(nc.sync, nc.vector, tab_rows[:], tab_scales)
+        load_scale_rows(nc.sync, tab_rows[:], tab_scales)
         nc.sync.dma_start(tab[:, TAB_FIRST:].bitcast(I32), tab_src[:, TAB_FIRST:])
 
         phi_sb = sb("phi_sb", [P, GROUPS, 2 * PACK], F32)
@@ -69,19 +70,19 @@ def tile_list_readout_phase_calibration_kernel(
         later_planes = sb("later_planes", [P, LOOKUP + N], U8)
         wp_plane, w4_plane = first_planes[:, LOOKUP:], later_planes[:, LOOKUP:]
         v_planes = [first_planes[:, :LOOKUP], later_planes[:, :LOOKUP]]
-        load_scale_rows(nc.scalar, nc.vector, w4_plane, w4_scales)
+        load_scale_rows(nc.scalar, w4_plane, w4_scales)
         zero = sb("zero", [P, 1], F32)
         nc.vector.memset(zero[:], 0.0)
         warm = sb("warm", [P, 1], F32)
         nc.scalar.activation(warm[:], zero[:], ACT.Sin)
 
-        def list_part(u):
-            return offsets[:, u * LOOKUP // 16:(u + 1) * LOOKUP // 16]
+        def list_part(part):
+            return offsets[:, part * LOOKUP // 16:(part + 1) * LOOKUP // 16]
 
-        def look_up_scales(u):
-            picked = sb("v_rows%d" % u, [P, LOOKUP], U8, tag="v_rows")
-            nc.vector.tensor_copy(picked[:], tab_rows[:].indirect(list_part(u)))
-            nc.vector.tensor_copy(v_planes[u].bitcast(I32), picked[:].bitcast(I32))
+        def look_up_scales(part):
+            picked = sb("v_rows%d" % part, [P, LOOKUP], U8, tag="v_rows")
+            nc.vector.tensor_copy(picked[:], tab_rows[:].indirect(list_part(part)))
+            nc.vector.tensor_copy(v_planes[part].bitcast(I32), picked[:].bitcast(I32))
 
         look_up_scales(0)
         nc.vector.tensor_copy(
@@ -96,10 +97,10 @@ def tile_list_readout_phase_calibration_kernel(
         )
         wa_raw, w3_raw, v_codes = [], [], []
         wa_parts = [(g, c0, PASS // 2) for g in range(GROUPS) for c0 in (0, PASS // 2)]
-        for n, (g, c0, width) in enumerate(wa_parts):
-            raw = sb("wa_raw%d" % n, [P, PACK, width], F32, tag="wp_rows" if n == 0 else None)
+        for part, (g, c0, width) in enumerate(wa_parts):
+            raw = sb("wa_raw%d" % part, [P, PACK, width], F32, tag="wp_rows" if part == 0 else None)
             src = wa[:, g * PASS + c0:g * PASS + c0 + width].rearrange("(p j) c -> p j c", j=PACK)
-            (nc.scalar if n == 0 else nc.sync).dma_start(raw[:], src)
+            (nc.scalar if part == 0 else nc.sync).dma_start(raw[:], src)
             wa_raw.append(raw)
         look_up_scales(1)
         seat_scale_rows(later_planes)
@@ -112,27 +113,26 @@ def tile_list_readout_phase_calibration_kernel(
         amp_sb = sb("amp_sb", [P, N // P, 1], F32)
         with nc.allow_non_contiguous_dma(reason="one value for each partition and row block"):
             nc.sync.dma_start(amp_sb[:, :, 0], amp.rearrange("(i p) -> p i", p=P))
-        for u in range(S // LOOKUP):
-            picked = sb("v_codes%d" % u, [P, LOOKUP], U32)
-            nc.vector.tensor_copy(picked[:], tab[:].indirect(list_part(u)))
+        for part in range(S // LOOKUP):
+            picked = sb("v_codes%d" % part, [P, LOOKUP], U32)
+            nc.vector.tensor_copy(picked[:], tab[:].indirect(list_part(part)))
             v_codes.append(picked)
 
         def shots(j0, width):
-            u, c0 = divmod(j0, LOOKUP)
-            return v_codes[u][:, c0:c0 + width].bitcast(FP8X4), v_planes[u][:, c0:c0 + width]
+            part, c0 = divmod(j0, LOOKUP)
+            return v_codes[part][:, c0:c0 + width].bitcast(FP8X4), v_planes[part][:, c0:c0 + width]
 
-        wa_codes, wa_planes, w3_codes, w3_planes = {}, {}, {}, {}
-        staged = {}
+        weight_codes, weight_planes, staged = {}, {}, {}
 
-        def cast_wa(n):
-            g, c0, width = wa_parts[n]
+        def round_wa(part):
+            g, c0, width = wa_parts[part]
             if c0 == 0:
                 staged["wa", g] = sb("wa_bf%d" % g, [P, PASS * PACK], BF16)
             dealt = staged["wa", g][:].rearrange("p (t m j) -> p m t j", t=PACK, j=PACK)
-            copy = nc.scalar.copy if n == 0 else nc.vector.tensor_copy
+            copy = nc.scalar.copy if part == 0 else nc.vector.tensor_copy
             copy(
                 dealt[:, c0 // PACK:(c0 + width) // PACK],
-                wa_raw[n][:].rearrange("p j (m t) -> p m t j", t=PACK),
+                wa_raw[part][:].rearrange("p j (m t) -> p m t j", t=PACK),
             )
 
         def interleave(copy, rounded, rows, c0, c1):
@@ -141,21 +141,31 @@ def tile_list_readout_phase_calibration_kernel(
                 rows[:, :, c0:c1].rearrange("p t (c i) -> p c t i", i=4),
             )
 
-        def cast_w3(g):
+        def round_w3(g):
             rounded = sb("w3_bf%d" % g, [P, N * PACK], BF16)
             interleave(nc.vector.tensor_copy if g == 0 else nc.scalar.copy, rounded, w3_raw[g], 0, N)
             staged["w3", g] = rounded
 
-        def quantise_weight(name, g, codes, planes):
-            codes[g] = sb("%s_codes%d" % (name, g), [P, PASS], U32)
-            planes[g] = sb("%s_plane%d" % (name, g), [P, PASS], U8)
-            nc.vector.quantize_mx(out=codes[g][:].bitcast(FP8X4), scales=planes[g][:], in_=staged[name, g][:])
+        def quantise_weight(name, g, calls=1):
+            codes = sb("%s_codes%d" % (name, g), [P, PASS], U32)
+            plane = sb("%s_plane%d" % (name, g), [P, PASS], U8)
+            size = PASS // calls
+            for c0 in range(0, PASS, size):
+                nc.vector.quantize_mx(
+                    out=codes[:, c0:c0 + size].bitcast(FP8X4), scales=plane[:, c0:c0 + size],
+                    in_=staged[name, g][:, PACK * c0:PACK * (c0 + size)],
+                )
+            weight_codes[name, g], weight_planes[name, g] = codes, plane
+
+        def stationary(name, g, block):
+            cols = slice(block * P, (block + 1) * P)
+            return weight_codes[name, g][:, cols].bitcast(FP8X4), weight_planes[name, g][:, cols]
 
         h_plane = sb("h_plane", [P, GROUPS * S], U8)
         h_codes = [sb("h_codes%d" % g, [P, S], U32) for g in range(GROUPS)]
         h_tiles, folded, cosines, pending = {}, {}, {}, {}
 
-        def slices(u, b):
+        def blocks(u, b):
             per = BANK // UNITS[u][2]
             return range(b * per, (b + 1) * per)
 
@@ -165,14 +175,14 @@ def tile_list_readout_phase_calibration_kernel(
             bank = psum.tile([P, BANK // width, width], F32, name="phase", tag="phase")
             if b == 0:
                 folded[u] = ring.tile([P, PACK * BANK], F32, name="folded", bufs=2)
-            for s, t in enumerate(slices(u, b)):
+            for s, t in enumerate(blocks(u, b)):
                 col = g * PASS + t * P
                 nc.tensor.matmul_mx(
                     out=bank[:, s, :],
                     lhsT=wp_codes[:, 2 * col:2 * (col + P)].bitcast(FP4X4), lhsT_scale=wp_plane[:, col:col + P],
                     rhs=rhs, rhs_scale=rhs_scale, start=True, stop=True,
                 )
-            for s, t in enumerate(slices(u, b)):
+            for s, t in enumerate(blocks(u, b)):
                 nc.scalar.activation(
                     folded[u][:, t * width:(t + 1) * width], bank[:, s, :], ACT.Abs, bias=phi_sb[:, g, t:t + 1]
                 )
@@ -189,10 +199,10 @@ def tile_list_readout_phase_calibration_kernel(
             if b == 0:
                 h_tiles[u] = sb("h%d" % u, [P, PACK, width], F32)
             bank = psum.tile([P, BANK // width, width], F32, name="ampl", tag="ampl")
-            for s, t in enumerate(slices(u, b)):
+            for s, t in enumerate(blocks(u, b)):
+                lhsT, lhsT_scale = stationary("wa", g, t)
                 nc.tensor.matmul_mx(
-                    out=bank[:, s, :],
-                    lhsT=wa_codes[g][:, t * P:(t + 1) * P].bitcast(FP8X4), lhsT_scale=wa_planes[g][:, t * P:(t + 1) * P],
+                    out=bank[:, s, :], lhsT=lhsT, lhsT_scale=lhsT_scale,
                     rhs=rhs, rhs_scale=rhs_scale, start=True, stop=True,
                 )
             cols = slice(b * BANK, (b + 1) * BANK)
@@ -202,16 +212,15 @@ def tile_list_readout_phase_calibration_kernel(
                 bank[:].rearrange("p s j -> p (s j)"), ALU.mult,
             )
             if b % 2 == 1:
-                t0, t1 = slices(u, b - 1).start, slices(u, b).stop
+                t0, t1 = blocks(u, b - 1).start, blocks(u, b).stop
                 rows = out_1[g * PASS:(g + 1) * PASS, j0:j0 + width].rearrange("(p t) j -> p t j", t=PACK)
                 nc.sync.dma_start(rows[:, t0:t1, :], h[:, t0:t1, :])
 
-        def cast_h(u):
+        def round_h(u):
             width = UNITS[u][2]
             rounded = sb("h_bf%d" % u, [P, PACK * width], BF16)
             split = width - SCALAR_SHARE[u]
-            if split > 0:
-                interleave(nc.vector.tensor_copy, rounded, h_tiles[u], 0, split)
+            interleave(nc.vector.tensor_copy, rounded, h_tiles[u], 0, split)
             if split < width:
                 interleave(nc.scalar.copy, rounded, h_tiles[u], split, width)
             staged["h", u] = rounded
@@ -223,7 +232,7 @@ def tile_list_readout_phase_calibration_kernel(
                 out=codes.bitcast(FP8X4), scales=h_plane[:, g * S + j0:g * S + j0 + width], in_=staged["h", u][:]
             )
             nc.sync.dma_start(out_2[g].rearrange("p m t -> p (m t)").bitcast(I32)[:, j0:j0 + width], codes.bitcast(I32))
-            if u == len(UNITS) - 1:
+            if u == LAST:
                 for r in range(4):
                     nc.sync.dma_start(
                         out_3[:, r:16:4, :].rearrange("g q m -> q g m").bitcast(I32),
@@ -231,73 +240,89 @@ def tile_list_readout_phase_calibration_kernel(
                     )
 
         def response(u, b):
-            g_last, j0, width = UNITS[u]
+            j0, width = UNITS[u][1:]
             rhs, rhs_scale = shots(j0, width)
-            freed = u == len(UNITS) - 1
-            resp = psum.tile([P, BANK // width, width], F32, name="resp", tag="phase" if freed else "resp")
-            lin = psum.tile([P, BANK // width, width], F32, name="lin", tag="ampl" if freed else "lin")
-            for s, i in enumerate(slices(u, b)):
+            resp = psum.tile([P, BANK // width, width], F32, name="resp", tag="phase" if u == LAST else "resp")
+            lin = psum.tile([P, BANK // width, width], F32, name="lin", tag="ampl" if u == LAST else "lin")
+            for s, i in enumerate(blocks(u, b)):
                 for g in range(GROUPS):
+                    lhsT, lhsT_scale = stationary("w3", g, i)
                     nc.tensor.matmul_mx(
-                        out=resp[:, s, :],
-                        lhsT=w3_codes[g][:, i * P:(i + 1) * P].bitcast(FP8X4),
-                        lhsT_scale=w3_planes[g][:, i * P:(i + 1) * P],
+                        out=resp[:, s, :], lhsT=lhsT, lhsT_scale=lhsT_scale,
                         rhs=h_codes[g][:, j0:j0 + width].bitcast(FP8X4),
                         rhs_scale=h_plane[:, g * S + j0:g * S + j0 + width],
                         start=(g == 0), stop=(g == GROUPS - 1),
                     )
-            for s, i in enumerate(slices(u, b)):
+            for s, i in enumerate(blocks(u, b)):
                 nc.tensor.matmul_mx(
                     out=lin[:, s, :],
                     lhsT=w4_codes[:, i * P:(i + 1) * P].bitcast(FP8X4), lhsT_scale=w4_plane[:, i * P:(i + 1) * P],
                     rhs=rhs, rhs_scale=rhs_scale, start=True, stop=True,
                 )
             sine = ring.tile([P, BANK // width, width], F32, name="sine", bufs=8)
-            nc.scalar.activation(sine[:].rearrange("p s j -> p (s j)"), resp[:].rearrange("p s j -> p (s j)"), ACT.Sin)
+            size = width if u == LAST else BANK
+            for c0 in range(0, BANK, size):
+                nc.scalar.activation(
+                    sine[:].rearrange("p s j -> p (s j)")[:, c0:c0 + size],
+                    resp[:].rearrange("p s j -> p (s j)")[:, c0:c0 + size], ACT.Sin,
+                )
             pending[u, b] = sine, lin
 
-        def result(u, b, tag=None):
-            g_last, j0, width = UNITS[u]
+        def result(u, b):
+            j0, width = UNITS[u][1:]
             sine, lin = pending[u, b]
-            y = sb("y%d_%d" % (u, b), [P, BANK // width, width], F32, tag=tag)
-            for s, i in enumerate(slices(u, b)):
+            y = sb("y%d_%d" % (u, b), [P, BANK // width, width], F32)
+            for s, i in enumerate(blocks(u, b)):
                 nc.vector.scalar_tensor_tensor(y[:, s, :], sine[:, s, :], amp_sb[:, i, :], lin[:, s, :], ALU.mult, ALU.add)
                 if (u, b) == steps[-1]:
                     nc.sync.dma_start(out_0[i * P:(i + 1) * P, j0:j0 + width], y[:, s, :])
             if (u, b) != steps[-1]:
-                n0, n1 = slices(u, b).start * P, slices(u, b).stop * P
+                n0, n1 = blocks(u, b).start * P, blocks(u, b).stop * P
                 nc.sync.dma_start(out_0[n0:n1, j0:j0 + width].rearrange("(s p) j -> p s j", p=P), y[:])
 
-        steps = [(u, b) for u in range(len(UNITS)) for b in range(PACK * UNITS[u][2] // BANK)]
-        after = {
-            1: [(cast_wa, 3)],
-            2: [(quantise_weight, "wa", 1, wa_codes, wa_planes)],
-            4: [(cast_h, 0), (cast_w3, 0)],
-            5: [(quantise_h, 0), (cast_w3, 1)],
-            6: [(quantise_weight, "w3", 0, w3_codes, w3_planes)],
-            7: [(quantise_weight, "w3", 1, w3_codes, w3_planes)],
-            8: [(cast_h, 1)],
-            9: [(quantise_h, 1)],
-            10: [(response, 1, 0)],
-            11: [(response, 1, 1), (result, 1, 0)],
-            12: [(cast_h, 2), (result, 1, 1)],
-            13: [(quantise_h, 2), (response, 1, 2)],
-            14: [(cast_h, 3), (response, 1, 3), (result, 1, 2)],
-            15: [(quantise_h, 3), (cast_h, 4), (result, 1, 3), (response, 3, 0), (response, 3, 1), (quantise_h, 4)]
-            + [(result, 3, 0), (result, 3, 1), (response, 4, 0), (response, 4, 1), (result, 4, 0), (result, 4, 1)],
-        }
-        cast_wa(0)
-        cast_wa(1)
-        quantise_weight("wa", 0, wa_codes, wa_planes)
-        cast_wa(2)
+        def banks(u):
+            return range(PACK * UNITS[u][2] // BANK)
+
+        steps = [(u, b) for u in range(len(UNITS)) for b in banks(u)]
+        final = len(steps) - 1
+        round_at = [min(steps.index((u, banks(u)[-1])) + 1, final) for u in range(len(UNITS))]
+        w3_at = [round_at[0] + g for g in range(GROUPS)]
+        respond_at = [n for n in range(round_at[1] + 2, final) if n != round_at[2]]
+
+        round_wa(0)
+        round_wa(1)
+        quantise_weight("wa", 0, calls=2)
+        round_wa(2)
         phase_bank(*steps[0])
         for n, (u, b) in enumerate(steps):
-            if n + 1 < len(steps):
+            if n < final:
                 phase_bank(*steps[n + 1])
-            if n < PACK or n >= len(steps) - 2:
+            if u in (0, LAST):
                 cosine(u, b, b + 1)
             elif b % 2 == 0:
                 cosine(u, b, b + 2)
             feature_bank(u, b)
-            for job, *args in after.get(n, []):
-                job(*args)
+            if n == 1:
+                round_wa(3)
+            if n == 2:
+                quantise_weight("wa", 1)
+            if n - 1 in round_at:
+                quantise_h(round_at.index(n - 1))
+            if n in round_at:
+                round_h(round_at.index(n))
+            if n in w3_at:
+                round_w3(w3_at.index(n))
+            if n - 2 in w3_at:
+                quantise_weight("w3", w3_at.index(n - 2))
+            if n in respond_at:
+                response(1, respond_at.index(n))
+            if n - 1 in respond_at:
+                result(1, respond_at.index(n - 1))
+        for b in banks(LAST - 1):
+            response(LAST - 1, b)
+        quantise_h(LAST)
+        for b in banks(LAST - 1):
+            result(LAST - 1, b)
+        for job in (response, result):
+            for b in banks(LAST):
+                job(LAST, b)

@@ -24,9 +24,8 @@ GROUPS = H // PASS
 BANK = 512
 LOOKUP = 512
 TAB_FIRST = 640
-UNITS = [(0, 0, 512), (1, 0, 512), (0, 512, 512), (1, 512, 256), (1, 768, 256)]
+UNITS = [(0, 0, 512), (1, 0, 512), (0, 512, 512), (1, 512, 512)]
 LAST = len(UNITS) - 1
-SCALAR_SHARE = [0, 0, 128, 0, 96]
 
 
 def tile_list_readout_phase_calibration_kernel(
@@ -36,7 +35,7 @@ def tile_list_readout_phase_calibration_kernel(
     nc = tc.nc
     with ExitStack() as ctx:
         keep = ctx.enter_context(tc.tile_pool(name="keep", bufs=1))
-        psum = ctx.enter_context(tc.psum_pool(name="psum", bufs=2))
+        psum = ctx.enter_context(tc.psum_pool(name="psum", bufs=1))
         ring = ctx.enter_context(tc.tile_pool(name="ring", bufs=4))
 
         def sb(name, shape, dtype, tag=None):
@@ -141,10 +140,25 @@ def tile_list_readout_phase_calibration_kernel(
                 rows[:, :, c0:c1].rearrange("p t (c i) -> p c t i", i=4),
             )
 
-        def round_w3(g):
-            rounded = sb("w3_bf%d" % g, [P, N * PACK], BF16)
-            interleave(nc.vector.tensor_copy if g == 0 else nc.scalar.copy, rounded, w3_raw[g], 0, N)
-            staged["w3", g] = rounded
+        def on_vector(rounded, rows, c0, c1):
+            interleave(nc.vector.tensor_copy, rounded, rows, c0, c1)
+
+        def on_scalar(rounded, rows, c0, c1):
+            interleave(nc.scalar.copy, rounded, rows, c0, c1)
+
+        def on_gpsimd(rounded, rows, c0, c1):
+            nc.gpsimd.tensor_scalar(
+                rounded[:, PACK * c0:PACK * c1].rearrange("p (c t) -> p c t", t=PACK),
+                rows[:, :, c0:c1].rearrange("p t c -> p c t"), 1.0, 1.0, ALU.mult, ALU.mult,
+            )
+
+        def round_part(key, rows, how, c0, c1, tag):
+            if key not in staged:
+                staged[key] = sb("%s_bf%d" % key, [P, PACK * rows.shape[2]], BF16, tag=tag)
+            how(staged[key], rows, c0, c1)
+
+        def round_w3(g, how, c0=0, c1=N, tag=None):
+            round_part(("w3", g), w3_raw[g], how, c0, c1, tag)
 
         def quantise_weight(name, g, calls=1):
             codes = sb("%s_codes%d" % (name, g), [P, PASS], U32)
@@ -169,10 +183,29 @@ def tile_list_readout_phase_calibration_kernel(
             per = BANK // UNITS[u][2]
             return range(b * per, (b + 1) * per)
 
+        def banks(u):
+            return range(PACK * UNITS[u][2] // BANK)
+
+        steps = [(u, b) for u in range(len(UNITS)) for b in banks(u)]
+
+        results = [(u, b) for u, b in steps if UNITS[u][0] == GROUPS - 1]
+
+        def phase_tag(u, b):
+            return "bank%d" % (steps.index((u, b)) % 4)
+
+        def ampl_tag(u, b):
+            return "bank%d" % (4 + steps.index((u, b)) % 4)
+
+        def resp_tag(u, b):
+            return "bank%d" % (results.index((u, b)) % 4)
+
+        def lin_tag(u, b):
+            return "bank%d" % (4 + results.index((u, b)) % 4)
+
         def phase_bank(u, b):
             g, j0, width = UNITS[u]
             rhs, rhs_scale = shots(j0, width)
-            bank = psum.tile([P, BANK // width, width], F32, name="phase", tag="phase")
+            bank = psum.tile([P, BANK // width, width], F32, name="phase", tag=phase_tag(u, b))
             if b == 0:
                 folded[u] = ring.tile([P, PACK * BANK], F32, name="folded", bufs=2)
             for s, t in enumerate(blocks(u, b)):
@@ -198,7 +231,7 @@ def tile_list_readout_phase_calibration_kernel(
             rhs, rhs_scale = shots(j0, width)
             if b == 0:
                 h_tiles[u] = sb("h%d" % u, [P, PACK, width], F32)
-            bank = psum.tile([P, BANK // width, width], F32, name="ampl", tag="ampl")
+            bank = psum.tile([P, BANK // width, width], F32, name="ampl", tag=ampl_tag(u, b))
             for s, t in enumerate(blocks(u, b)):
                 lhsT, lhsT_scale = stationary("wa", g, t)
                 nc.tensor.matmul_mx(
@@ -211,19 +244,13 @@ def tile_list_readout_phase_calibration_kernel(
                 h[:].rearrange("p t j -> p (t j)")[:, cols], cosines[u][:, cols],
                 bank[:].rearrange("p s j -> p (s j)"), ALU.mult,
             )
-            if b % 2 == 1:
-                t0, t1 = blocks(u, b - 1).start, blocks(u, b).stop
+            if b % 2 == 1 or b == banks(u)[-1]:
+                t0, t1 = blocks(u, b - b % 2).start, blocks(u, b).stop
                 rows = out_1[g * PASS:(g + 1) * PASS, j0:j0 + width].rearrange("(p t) j -> p t j", t=PACK)
                 nc.sync.dma_start(rows[:, t0:t1, :], h[:, t0:t1, :])
 
-        def round_h(u):
-            width = UNITS[u][2]
-            rounded = sb("h_bf%d" % u, [P, PACK * width], BF16)
-            split = width - SCALAR_SHARE[u]
-            interleave(nc.vector.tensor_copy, rounded, h_tiles[u], 0, split)
-            if split < width:
-                interleave(nc.scalar.copy, rounded, h_tiles[u], split, width)
-            staged["h", u] = rounded
+        def round_h(u, how, c0=0, c1=None, tag=None):
+            round_part(("h", u), h_tiles[u], how, c0, c1 or UNITS[u][2], tag)
 
         def quantise_h(u):
             g, j0, width = UNITS[u]
@@ -242,16 +269,16 @@ def tile_list_readout_phase_calibration_kernel(
         def response(u, b):
             j0, width = UNITS[u][1:]
             rhs, rhs_scale = shots(j0, width)
-            resp = psum.tile([P, BANK // width, width], F32, name="resp", tag="phase" if u == LAST else "resp")
-            lin = psum.tile([P, BANK // width, width], F32, name="lin", tag="ampl" if u == LAST else "lin")
-            for s, i in enumerate(blocks(u, b)):
-                for g in range(GROUPS):
+            resp = psum.tile([P, BANK // width, width], F32, name="resp", tag=resp_tag(u, b))
+            lin = psum.tile([P, BANK // width, width], F32, name="lin", tag=lin_tag(u, b))
+            for g in range(GROUPS):
+                for s, i in enumerate(blocks(u, b)):
                     lhsT, lhsT_scale = stationary("w3", g, i)
                     nc.tensor.matmul_mx(
                         out=resp[:, s, :], lhsT=lhsT, lhsT_scale=lhsT_scale,
                         rhs=h_codes[g][:, j0:j0 + width].bitcast(FP8X4),
                         rhs_scale=h_plane[:, g * S + j0:g * S + j0 + width],
-                        start=(g == 0), stop=(g == GROUPS - 1),
+                        start=(g == 0 and s == 0), stop=(g == GROUPS - 1 and i == blocks(u, b)[-1]),
                     )
             for s, i in enumerate(blocks(u, b)):
                 nc.tensor.matmul_mx(
@@ -260,7 +287,7 @@ def tile_list_readout_phase_calibration_kernel(
                     rhs=rhs, rhs_scale=rhs_scale, start=True, stop=True,
                 )
             sine = ring.tile([P, BANK // width, width], F32, name="sine", bufs=8)
-            size = width if u == LAST else BANK
+            size = BANK
             for c0 in range(0, BANK, size):
                 nc.scalar.activation(
                     sine[:].rearrange("p s j -> p (s j)")[:, c0:c0 + size],
@@ -274,55 +301,67 @@ def tile_list_readout_phase_calibration_kernel(
             y = sb("y%d_%d" % (u, b), [P, BANK // width, width], F32)
             for s, i in enumerate(blocks(u, b)):
                 nc.vector.scalar_tensor_tensor(y[:, s, :], sine[:, s, :], amp_sb[:, i, :], lin[:, s, :], ALU.mult, ALU.add)
-                if (u, b) == steps[-1]:
-                    nc.sync.dma_start(out_0[i * P:(i + 1) * P, j0:j0 + width], y[:, s, :])
-            if (u, b) != steps[-1]:
-                n0, n1 = blocks(u, b).start * P, blocks(u, b).stop * P
-                nc.sync.dma_start(out_0[n0:n1, j0:j0 + width].rearrange("(s p) j -> p s j", p=P), y[:])
+                per = 1 if (u, b) == steps[-1] else len(blocks(u, b))
+                if (s + 1) % per == 0:
+                    rows = out_0[(i + 1 - per) * P:(i + 1) * P, j0:j0 + width]
+                    nc.sync.dma_start(rows.rearrange("(s p) j -> p s j", p=P), y[:, s + 1 - per:s + 1, :])
 
-        def banks(u):
-            return range(PACK * UNITS[u][2] // BANK)
-
-        steps = [(u, b) for u in range(len(UNITS)) for b in banks(u)]
-        final = len(steps) - 1
-        round_at = [min(steps.index((u, banks(u)[-1])) + 1, final) for u in range(len(UNITS))]
-        w3_at = [round_at[0] + g for g in range(GROUPS)]
-        respond_at = [n for n in range(round_at[1] + 2, final) if n != round_at[2]]
+        def step(u, b):
+            n = steps.index((u, b))
+            if n + 1 < len(steps):
+                phase_bank(*steps[n + 1])
+            if u == 0 or n >= len(steps) - 2:
+                cosine(u, b, b + 1)
+            elif b % 2 == 0:
+                cosine(u, b, b + 2)
+            feature_bank(u, b)
 
         round_wa(0)
         round_wa(1)
         quantise_weight("wa", 0, calls=2)
         round_wa(2)
         phase_bank(*steps[0])
-        for n, (u, b) in enumerate(steps):
-            if n < final:
-                phase_bank(*steps[n + 1])
-            if u in (0, LAST):
-                cosine(u, b, b + 1)
-            elif b % 2 == 0:
-                cosine(u, b, b + 2)
-            feature_bank(u, b)
-            if n == 1:
-                round_wa(3)
-            if n == 2:
-                quantise_weight("wa", 1)
-            if n - 1 in round_at:
-                quantise_h(round_at.index(n - 1))
-            if n in round_at:
-                round_h(round_at.index(n))
-            if n in w3_at:
-                round_w3(w3_at.index(n))
-            if n - 2 in w3_at:
-                quantise_weight("w3", w3_at.index(n - 2))
-            if n in respond_at:
-                response(1, respond_at.index(n))
-            if n - 1 in respond_at:
-                result(1, respond_at.index(n - 1))
-        for b in banks(LAST - 1):
-            response(LAST - 1, b)
-        quantise_h(LAST)
-        for b in banks(LAST - 1):
-            result(LAST - 1, b)
+        step(0, 0)
+        step(0, 1)
+        round_wa(3)
+        step(0, 2)
+        quantise_weight("wa", 1)
+        step(0, 3)
+        step(1, 0)
+        step(1, 1)
+        round_h(0, on_vector)
+        step(1, 2)
+        step(1, 3)
+        quantise_h(0)
+        round_w3(0, on_vector)
+        step(2, 0)
+        step(2, 1)
+        quantise_weight("w3", 0)
+        round_h(1, on_vector)
+        step(2, 2)
+        round_w3(1, on_scalar, 0, 192)
+        step(2, 3)
+        quantise_h(1)
+        round_w3(1, on_vector, 192, N)
+        step(3, 0)
+        step(3, 1)
+        quantise_weight("w3", 1)
+        step(3, 2)
+        step(3, 3)
+        response(1, 0)
+        round_h(2, on_scalar, 128, 512)
+        round_h(2, on_vector, 0, 128)
+        response(1, 1)
+        round_h(3, on_vector, 0, 352)
+        round_h(3, on_scalar, 352, 512)
+        result(1, 0)
+        quantise_h(2)
+        quantise_h(3)
+        response(1, 2)
+        response(1, 3)
+        result(1, 1)
+        result(1, 2)
+        result(1, 3)
         for job in (response, result):
             for b in banks(LAST):
                 job(LAST, b)

@@ -102,11 +102,12 @@ def tile_list_readout_phase_calibration_kernel(
             (nc.scalar if part == 0 else nc.sync).dma_start(raw[:], src)
             wa_raw.append(raw)
         look_up_scales(1)
-        seat_scale_rows(later_planes)
         for g in range(GROUPS):
             raw = sb("w3_raw%d" % g, [P, PACK, N], F32)
             nc.sync.dma_start(raw[:], w3[g * PASS:(g + 1) * PASS, :].rearrange("(p j) n -> p j n", j=PACK))
             w3_raw.append(raw)
+            if g == 0:
+                seat_scale_rows(later_planes)
         w4_codes = sb("w4_codes", [P, N], U32)
         nc.sync.dma_start(w4_codes[:].bitcast(I32), w4_words[0].rearrange("p c i -> p (c i)").bitcast(I32))
         amp_sb = sb("amp_sb", [P, N // P, 1], F32)
@@ -126,8 +127,8 @@ def tile_list_readout_phase_calibration_kernel(
         def round_wa(part):
             g, c0, width = wa_parts[part]
             if c0 == 0:
-                staged["wa", g] = sb("wa_bf%d" % g, [P, PASS * PACK], BF16)
-            dealt = staged["wa", g][:].rearrange("p (t m j) -> p m t j", t=PACK, j=PACK)
+                staged["wa", g, 0] = sb("wa_bf%d" % g, [P, PASS * PACK], BF16)
+            dealt = staged["wa", g, 0][:].rearrange("p (t m j) -> p m t j", t=PACK, j=PACK)
             copy = nc.scalar.copy if part == 0 else nc.vector.tensor_copy
             copy(
                 dealt[:, c0 // PACK:(c0 + width) // PACK],
@@ -152,24 +153,22 @@ def tile_list_readout_phase_calibration_kernel(
                 rows[:, :, c0:c1].rearrange("p t c -> p c t"), 1.0, 1.0, ALU.mult, ALU.mult,
             )
 
-        def round_part(key, rows, how, c0, c1, tag):
-            if key not in staged:
-                staged[key] = sb("%s_bf%d" % key, [P, PACK * rows.shape[2]], BF16, tag=tag)
-            how(staged[key], rows, c0, c1)
+        def round_part(key, rows, how, c0, c1, first, width, tag):
+            if key + (first,) not in staged:
+                staged[key + (first,)] = sb("%s_bf%d_%d" % (key + (first,)), [P, PACK * width], BF16, tag=tag)
+            how(staged[key + (first,)], rows[:, :, first:first + width], c0 - first, c1 - first)
 
-        def round_w3(g, how, c0=0, c1=N, tag=None):
-            round_part(("w3", g), w3_raw[g], how, c0, c1, tag)
+        def round_w3(g, how, c0=0, c1=N, tile=(0, N), tag=None):
+            round_part(("w3", g), w3_raw[g], how, c0, c1, tile[0], tile[1], tag)
 
-        def quantise_weight(name, g, calls=1):
-            codes = sb("%s_codes%d" % (name, g), [P, PASS], U32)
-            plane = sb("%s_plane%d" % (name, g), [P, PASS], U8)
-            size = PASS // calls
-            for c0 in range(0, PASS, size):
-                nc.vector.quantize_mx(
-                    out=codes[:, c0:c0 + size].bitcast(FP8X4), scales=plane[:, c0:c0 + size],
-                    in_=staged[name, g][:, PACK * c0:PACK * (c0 + size)],
-                )
-            weight_codes[name, g], weight_planes[name, g] = codes, plane
+        def quantise_weight(name, g, c0=0, c1=PASS, first=0):
+            if (name, g) not in weight_codes:
+                weight_codes[name, g] = sb("%s_codes%d" % (name, g), [P, PASS], U32)
+                weight_planes[name, g] = sb("%s_plane%d" % (name, g), [P, PASS], U8)
+            nc.vector.quantize_mx(
+                out=weight_codes[name, g][:, c0:c1].bitcast(FP8X4), scales=weight_planes[name, g][:, c0:c1],
+                in_=staged[name, g, first][:, PACK * (c0 - first):PACK * (c1 - first)],
+            )
 
         def stationary(name, g, block):
             cols = slice(block * P, (block + 1) * P)
@@ -230,7 +229,7 @@ def tile_list_readout_phase_calibration_kernel(
             g, j0, width = UNITS[u]
             rhs, rhs_scale = shots(j0, width)
             if b == 0:
-                h_tiles[u] = sb("h%d" % u, [P, PACK, width], F32)
+                h_tiles[u] = sb("h%d" % u, [P, PACK, width], F32, tag="w3_raw0" if u == 1 else None)
             bank = psum.tile([P, BANK // width, width], F32, name="ampl", tag=ampl_tag(u, b))
             for s, t in enumerate(blocks(u, b)):
                 lhsT, lhsT_scale = stationary("wa", g, t)
@@ -249,16 +248,20 @@ def tile_list_readout_phase_calibration_kernel(
                 rows = out_1[g * PASS:(g + 1) * PASS, j0:j0 + width].rearrange("(p t) j -> p t j", t=PACK)
                 nc.sync.dma_start(rows[:, t0:t1, :], h[:, t0:t1, :])
 
-        def round_h(u, how, c0=0, c1=None, tag=None):
-            round_part(("h", u), h_tiles[u], how, c0, c1 or UNITS[u][2], tag)
+        def round_h(u, how, c0=0, c1=BANK, tile=(0, BANK), tag=None):
+            round_part(("h", u), h_tiles[u], how, c0, c1, tile[0], tile[1], tag)
 
-        def quantise_h(u):
+        def quantise_h(u, c0=0, c1=BANK):
             g, j0, width = UNITS[u]
-            codes = h_codes[g][:, j0:j0 + width]
             nc.vector.quantize_mx(
-                out=codes.bitcast(FP8X4), scales=h_plane[:, g * S + j0:g * S + j0 + width], in_=staged["h", u][:]
+                out=h_codes[g][:, j0 + c0:j0 + c1].bitcast(FP8X4),
+                scales=h_plane[:, g * S + j0 + c0:g * S + j0 + c1], in_=staged["h", u, c0][:],
             )
-            nc.sync.dma_start(out_2[g].rearrange("p m t -> p (m t)").bitcast(I32)[:, j0:j0 + width], codes.bitcast(I32))
+
+        def store_codes(u):
+            g, j0, width = UNITS[u]
+            words = out_2[g].rearrange("p m t -> p (m t)").bitcast(I32)
+            nc.sync.dma_start(words[:, j0:j0 + width], h_codes[g][:, j0:j0 + width].bitcast(I32))
             if u == LAST:
                 for r in range(4):
                     nc.sync.dma_start(
@@ -318,7 +321,8 @@ def tile_list_readout_phase_calibration_kernel(
 
         round_wa(0)
         round_wa(1)
-        quantise_weight("wa", 0, calls=2)
+        quantise_weight("wa", 0, 0, 256)
+        quantise_weight("wa", 0, 256, 512)
         round_wa(2)
         phase_bank(*steps[0])
         step(0, 0)
@@ -327,39 +331,40 @@ def tile_list_readout_phase_calibration_kernel(
         step(0, 2)
         quantise_weight("wa", 1)
         step(0, 3)
-        step(1, 0)
-        step(1, 1)
-        round_h(0, on_vector)
-        step(1, 2)
-        step(1, 3)
-        quantise_h(0)
         round_w3(0, on_vector)
-        step(2, 0)
-        step(2, 1)
+        round_h(0, on_vector, 0, 256, (0, 256))
         quantise_weight("w3", 0)
+        quantise_h(0, 0, 256)
+        round_h(0, on_gpsimd, 256, 512, (256, 256), "w3_bf0_0")
+        for b in banks(1):
+            step(1, b)
+        round_w3(1, on_vector, 0, 128, (0, 128))
         round_h(1, on_vector)
-        step(2, 2)
-        round_w3(1, on_scalar, 0, 192)
-        step(2, 3)
+        quantise_weight("w3", 1, 0, 128)
+        quantise_h(0, 256, 512)
+        store_codes(0)
         quantise_h(1)
-        round_w3(1, on_vector, 192, N)
-        step(3, 0)
-        step(3, 1)
-        quantise_weight("w3", 1)
-        step(3, 2)
-        step(3, 3)
+        store_codes(1)
+        round_w3(1, on_gpsimd, 128, 512, (128, 384), "w3_bf0_0")
+        for b in banks(2):
+            step(2, b)
+        quantise_weight("w3", 1, 128, 512, 128)
+        round_h(2, on_gpsimd, 128, 512, tag="w3_bf0_0")
+        for b in banks(3):
+            step(3, b)
         response(1, 0)
-        round_h(2, on_scalar, 128, 512)
-        round_h(2, on_vector, 0, 128)
-        response(1, 1)
-        round_h(3, on_vector, 0, 352)
-        round_h(3, on_scalar, 352, 512)
+        round_h(2, on_scalar, 0, 128)
         result(1, 0)
+        round_h(3, on_vector, 0, 320)
+        round_h(3, on_scalar, 320, 512)
+        response(1, 1)
         quantise_h(2)
+        store_codes(2)
         quantise_h(3)
+        store_codes(3)
+        result(1, 1)
         response(1, 2)
         response(1, 3)
-        result(1, 1)
         result(1, 2)
         result(1, 3)
         for job in (response, result):

@@ -23,9 +23,11 @@ PASS = P * PACK
 GROUPS = H // PASS
 BANK = 512
 LOOKUP = 512
-TAB_FIRST = 640
+TAB_FIRST = 800
 UNITS = [(0, 0, 512), (1, 0, 512), (0, 512, 512), (1, 512, 512)]
 LAST = len(UNITS) - 1
+PHASE_BANKS, AMPL_BANKS = (0, 1, 4, 5), (2, 3, 6, 7)
+SPANS = [(0, 512), (512, 256), (768, 256)]
 
 
 def tile_list_readout_phase_calibration_kernel(
@@ -52,6 +54,11 @@ def tile_list_readout_phase_calibration_kernel(
             for r in range(1, 4):
                 nc.sync.dma_start(plane[r:P:32, :].bitcast(I32), plane[8 * r:P:32, :].bitcast(I32))
 
+        first_planes = sb("first_planes", [P, LOOKUP + H], U8)
+        later_planes = sb("later_planes", [P, LOOKUP + N], U8)
+        wp_plane, w4_plane = first_planes[:, LOOKUP:], later_planes[:, LOOKUP:]
+        v_planes = [first_planes[:, :LOOKUP], later_planes[:, :LOOKUP]]
+        load_scale_rows(nc.scalar, w4_plane, w4_scales)
         wp_raw = sb("wp_raw", [P, 2 * H], U8)
         nc.sync.dma_start(wp_raw[:].bitcast(I32), wp_words[0].bitcast(I32))
         wp_rows = sb("wp_rows", [P, H], U8)
@@ -65,11 +72,6 @@ def tile_list_readout_phase_calibration_kernel(
 
         phi_sb = sb("phi_sb", [P, GROUPS, 2 * PACK], F32)
         nc.scalar.dma_start(phi_sb[:, :, :PACK], phi.rearrange("(g p t) -> p g t", g=GROUPS, t=PACK))
-        first_planes = sb("first_planes", [P, LOOKUP + H], U8)
-        later_planes = sb("later_planes", [P, LOOKUP + N], U8)
-        wp_plane, w4_plane = first_planes[:, LOOKUP:], later_planes[:, LOOKUP:]
-        v_planes = [first_planes[:, :LOOKUP], later_planes[:, :LOOKUP]]
-        load_scale_rows(nc.scalar, w4_plane, w4_scales)
         zero = sb("zero", [P, 1], F32)
         nc.vector.memset(zero[:], 0.0)
         warm = sb("warm", [P, 1], F32)
@@ -95,7 +97,7 @@ def tile_list_readout_phase_calibration_kernel(
             wp_raw[:].bitcast(U16).rearrange("p (g m t) -> p g t m", g=GROUPS, t=PACK),
         )
         wa_raw, w3_raw, v_codes = [], [], []
-        wa_parts = [(g, c0, PASS // 2) for g in range(GROUPS) for c0 in (0, PASS // 2)]
+        wa_parts = [(0, 0, 128), (0, 128, 192), (0, 320, 192), (1, 0, 256), (1, 256, 256)]
         for part, (g, c0, width) in enumerate(wa_parts):
             raw = sb("wa_raw%d" % part, [P, PACK, width], F32, tag="wp_rows" if part == 0 else None)
             src = wa[:, g * PASS + c0:g * PASS + c0 + width].rearrange("(p j) c -> p j c", j=PACK)
@@ -187,19 +189,11 @@ def tile_list_readout_phase_calibration_kernel(
 
         steps = [(u, b) for u in range(len(UNITS)) for b in banks(u)]
 
-        results = [(u, b) for u, b in steps if UNITS[u][0] == GROUPS - 1]
-
         def phase_tag(u, b):
-            return "bank%d" % (steps.index((u, b)) % 4)
+            return "bank%d" % (PHASE_BANKS[b] if u > 0 else b)
 
         def ampl_tag(u, b):
-            return "bank%d" % (4 + steps.index((u, b)) % 4)
-
-        def resp_tag(u, b):
-            return "bank%d" % (results.index((u, b)) % 4)
-
-        def lin_tag(u, b):
-            return "bank%d" % (4 + results.index((u, b)) % 4)
+            return "bank%d" % (AMPL_BANKS[b] if u > 0 else 4 + b)
 
         def phase_bank(u, b):
             g, j0, width = UNITS[u]
@@ -269,42 +263,52 @@ def tile_list_readout_phase_calibration_kernel(
                         h_plane[r:P:32, :].rearrange("q (g m) -> q g m", g=GROUPS).bitcast(I32),
                     )
 
-        def response(u, b):
-            j0, width = UNITS[u][1:]
+        def row_blocks(span, b):
+            per = BANK // SPANS[span][1]
+            return range(b * per, (b + 1) * per)
+
+        def result_banks(span):
+            return range(N // P * SPANS[span][1] // BANK)
+
+        results = [(span, b) for span in range(len(SPANS)) for b in result_banks(span)]
+
+        def response(span, b):
+            j0, width = SPANS[span]
             rhs, rhs_scale = shots(j0, width)
-            resp = psum.tile([P, BANK // width, width], F32, name="resp", tag=resp_tag(u, b))
-            lin = psum.tile([P, BANK // width, width], F32, name="lin", tag=lin_tag(u, b))
+            bank = results.index((span, b)) % 4
+            resp = psum.tile([P, BANK // width, width], F32, name="resp", tag="bank%d" % PHASE_BANKS[bank])
+            lin = psum.tile([P, BANK // width, width], F32, name="lin", tag="bank%d" % AMPL_BANKS[bank])
             for g in range(GROUPS):
-                for s, i in enumerate(blocks(u, b)):
+                for s, i in enumerate(row_blocks(span, b)):
                     lhsT, lhsT_scale = stationary("w3", g, i)
                     nc.tensor.matmul_mx(
                         out=resp[:, s, :], lhsT=lhsT, lhsT_scale=lhsT_scale,
                         rhs=h_codes[g][:, j0:j0 + width].bitcast(FP8X4),
                         rhs_scale=h_plane[:, g * S + j0:g * S + j0 + width],
-                        start=(g == 0 and s == 0), stop=(g == GROUPS - 1 and i == blocks(u, b)[-1]),
+                        start=(g == 0 and s == 0), stop=(g == GROUPS - 1 and i == row_blocks(span, b)[-1]),
                     )
-            for s, i in enumerate(blocks(u, b)):
+            for s, i in enumerate(row_blocks(span, b)):
                 nc.tensor.matmul_mx(
                     out=lin[:, s, :],
                     lhsT=w4_codes[:, i * P:(i + 1) * P].bitcast(FP8X4), lhsT_scale=w4_plane[:, i * P:(i + 1) * P],
                     rhs=rhs, rhs_scale=rhs_scale, start=True, stop=True,
                 )
             sine = ring.tile([P, BANK // width, width], F32, name="sine", bufs=8)
-            size = BANK
+            size = width if (span, b) == results[-1] else BANK
             for c0 in range(0, BANK, size):
                 nc.scalar.activation(
                     sine[:].rearrange("p s j -> p (s j)")[:, c0:c0 + size],
                     resp[:].rearrange("p s j -> p (s j)")[:, c0:c0 + size], ACT.Sin,
                 )
-            pending[u, b] = sine, lin
+            pending[span, b] = sine, lin
 
-        def result(u, b):
-            j0, width = UNITS[u][1:]
-            sine, lin = pending[u, b]
-            y = sb("y%d_%d" % (u, b), [P, BANK // width, width], F32)
-            for s, i in enumerate(blocks(u, b)):
+        def result(span, b):
+            j0, width = SPANS[span]
+            sine, lin = pending[span, b]
+            y = sb("y%d_%d" % (span, b), [P, BANK // width, width], F32)
+            per = 1 if (span, b) == results[-1] else BANK // width
+            for s, i in enumerate(row_blocks(span, b)):
                 nc.vector.scalar_tensor_tensor(y[:, s, :], sine[:, s, :], amp_sb[:, i, :], lin[:, s, :], ALU.mult, ALU.add)
-                per = 1 if (u, b) == steps[-1] else len(blocks(u, b))
                 if (s + 1) % per == 0:
                     rows = out_0[(i + 1 - per) * P:(i + 1) * P, j0:j0 + width]
                     nc.sync.dma_start(rows.rearrange("(s p) j -> p s j", p=P), y[:, s + 1 - per:s + 1, :])
@@ -313,7 +317,7 @@ def tile_list_readout_phase_calibration_kernel(
             n = steps.index((u, b))
             if n + 1 < len(steps):
                 phase_bank(*steps[n + 1])
-            if u == 0 or n >= len(steps) - 2:
+            if u == 0 or (u % 2 == 1 and b >= 2):
                 cosine(u, b, b + 1)
             elif b % 2 == 0:
                 cosine(u, b, b + 2)
@@ -321,13 +325,14 @@ def tile_list_readout_phase_calibration_kernel(
 
         round_wa(0)
         round_wa(1)
-        quantise_weight("wa", 0, 0, 256)
-        quantise_weight("wa", 0, 256, 512)
         round_wa(2)
+        quantise_weight("wa", 0, 0, 128)
+        quantise_weight("wa", 0, 128, 512)
+        round_wa(3)
         phase_bank(*steps[0])
         step(0, 0)
         step(0, 1)
-        round_wa(3)
+        round_wa(4)
         step(0, 2)
         quantise_weight("wa", 1)
         step(0, 3)
@@ -338,35 +343,39 @@ def tile_list_readout_phase_calibration_kernel(
         round_h(0, on_gpsimd, 256, 512, (256, 256), "w3_bf0_0")
         for b in banks(1):
             step(1, b)
-        round_w3(1, on_vector, 0, 128, (0, 128))
-        round_h(1, on_vector)
-        quantise_weight("w3", 1, 0, 128)
         quantise_h(0, 256, 512)
         store_codes(0)
-        quantise_h(1)
+        round_w3(1, on_vector, 0, 128, (0, 128))
+        round_h(1, on_vector, 128, 512, (128, 384))
+        quantise_weight("w3", 1, 0, 128)
+        round_h(1, on_vector, 0, 128, (0, 128))
+        quantise_h(1, 128, 512)
+        quantise_h(1, 0, 128)
         store_codes(1)
-        round_w3(1, on_gpsimd, 128, 512, (128, 384), "w3_bf0_0")
+        round_w3(1, on_gpsimd, 128, 512, (128, 384), "h_bf1_128")
         for b in banks(2):
             step(2, b)
         quantise_weight("w3", 1, 128, 512, 128)
-        round_h(2, on_gpsimd, 128, 512, tag="w3_bf0_0")
+        round_h(2, on_gpsimd, 128, 512, tag="h_bf1_128")
         for b in banks(3):
             step(3, b)
-        response(1, 0)
+        response(0, 0)
         round_h(2, on_scalar, 0, 128)
-        result(1, 0)
-        round_h(3, on_vector, 0, 320)
-        round_h(3, on_scalar, 320, 512)
-        response(1, 1)
         quantise_h(2)
         store_codes(2)
-        quantise_h(3)
+        round_h(3, on_vector, 0, 256, (0, 256))
+        round_h(3, on_scalar, 256, 512, (256, 256))
+        result(0, 0)
+        response(0, 1)
+        quantise_h(3, 0, 256)
+        response(0, 2)
+        response(0, 3)
+        result(0, 1)
+        quantise_h(3, 256, 512)
         store_codes(3)
-        result(1, 1)
-        response(1, 2)
-        response(1, 3)
-        result(1, 2)
-        result(1, 3)
+        result(0, 2)
+        result(0, 3)
         for job in (response, result):
-            for b in banks(LAST):
-                job(LAST, b)
+            for span in (1, 2):
+                for b in result_banks(span):
+                    job(span, b)

@@ -27,7 +27,7 @@ TAB_FIRST = 800
 UNITS = [(0, 0, 512), (1, 0, 512), (0, 512, 512), (1, 512, 512)]
 LAST = len(UNITS) - 1
 PHASE_BANKS, AMPL_BANKS = (0, 1, 4, 5), (2, 3, 6, 7)
-SPANS = [(0, 512), (512, 256), (768, 256)]
+SPANS = [(0, 512), (512, 512)]
 
 
 def tile_list_readout_phase_calibration_kernel(
@@ -176,7 +176,11 @@ def tile_list_readout_phase_calibration_kernel(
             cols = slice(block * P, (block + 1) * P)
             return weight_codes[name, g][:, cols].bitcast(FP8X4), weight_planes[name, g][:, cols]
 
-        h_plane = sb("h_plane", [P, GROUPS * S], U8)
+        h_planes = [sb("h_plane%d" % part, [P, GROUPS, LOOKUP], U8) for part in range(S // LOOKUP)]
+
+        def h_scales(g, j0, width):
+            return h_planes[j0 // LOOKUP][:, g, j0 % LOOKUP:j0 % LOOKUP + width]
+
         h_codes = [sb("h_codes%d" % g, [P, S], U32) for g in range(GROUPS)]
         h_tiles, folded, cosines, pending = {}, {}, {}, {}
 
@@ -237,8 +241,9 @@ def tile_list_readout_phase_calibration_kernel(
                 h[:].rearrange("p t j -> p (t j)")[:, cols], cosines[u][:, cols],
                 bank[:].rearrange("p s j -> p (s j)"), ALU.mult,
             )
-            if b % 2 == 1 or b == banks(u)[-1]:
-                t0, t1 = blocks(u, b - b % 2).start, blocks(u, b).stop
+            per = 1 if u == LAST else 2
+            if (b + 1) % per == 0:
+                t0, t1 = blocks(u, b + 1 - per).start, blocks(u, b).stop
                 rows = out_1[g * PASS:(g + 1) * PASS, j0:j0 + width].rearrange("(p t) j -> p t j", t=PACK)
                 nc.sync.dma_start(rows[:, t0:t1, :], h[:, t0:t1, :])
 
@@ -249,18 +254,18 @@ def tile_list_readout_phase_calibration_kernel(
             g, j0, width = UNITS[u]
             nc.vector.quantize_mx(
                 out=h_codes[g][:, j0 + c0:j0 + c1].bitcast(FP8X4),
-                scales=h_plane[:, g * S + j0 + c0:g * S + j0 + c1], in_=staged["h", u, c0][:],
+                scales=h_scales(g, j0 + c0, c1 - c0), in_=staged["h", u, c0][:],
             )
 
         def store_codes(u):
             g, j0, width = UNITS[u]
             words = out_2[g].rearrange("p m t -> p (m t)").bitcast(I32)
             nc.sync.dma_start(words[:, j0:j0 + width], h_codes[g][:, j0:j0 + width].bitcast(I32))
-            if u == LAST:
+            if g == GROUPS - 1:
                 for r in range(4):
                     nc.sync.dma_start(
-                        out_3[:, r:16:4, :].rearrange("g q m -> q g m").bitcast(I32),
-                        h_plane[r:P:32, :].rearrange("q (g m) -> q g m", g=GROUPS).bitcast(I32),
+                        out_3[:, r:16:4, j0:j0 + width].rearrange("g q m -> q g m").bitcast(I32),
+                        h_planes[j0 // LOOKUP][r:P:32].bitcast(I32),
                     )
 
         def row_blocks(span, b):
@@ -284,7 +289,7 @@ def tile_list_readout_phase_calibration_kernel(
                     nc.tensor.matmul_mx(
                         out=resp[:, s, :], lhsT=lhsT, lhsT_scale=lhsT_scale,
                         rhs=h_codes[g][:, j0:j0 + width].bitcast(FP8X4),
-                        rhs_scale=h_plane[:, g * S + j0:g * S + j0 + width],
+                        rhs_scale=h_scales(g, j0, width),
                         start=(g == 0 and s == 0), stop=(g == GROUPS - 1 and i == row_blocks(span, b)[-1]),
                     )
             for s, i in enumerate(row_blocks(span, b)):
@@ -361,21 +366,19 @@ def tile_list_readout_phase_calibration_kernel(
             step(3, b)
         response(0, 0)
         round_h(2, on_scalar, 0, 128)
+        result(0, 0)
+        round_h(3, on_vector, 0, 288)
+        round_h(3, on_scalar, 288, 512)
+        response(0, 1)
         quantise_h(2)
         store_codes(2)
-        round_h(3, on_vector, 0, 256, (0, 256))
-        round_h(3, on_scalar, 256, 512, (256, 256))
-        result(0, 0)
-        response(0, 1)
-        quantise_h(3, 0, 256)
+        quantise_h(3)
+        store_codes(3)
+        result(0, 1)
         response(0, 2)
         response(0, 3)
-        result(0, 1)
-        quantise_h(3, 256, 512)
-        store_codes(3)
         result(0, 2)
         result(0, 3)
         for job in (response, result):
-            for span in (1, 2):
-                for b in result_banks(span):
-                    job(span, b)
+            for b in result_banks(1):
+                job(1, b)

@@ -70,12 +70,12 @@ def tile_list_readout_phase_calibration_kernel(
         load_scale_rows(nc.sync, tab_rows[:], tab_scales)
         nc.sync.dma_start(tab[:, TAB_FIRST:].bitcast(I32), tab_src[:, TAB_FIRST:])
 
-        phi_sb = sb("phi_sb", [P, GROUPS, 2 * PACK], F32)
-        nc.scalar.dma_start(phi_sb[:, :, :PACK], phi.rearrange("(g p t) -> p g t", g=GROUPS, t=PACK))
         zero = sb("zero", [P, 1], F32)
         nc.vector.memset(zero[:], 0.0)
         warm = sb("warm", [P, 1], F32)
         nc.scalar.activation(warm[:], zero[:], ACT.Sin)
+        phi_sb = sb("phi_sb", [P, GROUPS, 2 * PACK], F32, tag="warm")
+        nc.scalar.dma_start(phi_sb[:, :, :PACK], phi.rearrange("(g p t) -> p g t", g=GROUPS, t=PACK))
 
         def list_part(part):
             return offsets[:, part * LOOKUP // 16:(part + 1) * LOOKUP // 16]
@@ -139,8 +139,8 @@ def tile_list_readout_phase_calibration_kernel(
 
         def interleave(copy, rounded, rows, c0, c1):
             copy(
-                rounded[:, PACK * c0:PACK * c1].rearrange("p (c i t) -> p c t i", i=4, t=PACK),
-                rows[:, :, c0:c1].rearrange("p t (c i) -> p c t i", i=4),
+                rounded[:, PACK * c0:PACK * c1].rearrange("p (c i u w) -> p c u i w", i=2, u=2, w=2),
+                rows[:, :, c0:c1].rearrange("p (u w) (c i) -> p c u i w", i=2, w=2),
             )
 
         def on_vector(rounded, rows, c0, c1):
@@ -342,18 +342,19 @@ def tile_list_readout_phase_calibration_kernel(
         quantise_weight("wa", 1)
         step(0, 3)
         round_w3(0, on_vector)
-        round_h(0, on_vector, 0, 256, (0, 256))
+        round_h(0, on_vector, 0, 128, (0, 256))
         quantise_weight("w3", 0)
-        quantise_h(0, 0, 256)
+        round_h(0, on_scalar, 128, 256, (0, 256))
         round_h(0, on_gpsimd, 256, 512, (256, 256), "w3_bf0_0")
         for b in banks(1):
             step(1, b)
+        quantise_h(0, 0, 256)
         quantise_h(0, 256, 512)
         store_codes(0)
-        round_w3(1, on_vector, 0, 128, (0, 128))
         round_h(1, on_vector, 128, 512, (128, 384))
-        quantise_weight("w3", 1, 0, 128)
+        round_w3(1, on_vector, 0, 128, (0, 128))
         round_h(1, on_vector, 0, 128, (0, 128))
+        quantise_weight("w3", 1, 0, 128)
         quantise_h(1, 128, 512)
         quantise_h(1, 0, 128)
         store_codes(1)
@@ -367,8 +368,8 @@ def tile_list_readout_phase_calibration_kernel(
         response(0, 0)
         round_h(2, on_scalar, 0, 128)
         result(0, 0)
-        round_h(3, on_vector, 0, 288)
-        round_h(3, on_scalar, 288, 512)
+        round_h(3, on_vector, 0, 256)
+        round_h(3, on_scalar, 256, 512)
         response(0, 1)
         quantise_h(2)
         store_codes(2)

@@ -130,11 +130,11 @@ def tile_list_readout_phase_calibration_kernel(
             g, c0, width = wa_parts[part]
             if c0 == 0:
                 staged["wa", g, 0] = sb("wa_bf%d" % g, [P, PASS * PACK], BF16)
-            dealt = staged["wa", g, 0][:].rearrange("p (t m j) -> p m t j", t=PACK, j=PACK)
+            dealt = staged["wa", g, 0][:].rearrange("p (t m u w) -> p m u t w", t=PACK, u=2, w=2)
             copy = nc.scalar.copy if part == 0 else nc.vector.tensor_copy
             copy(
                 dealt[:, c0 // PACK:(c0 + width) // PACK],
-                wa_raw[part][:].rearrange("p j (m t) -> p m t j", t=PACK),
+                wa_raw[part][:].rearrange("p (u w) (m t) -> p m u t w", w=2, t=PACK),
             )
 
         def interleave(copy, rounded, rows, c0, c1):
@@ -342,9 +342,9 @@ def tile_list_readout_phase_calibration_kernel(
         quantise_weight("wa", 1)
         step(0, 3)
         round_w3(0, on_vector)
-        round_h(0, on_vector, 0, 128, (0, 256))
+        round_h(0, on_vector, 0, 192, (0, 256))
         quantise_weight("w3", 0)
-        round_h(0, on_scalar, 128, 256, (0, 256))
+        round_h(0, on_scalar, 192, 256, (0, 256))
         round_h(0, on_gpsimd, 256, 512, (256, 256), "w3_bf0_0")
         for b in banks(1):
             step(1, b)
@@ -367,10 +367,10 @@ def tile_list_readout_phase_calibration_kernel(
             step(3, b)
         response(0, 0)
         round_h(2, on_scalar, 0, 128)
-        result(0, 0)
-        round_h(3, on_vector, 0, 256)
-        round_h(3, on_scalar, 256, 512)
         response(0, 1)
+        result(0, 0)
+        round_h(3, on_vector, 0, 320)
+        round_h(3, on_scalar, 320, 512)
         quantise_h(2)
         store_codes(2)
         quantise_h(3)

@@ -349,20 +349,18 @@ def tile_list_readout_phase_calibration_kernel(
         for b in banks(1):
             step(1, b)
         quantise_h(0, 0, 256)
+        round_h(1, on_vector)
+        round_w3(1, on_vector, 0, 256, (0, 256))
         quantise_h(0, 256, 512)
         store_codes(0)
-        round_h(1, on_vector, 128, 512, (128, 384))
-        round_w3(1, on_vector, 0, 128, (0, 128))
-        round_h(1, on_vector, 0, 128, (0, 128))
-        quantise_weight("w3", 1, 0, 128)
-        quantise_h(1, 128, 512)
-        quantise_h(1, 0, 128)
+        quantise_weight("w3", 1, 0, 256)
+        quantise_h(1)
         store_codes(1)
-        round_w3(1, on_gpsimd, 128, 512, (128, 384), "h_bf1_128")
+        round_w3(1, on_gpsimd, 256, 512, (256, 256), "h_bf1_0")
         for b in banks(2):
             step(2, b)
-        quantise_weight("w3", 1, 128, 512, 128)
-        round_h(2, on_gpsimd, 128, 512, tag="h_bf1_128")
+        quantise_weight("w3", 1, 256, 512, 256)
+        round_h(2, on_gpsimd, 128, 512, tag="h_bf1_0")
         for b in banks(3):
             step(3, b)
         response(0, 0)

@@ -21,13 +21,14 @@ P = 128
 PACK = 4
 PASS = P * PACK
 GROUPS = H // PASS
-BANK = 512
-LOOKUP = 512
+SHOTS = 512
+HALVES = S // SHOTS
+UNITS = GROUPS * HALVES
+MID = SHOTS // 2
 TAB_FIRST = 800
-UNITS = [(0, 0, 512), (1, 0, 512), (0, 512, 512), (1, 512, 512)]
-LAST = len(UNITS) - 1
+WA_PARTS = [(0, 0, 128), (0, 128, 192), (0, 320, 192), (1, 0, 256), (1, 256, 256)]
+SCALAR_SHOTS = {0: 64, 2: 128, 3: 192}
 PHASE_BANKS, AMPL_BANKS = (0, 1, 4, 5), (2, 3, 6, 7)
-SPANS = [(0, 512), (512, 512)]
 
 
 def tile_list_readout_phase_calibration_kernel(
@@ -38,10 +39,13 @@ def tile_list_readout_phase_calibration_kernel(
     with ExitStack() as ctx:
         keep = ctx.enter_context(tc.tile_pool(name="keep", bufs=1))
         psum = ctx.enter_context(tc.psum_pool(name="psum", bufs=1))
-        ring = ctx.enter_context(tc.tile_pool(name="ring", bufs=4))
+        ring = ctx.enter_context(tc.tile_pool(name="ring", bufs=1))
 
         def sb(name, shape, dtype, tag=None):
             return keep.tile(shape, dtype, name=name, tag=tag or name, align_bytes=64)
+
+        def bank(name, number):
+            return psum.tile([P, SHOTS], F32, name=name, tag="bank%d" % number)
 
         offsets = keep.tile([P, S // 16], U16, name="offsets")
         nc.sync.dma_start(offsets[:], offs)
@@ -54,10 +58,10 @@ def tile_list_readout_phase_calibration_kernel(
             for r in range(1, 4):
                 nc.sync.dma_start(plane[r:P:32, :].bitcast(I32), plane[8 * r:P:32, :].bitcast(I32))
 
-        first_planes = sb("first_planes", [P, LOOKUP + H], U8)
-        later_planes = sb("later_planes", [P, LOOKUP + N], U8)
-        wp_plane, w4_plane = first_planes[:, LOOKUP:], later_planes[:, LOOKUP:]
-        v_planes = [first_planes[:, :LOOKUP], later_planes[:, :LOOKUP]]
+        first_planes = sb("first_planes", [P, SHOTS + H], U8)
+        later_planes = sb("later_planes", [P, SHOTS + N], U8)
+        wp_plane, w4_plane = first_planes[:, SHOTS:], later_planes[:, SHOTS:]
+        v_planes = [first_planes[:, :SHOTS], later_planes[:, :SHOTS]]
         load_scale_rows(nc.scalar, w4_plane, w4_scales)
         wp_raw = sb("wp_raw", [P, 2 * H], U8)
         nc.sync.dma_start(wp_raw[:].bitcast(I32), wp_words[0].bitcast(I32))
@@ -74,16 +78,14 @@ def tile_list_readout_phase_calibration_kernel(
         nc.vector.memset(zero[:], 0.0)
         warm = sb("warm", [P, 1], F32)
         nc.scalar.activation(warm[:], zero[:], ACT.Sin)
-        phi_sb = sb("phi_sb", [P, GROUPS, 2 * PACK], F32, tag="warm")
-        nc.scalar.dma_start(phi_sb[:, :, :PACK], phi.rearrange("(g p t) -> p g t", g=GROUPS, t=PACK))
 
-        def list_part(part):
-            return offsets[:, part * LOOKUP // 16:(part + 1) * LOOKUP // 16]
+        def list_half(half):
+            return offsets[:, half * SHOTS // 16:(half + 1) * SHOTS // 16]
 
-        def look_up_scales(part):
-            picked = sb("v_rows%d" % part, [P, LOOKUP], U8, tag="v_rows")
-            nc.vector.tensor_copy(picked[:], tab_rows[:].indirect(list_part(part)))
-            nc.vector.tensor_copy(v_planes[part].bitcast(I32), picked[:].bitcast(I32))
+        def look_up_scales(half):
+            picked = sb("v_rows%d" % half, [P, SHOTS], U8, tag="v_rows")
+            nc.vector.tensor_copy(picked[:], tab_rows[:].indirect(list_half(half)))
+            nc.vector.tensor_copy(v_planes[half].bitcast(I32), picked[:].bitcast(I32))
 
         look_up_scales(0)
         nc.vector.tensor_copy(
@@ -96,9 +98,10 @@ def tile_list_readout_phase_calibration_kernel(
             wp_codes[:].bitcast(U16).rearrange("p (g t m) -> p g t m", g=GROUPS, t=PACK),
             wp_raw[:].bitcast(U16).rearrange("p (g m t) -> p g t m", g=GROUPS, t=PACK),
         )
+        phi_sb = sb("phi_sb", [P, GROUPS, 2 * PACK], F32, tag="wp_raw")
+        nc.scalar.dma_start(phi_sb[:, :, :PACK], phi.rearrange("(g p t) -> p g t", g=GROUPS, t=PACK))
         wa_raw, w3_raw, v_codes = [], [], []
-        wa_parts = [(0, 0, 128), (0, 128, 192), (0, 320, 192), (1, 0, 256), (1, 256, 256)]
-        for part, (g, c0, width) in enumerate(wa_parts):
+        for part, (g, c0, width) in enumerate(WA_PARTS):
             raw = sb("wa_raw%d" % part, [P, PACK, width], F32, tag="wp_rows" if part == 0 else None)
             src = wa[:, g * PASS + c0:g * PASS + c0 + width].rearrange("(p j) c -> p j c", j=PACK)
             (nc.scalar if part == 0 else nc.sync).dma_start(raw[:], src)
@@ -115,21 +118,28 @@ def tile_list_readout_phase_calibration_kernel(
         amp_sb = sb("amp_sb", [P, N // P, 1], F32)
         with nc.allow_non_contiguous_dma(reason="one value for each partition and row block"):
             nc.sync.dma_start(amp_sb[:, :, 0], amp.rearrange("(i p) -> p i", p=P))
-        for part in range(S // LOOKUP):
-            picked = sb("v_codes%d" % part, [P, LOOKUP], U32)
-            nc.vector.tensor_copy(picked[:], tab[:].indirect(list_part(part)))
+        for half in range(HALVES):
+            picked = sb("v_codes%d" % half, [P, SHOTS], U32)
+            nc.vector.tensor_copy(picked[:], tab[:].indirect(list_half(half)))
             v_codes.append(picked)
 
-        def shots(j0, width):
-            part, c0 = divmod(j0, LOOKUP)
-            return v_codes[part][:, c0:c0 + width].bitcast(FP8X4), v_planes[part][:, c0:c0 + width]
+        def product(out, lhsT, rhs, start=True, stop=True):
+            nc.tensor.matmul_mx(
+                out=out[:], lhsT=lhsT[0], lhsT_scale=lhsT[1], rhs=rhs[0], rhs_scale=rhs[1], start=start, stop=stop
+            )
+
+        def picked_shots(half):
+            return v_codes[half][:].bitcast(FP8X4), v_planes[half]
 
         weight_codes, weight_planes, staged = {}, {}, {}
 
+        def stage(name, index, first=0, width=SHOTS, tag=None):
+            staged[name, index, first] = sb("%s_bf%d_%d" % (name, index, first), [P, PACK * width], BF16, tag=tag)
+
         def round_wa(part):
-            g, c0, width = wa_parts[part]
+            g, c0, width = WA_PARTS[part]
             if c0 == 0:
-                staged["wa", g, 0] = sb("wa_bf%d" % g, [P, PASS * PACK], BF16)
+                stage("wa", g)
             dealt = staged["wa", g, 0][:].rearrange("p (t m u w) -> p m u t w", t=PACK, u=2, w=2)
             copy = nc.scalar.copy if part == 0 else nc.vector.tensor_copy
             copy(
@@ -137,31 +147,27 @@ def tile_list_readout_phase_calibration_kernel(
                 wa_raw[part][:].rearrange("p (u w) (m t) -> p m u t w", w=2, t=PACK),
             )
 
-        def interleave(copy, rounded, rows, c0, c1):
+        def interleave(copy, rounded, rows):
             copy(
-                rounded[:, PACK * c0:PACK * c1].rearrange("p (c i u w) -> p c u i w", i=2, u=2, w=2),
-                rows[:, :, c0:c1].rearrange("p (u w) (c i) -> p c u i w", i=2, w=2),
+                rounded.rearrange("p (c i u w) -> p c u i w", i=2, u=2, w=2),
+                rows.rearrange("p (u w) (c i) -> p c u i w", i=2, w=2),
             )
 
-        def on_vector(rounded, rows, c0, c1):
-            interleave(nc.vector.tensor_copy, rounded, rows, c0, c1)
+        def on_vector(rounded, rows):
+            interleave(nc.vector.tensor_copy, rounded, rows)
 
-        def on_scalar(rounded, rows, c0, c1):
-            interleave(nc.scalar.copy, rounded, rows, c0, c1)
+        def on_scalar(rounded, rows):
+            interleave(nc.scalar.copy, rounded, rows)
 
-        def on_gpsimd(rounded, rows, c0, c1):
+        def on_gpsimd(rounded, rows):
             nc.gpsimd.tensor_scalar(
-                rounded[:, PACK * c0:PACK * c1].rearrange("p (c t) -> p c t", t=PACK),
-                rows[:, :, c0:c1].rearrange("p t c -> p c t"), 1.0, 1.0, ALU.mult, ALU.mult,
+                rounded.rearrange("p (c t) -> p c t", t=PACK), rows.rearrange("p t c -> p c t"),
+                1.0, 1.0, ALU.mult, ALU.mult,
             )
 
-        def round_part(key, rows, how, c0, c1, first, width, tag):
-            if key + (first,) not in staged:
-                staged[key + (first,)] = sb("%s_bf%d_%d" % (key + (first,)), [P, PACK * width], BF16, tag=tag)
-            how(staged[key + (first,)], rows[:, :, first:first + width], c0 - first, c1 - first)
-
-        def round_w3(g, how, c0=0, c1=N, tile=(0, N), tag=None):
-            round_part(("w3", g), w3_raw[g], how, c0, c1, tile[0], tile[1], tag)
+        def round_columns(name, index, how, c0=0, c1=SHOTS, first=0):
+            rows = w3_raw[index] if name == "w3" else h_tiles[index]
+            how(staged[name, index, first][:, PACK * (c0 - first):PACK * (c1 - first)], rows[:, :, c0:c1])
 
         def quantise_weight(name, g, c0=0, c1=PASS, first=0):
             if (name, g) not in weight_codes:
@@ -176,208 +182,146 @@ def tile_list_readout_phase_calibration_kernel(
             cols = slice(block * P, (block + 1) * P)
             return weight_codes[name, g][:, cols].bitcast(FP8X4), weight_planes[name, g][:, cols]
 
-        h_planes = [sb("h_plane%d" % part, [P, GROUPS, LOOKUP], U8) for part in range(S // LOOKUP)]
-
-        def h_scales(g, j0, width):
-            return h_planes[j0 // LOOKUP][:, g, j0 % LOOKUP:j0 % LOOKUP + width]
-
+        h_planes = [sb("h_plane%d" % half, [P, GROUPS, SHOTS], U8) for half in range(HALVES)]
         h_codes = [sb("h_codes%d" % g, [P, S], U32) for g in range(GROUPS)]
         h_tiles, folded, cosines, pending = {}, {}, {}, {}
 
-        def blocks(u, b):
-            per = BANK // UNITS[u][2]
-            return range(b * per, (b + 1) * per)
+        def shot_range(half):
+            return slice(half * SHOTS, (half + 1) * SHOTS)
 
-        def banks(u):
-            return range(PACK * UNITS[u][2] // BANK)
+        def phase(u, t):
+            half, g = divmod(u, GROUPS)
+            col = g * PASS + t * P
+            out = bank("phase", PHASE_BANKS[t] if u > 0 else t)
+            if t == 0:
+                folded[u] = ring.tile([P, PACK, SHOTS], F32, name="folded", bufs=2)
+            lhsT = wp_codes[:, 2 * col:2 * (col + P)].bitcast(FP4X4), wp_plane[:, col:col + P]
+            product(out, lhsT, picked_shots(half))
+            nc.scalar.activation(folded[u][:, t, :], out[:], ACT.Abs, bias=phi_sb[:, g, t:t + 1])
 
-        steps = [(u, b) for u in range(len(UNITS)) for b in banks(u)]
-
-        def phase_tag(u, b):
-            return "bank%d" % (PHASE_BANKS[b] if u > 0 else b)
-
-        def ampl_tag(u, b):
-            return "bank%d" % (AMPL_BANKS[b] if u > 0 else 4 + b)
-
-        def phase_bank(u, b):
-            g, j0, width = UNITS[u]
-            rhs, rhs_scale = shots(j0, width)
-            bank = psum.tile([P, BANK // width, width], F32, name="phase", tag=phase_tag(u, b))
-            if b == 0:
-                folded[u] = ring.tile([P, PACK * BANK], F32, name="folded", bufs=2)
-            for s, t in enumerate(blocks(u, b)):
-                col = g * PASS + t * P
-                nc.tensor.matmul_mx(
-                    out=bank[:, s, :],
-                    lhsT=wp_codes[:, 2 * col:2 * (col + P)].bitcast(FP4X4), lhsT_scale=wp_plane[:, col:col + P],
-                    rhs=rhs, rhs_scale=rhs_scale, start=True, stop=True,
-                )
-            for s, t in enumerate(blocks(u, b)):
-                nc.scalar.activation(
-                    folded[u][:, t * width:(t + 1) * width], bank[:, s, :], ACT.Abs, bias=phi_sb[:, g, t:t + 1]
-                )
-
-        def cosine(u, b0, b1):
-            if b0 == 0:
-                cosines[u] = ring.tile([P, PACK * BANK], F32, name="cos", bufs=3)
-            cols = slice(b0 * BANK, b1 * BANK)
-            nc.scalar.activation(cosines[u][:, cols], folded[u][:, cols], ACT.Sin, bias=math.pi / 2, scale=-1.0)
-
-        def feature_bank(u, b):
-            g, j0, width = UNITS[u]
-            rhs, rhs_scale = shots(j0, width)
-            if b == 0:
-                h_tiles[u] = sb("h%d" % u, [P, PACK, width], F32, tag="w3_raw0" if u == 1 else None)
-            bank = psum.tile([P, BANK // width, width], F32, name="ampl", tag=ampl_tag(u, b))
-            for s, t in enumerate(blocks(u, b)):
-                lhsT, lhsT_scale = stationary("wa", g, t)
-                nc.tensor.matmul_mx(
-                    out=bank[:, s, :], lhsT=lhsT, lhsT_scale=lhsT_scale,
-                    rhs=rhs, rhs_scale=rhs_scale, start=True, stop=True,
-                )
-            cols = slice(b * BANK, (b + 1) * BANK)
-            h = h_tiles[u]
-            nc.vector.tensor_tensor(
-                h[:].rearrange("p t j -> p (t j)")[:, cols], cosines[u][:, cols],
-                bank[:].rearrange("p s j -> p (s j)"), ALU.mult,
+        def cosine(u, t0, t1):
+            if t0 == 0:
+                cosines[u] = ring.tile([P, PACK, SHOTS], F32, name="cos", bufs=3)
+            nc.scalar.activation(
+                cosines[u][:, t0:t1, :], folded[u][:, t0:t1, :], ACT.Sin, bias=math.pi / 2, scale=-1.0
             )
-            per = 1 if u == LAST else 2
-            if (b + 1) % per == 0:
-                t0, t1 = blocks(u, b + 1 - per).start, blocks(u, b).stop
-                rows = out_1[g * PASS:(g + 1) * PASS, j0:j0 + width].rearrange("(p t) j -> p t j", t=PACK)
-                nc.sync.dma_start(rows[:, t0:t1, :], h[:, t0:t1, :])
 
-        def round_h(u, how, c0=0, c1=BANK, tile=(0, BANK), tag=None):
-            round_part(("h", u), h_tiles[u], how, c0, c1, tile[0], tile[1], tag)
+        def feature(u, t):
+            half, g = divmod(u, GROUPS)
+            if t == 0:
+                h_tiles[u] = sb("h%d" % u, [P, PACK, SHOTS], F32, tag="w3_raw0" if u == 1 else None)
+            ampl = bank("ampl", AMPL_BANKS[t] if u > 0 else PACK + t)
+            product(ampl, stationary("wa", g, t), picked_shots(half))
+            nc.vector.tensor_tensor(h_tiles[u][:, t, :], cosines[u][:, t, :], ampl[:], ALU.mult)
+            per = 1 if u == UNITS - 1 else 2
+            if (t + 1) % per == 0:
+                rows = out_1[g * PASS:(g + 1) * PASS, shot_range(half)].rearrange("(p t) j -> p t j", t=PACK)
+                nc.sync.dma_start(rows[:, t + 1 - per:t + 1, :], h_tiles[u][:, t + 1 - per:t + 1, :])
 
-        def quantise_h(u, c0=0, c1=BANK):
-            g, j0, width = UNITS[u]
+        def step(u, t):
+            n = PACK * u + t + 1
+            if n < PACK * UNITS:
+                phase(*divmod(n, PACK))
+            if u == 0 or (u % GROUPS == GROUPS - 1 and t >= 2):
+                cosine(u, t, t + 1)
+            elif t % 2 == 0:
+                cosine(u, t, t + 2)
+            feature(u, t)
+
+        def quantise_h(u, c0=0, c1=SHOTS):
+            half, g = divmod(u, GROUPS)
             nc.vector.quantize_mx(
-                out=h_codes[g][:, j0 + c0:j0 + c1].bitcast(FP8X4),
-                scales=h_scales(g, j0 + c0, c1 - c0), in_=staged["h", u, c0][:],
+                out=h_codes[g][:, half * SHOTS + c0:half * SHOTS + c1].bitcast(FP8X4),
+                scales=h_planes[half][:, g, c0:c1], in_=staged["h", u, c0][:],
             )
 
         def store_codes(u):
-            g, j0, width = UNITS[u]
+            half, g = divmod(u, GROUPS)
             words = out_2[g].rearrange("p m t -> p (m t)").bitcast(I32)
-            nc.sync.dma_start(words[:, j0:j0 + width], h_codes[g][:, j0:j0 + width].bitcast(I32))
+            nc.sync.dma_start(words[:, shot_range(half)], h_codes[g][:, shot_range(half)].bitcast(I32))
             if g == GROUPS - 1:
                 for r in range(4):
                     nc.sync.dma_start(
-                        out_3[:, r:16:4, j0:j0 + width].rearrange("g q m -> q g m").bitcast(I32),
-                        h_planes[j0 // LOOKUP][r:P:32].bitcast(I32),
+                        out_3[:, r:16:4, shot_range(half)].rearrange("g q m -> q g m").bitcast(I32),
+                        h_planes[half][r:P:32].bitcast(I32),
                     )
 
-        def row_blocks(span, b):
-            per = BANK // SPANS[span][1]
-            return range(b * per, (b + 1) * per)
-
-        def result_banks(span):
-            return range(N // P * SPANS[span][1] // BANK)
-
-        results = [(span, b) for span in range(len(SPANS)) for b in result_banks(span)]
-
-        def response(span, b):
-            j0, width = SPANS[span]
-            rhs, rhs_scale = shots(j0, width)
-            bank = results.index((span, b)) % 4
-            resp = psum.tile([P, BANK // width, width], F32, name="resp", tag="bank%d" % PHASE_BANKS[bank])
-            lin = psum.tile([P, BANK // width, width], F32, name="lin", tag="bank%d" % AMPL_BANKS[bank])
+        def response(half, i):
+            resp, lin = bank("resp", PHASE_BANKS[i]), bank("lin", AMPL_BANKS[i])
             for g in range(GROUPS):
-                for s, i in enumerate(row_blocks(span, b)):
-                    lhsT, lhsT_scale = stationary("w3", g, i)
-                    nc.tensor.matmul_mx(
-                        out=resp[:, s, :], lhsT=lhsT, lhsT_scale=lhsT_scale,
-                        rhs=h_codes[g][:, j0:j0 + width].bitcast(FP8X4),
-                        rhs_scale=h_scales(g, j0, width),
-                        start=(g == 0 and s == 0), stop=(g == GROUPS - 1 and i == row_blocks(span, b)[-1]),
-                    )
-            for s, i in enumerate(row_blocks(span, b)):
-                nc.tensor.matmul_mx(
-                    out=lin[:, s, :],
-                    lhsT=w4_codes[:, i * P:(i + 1) * P].bitcast(FP8X4), lhsT_scale=w4_plane[:, i * P:(i + 1) * P],
-                    rhs=rhs, rhs_scale=rhs_scale, start=True, stop=True,
-                )
-            sine = ring.tile([P, BANK // width, width], F32, name="sine", bufs=8)
-            size = width if (span, b) == results[-1] else BANK
-            for c0 in range(0, BANK, size):
-                nc.scalar.activation(
-                    sine[:].rearrange("p s j -> p (s j)")[:, c0:c0 + size],
-                    resp[:].rearrange("p s j -> p (s j)")[:, c0:c0 + size], ACT.Sin,
-                )
-            pending[span, b] = sine, lin
+                rhs = h_codes[g][:, shot_range(half)].bitcast(FP8X4), h_planes[half][:, g, :]
+                product(resp, stationary("w3", g, i), rhs, start=(g == 0), stop=(g == GROUPS - 1))
+            cols = slice(i * P, (i + 1) * P)
+            product(lin, (w4_codes[:, cols].bitcast(FP8X4), w4_plane[:, cols]), picked_shots(half))
+            sine = ring.tile([P, SHOTS], F32, name="sine", bufs=HALVES * N // P)
+            nc.scalar.activation(sine[:], resp[:], ACT.Sin)
+            pending[half, i] = sine, lin
 
-        def result(span, b):
-            j0, width = SPANS[span]
-            sine, lin = pending[span, b]
-            y = sb("y%d_%d" % (span, b), [P, BANK // width, width], F32)
-            per = 1 if (span, b) == results[-1] else BANK // width
-            for s, i in enumerate(row_blocks(span, b)):
-                nc.vector.scalar_tensor_tensor(y[:, s, :], sine[:, s, :], amp_sb[:, i, :], lin[:, s, :], ALU.mult, ALU.add)
-                if (s + 1) % per == 0:
-                    rows = out_0[(i + 1 - per) * P:(i + 1) * P, j0:j0 + width]
-                    nc.sync.dma_start(rows.rearrange("(s p) j -> p s j", p=P), y[:, s + 1 - per:s + 1, :])
+        def result(half, i):
+            sine, lin = pending[half, i]
+            y = sb("y%d_%d" % (half, i), [P, SHOTS], F32)
+            nc.vector.scalar_tensor_tensor(y[:], sine[:], amp_sb[:, i, :], lin[:], ALU.mult, ALU.add)
+            nc.sync.dma_start(out_0[i * P:(i + 1) * P, shot_range(half)], y[:])
 
-        def step(u, b):
-            n = steps.index((u, b))
-            if n + 1 < len(steps):
-                phase_bank(*steps[n + 1])
-            if u == 0 or (u % 2 == 1 and b >= 2):
-                cosine(u, b, b + 1)
-            elif b % 2 == 0:
-                cosine(u, b, b + 2)
-            feature_bank(u, b)
-
-        round_wa(0)
-        round_wa(1)
-        round_wa(2)
-        quantise_weight("wa", 0, 0, 128)
-        quantise_weight("wa", 0, 128, 512)
+        for part in range(3):
+            round_wa(part)
+        quantise_weight("wa", 0, 0, P)
+        quantise_weight("wa", 0, P, PASS)
         round_wa(3)
-        phase_bank(*steps[0])
+        phase(0, 0)
         step(0, 0)
         step(0, 1)
         round_wa(4)
         step(0, 2)
         quantise_weight("wa", 1)
         step(0, 3)
-        round_w3(0, on_vector)
-        round_h(0, on_vector, 0, 192, (0, 256))
+
+        stage("w3", 0)
+        round_columns("w3", 0, on_vector)
+        stage("h", 0, 0, MID)
+        round_columns("h", 0, on_vector, 0, MID - SCALAR_SHOTS[0])
         quantise_weight("w3", 0)
-        round_h(0, on_scalar, 192, 256, (0, 256))
-        round_h(0, on_gpsimd, 256, 512, (256, 256), "w3_bf0_0")
-        for b in banks(1):
-            step(1, b)
-        quantise_h(0, 0, 256)
-        round_h(1, on_vector)
-        round_w3(1, on_vector, 0, 256, (0, 256))
-        quantise_h(0, 256, 512)
+        round_columns("h", 0, on_scalar, MID - SCALAR_SHOTS[0], MID)
+        stage("h", 0, MID, MID, tag="w3_bf0_0")
+        round_columns("h", 0, on_gpsimd, MID, SHOTS, MID)
+        for t in range(PACK):
+            step(1, t)
+
+        quantise_h(0, 0, MID)
+        stage("h", 1)
+        round_columns("h", 1, on_vector)
+        stage("w3", 1, 0, MID)
+        round_columns("w3", 1, on_vector, 0, MID)
+        quantise_h(0, MID, SHOTS)
         store_codes(0)
-        quantise_weight("w3", 1, 0, 256)
+        quantise_weight("w3", 1, 0, MID)
         quantise_h(1)
         store_codes(1)
-        round_w3(1, on_gpsimd, 256, 512, (256, 256), "h_bf1_0")
-        for b in banks(2):
-            step(2, b)
-        quantise_weight("w3", 1, 256, 512, 256)
-        round_h(2, on_gpsimd, 128, 512, tag="h_bf1_0")
-        for b in banks(3):
-            step(3, b)
+        stage("w3", 1, MID, MID, tag="h_bf1_0")
+        round_columns("w3", 1, on_gpsimd, MID, N, MID)
+        for t in range(PACK):
+            step(2, t)
+
+        quantise_weight("w3", 1, MID, N, MID)
+        stage("h", 2, tag="h_bf1_0")
+        round_columns("h", 2, on_gpsimd, SCALAR_SHOTS[2], SHOTS)
+        for t in range(PACK):
+            step(3, t)
+
         response(0, 0)
-        round_h(2, on_scalar, 0, 128)
+        round_columns("h", 2, on_scalar, 0, SCALAR_SHOTS[2])
         response(0, 1)
         result(0, 0)
-        round_h(3, on_vector, 0, 320)
-        round_h(3, on_scalar, 320, 512)
-        quantise_h(2)
-        store_codes(2)
-        quantise_h(3)
-        store_codes(3)
+        stage("h", 3)
+        round_columns("h", 3, on_vector, 0, SHOTS - SCALAR_SHOTS[3])
+        round_columns("h", 3, on_scalar, SHOTS - SCALAR_SHOTS[3], SHOTS)
+        for u in (2, 3):
+            quantise_h(u)
+            store_codes(u)
         result(0, 1)
-        response(0, 2)
-        response(0, 3)
-        result(0, 2)
-        result(0, 3)
         for job in (response, result):
-            for b in result_banks(1):
-                job(1, b)
+            for i in (2, 3):
+                job(0, i)
+        for job in (response, result):
+            for i in range(N // P):
+                job(1, i)

@@ -74,6 +74,8 @@ def tile_list_readout_phase_calibration_kernel(
         load_scale_rows(nc.sync, tab_rows[:], tab_scales)
         nc.sync.dma_start(tab[:, TAB_FIRST:].bitcast(I32), tab_src[:, TAB_FIRST:])
 
+        phi_sb = sb("phi_sb", [P, GROUPS, 2 * PACK], F32)
+        nc.scalar.dma_start(phi_sb[:, :, :PACK], phi.rearrange("(g p t) -> p g t", g=GROUPS, t=PACK))
         zero = sb("zero", [P, 1], F32)
         nc.vector.memset(zero[:], 0.0)
         warm = sb("warm", [P, 1], F32)
@@ -98,8 +100,6 @@ def tile_list_readout_phase_calibration_kernel(
             wp_codes[:].bitcast(U16).rearrange("p (g t m) -> p g t m", g=GROUPS, t=PACK),
             wp_raw[:].bitcast(U16).rearrange("p (g m t) -> p g t m", g=GROUPS, t=PACK),
         )
-        phi_sb = sb("phi_sb", [P, GROUPS, 2 * PACK], F32, tag="wp_raw")
-        nc.scalar.dma_start(phi_sb[:, :, :PACK], phi.rearrange("(g p t) -> p g t", g=GROUPS, t=PACK))
         wa_raw, w3_raw, v_codes = [], [], []
         for part, (g, c0, width) in enumerate(WA_PARTS):
             raw = sb("wa_raw%d" % part, [P, PACK, width], F32, tag="wp_rows" if part == 0 else None)

@@ -24,10 +24,19 @@ GROUPS = H // PASS
 SHOTS = 512
 HALVES = S // SHOTS
 UNITS = GROUPS * HALVES
-MID = SHOTS // 2
-TAB_FIRST = 800
-WA_PARTS = [(0, 0, 128), (0, 128, 192), (0, 320, 192), (1, 0, 256), (1, 256, 256)]
-SCALAR_SHOTS = {0: 64, 2: 128, 3: 192}
+BLOCKS = N // P
+MID = 256
+CUT = 128
+UNIT_BYTES = PACK * SHOTS * 4
+WA_PARTS = [(0, 0, 256), (0, 256, 256), (1, 0, 256), (1, 256, 256)]
+TAB_FIRST = 768
+SCALAR_SHOTS = {2: 128, 3: 192}
+KB = 1024
+SECOND_JOB_AT = 32 * KB
+FIRST_JOB_AT = 35 * KB - 64
+H_AT = {2: 36 * KB, 1: 44 * KB}
+W3_FIRST_AT = 37 * KB
+COS_AT = [0, UNIT_BYTES, 2 * UNIT_BYTES, 3 * UNIT_BYTES]
 PHASE_BANKS, AMPL_BANKS = (0, 1, 4, 5), (2, 3, 6, 7)
 
 
@@ -40,6 +49,7 @@ def tile_list_readout_phase_calibration_kernel(
         keep = ctx.enter_context(tc.tile_pool(name="keep", bufs=1))
         psum = ctx.enter_context(tc.psum_pool(name="psum", bufs=1))
         ring = ctx.enter_context(tc.tile_pool(name="ring", bufs=1))
+        placed = ctx.enter_context(tc.tile_pool(name="placed", bufs=1))
 
         def sb(name, shape, dtype, tag=None):
             return keep.tile(shape, dtype, name=name, tag=tag or name, align_bytes=64)
@@ -49,10 +59,13 @@ def tile_list_readout_phase_calibration_kernel(
 
         offsets = keep.tile([P, S // 16], U16, name="offsets")
         nc.sync.dma_start(offsets[:], offs)
+        tab = sb("tab", [P, T], U32)
+        tab_src = tab_words[0].rearrange("p t i -> p (t i)").bitcast(I32)
+        nc.sync.dma_start(tab[:, :TAB_FIRST].bitcast(I32), tab_src[:, :TAB_FIRST])
 
-        def load_scale_rows(queue, rows, src):
+        def load_scale_rows(rows, src):
             nc.vector.memset(rows.bitcast(I32), 0)
-            queue.dma_start(rows[0:P:8, :].bitcast(I32), src[0].bitcast(I32))
+            nc.sync.dma_start(rows[0:P:8, :].bitcast(I32), src[0].bitcast(I32))
 
         def seat_scale_rows(plane):
             for r in range(1, 4):
@@ -62,17 +75,13 @@ def tile_list_readout_phase_calibration_kernel(
         later_planes = sb("later_planes", [P, SHOTS + N], U8)
         wp_plane, w4_plane = first_planes[:, SHOTS:], later_planes[:, SHOTS:]
         v_planes = [first_planes[:, :SHOTS], later_planes[:, :SHOTS]]
-        load_scale_rows(nc.scalar, w4_plane, w4_scales)
+        tab_rows = sb("tab_rows", [P, T], U8)
+        load_scale_rows(tab_rows[:], tab_scales)
+        wp_rows = sb("wp_rows", [P, H], U8)
+        load_scale_rows(wp_rows[:], wp_scales)
+        nc.sync.dma_start(tab[:, TAB_FIRST:].bitcast(I32), tab_src[:, TAB_FIRST:])
         wp_raw = sb("wp_raw", [P, 2 * H], U8)
         nc.sync.dma_start(wp_raw[:].bitcast(I32), wp_words[0].bitcast(I32))
-        wp_rows = sb("wp_rows", [P, H], U8)
-        load_scale_rows(nc.sync, wp_rows[:], wp_scales)
-        tab = sb("tab", [P, T], U32)
-        tab_src = tab_words[0].rearrange("p t i -> p (t i)").bitcast(I32)
-        nc.sync.dma_start(tab[:, :TAB_FIRST].bitcast(I32), tab_src[:, :TAB_FIRST])
-        tab_rows = sb("tab_rows", [P, T], U8)
-        load_scale_rows(nc.sync, tab_rows[:], tab_scales)
-        nc.sync.dma_start(tab[:, TAB_FIRST:].bitcast(I32), tab_src[:, TAB_FIRST:])
 
         phi_sb = sb("phi_sb", [P, GROUPS, 2 * PACK], F32)
         nc.scalar.dma_start(phi_sb[:, :, :PACK], phi.rearrange("(g p t) -> p g t", g=GROUPS, t=PACK))
@@ -87,41 +96,62 @@ def tile_list_readout_phase_calibration_kernel(
         def look_up_scales(half):
             picked = sb("v_rows%d" % half, [P, SHOTS], U8, tag="v_rows")
             nc.vector.tensor_copy(picked[:], tab_rows[:].indirect(list_half(half)))
+            return picked
+
+        def place_scales(half, picked):
             nc.vector.tensor_copy(v_planes[half].bitcast(I32), picked[:].bitcast(I32))
 
-        look_up_scales(0)
+        picked_rows = look_up_scales(0)
         nc.vector.tensor_copy(
             wp_plane.rearrange("p (g t m) -> p g t m", g=GROUPS, t=PACK),
             wp_rows[:].rearrange("p (g m t) -> p g t m", g=GROUPS, t=PACK),
         )
+        place_scales(0, picked_rows)
         seat_scale_rows(first_planes)
-        wp_codes = sb("wp_codes", [P, 2 * H], U8)
-        nc.vector.tensor_copy(
-            wp_codes[:].bitcast(U16).rearrange("p (g t m) -> p g t m", g=GROUPS, t=PACK),
-            wp_raw[:].bitcast(U16).rearrange("p (g m t) -> p g t m", g=GROUPS, t=PACK),
-        )
-        wa_raw, w3_raw, v_codes = [], [], []
-        for part, (g, c0, width) in enumerate(WA_PARTS):
-            raw = sb("wa_raw%d" % part, [P, PACK, width], F32, tag="wp_rows" if part == 0 else None)
-            src = wa[:, g * PASS + c0:g * PASS + c0 + width].rearrange("(p j) c -> p j c", j=PACK)
-            (nc.scalar if part == 0 else nc.sync).dma_start(raw[:], src)
-            wa_raw.append(raw)
-        look_up_scales(1)
+        load_scale_rows(w4_plane, w4_scales)
+        place_scales(1, look_up_scales(1))
+        wp_codes = [sb("wp_codes%d" % g, [P, 2 * PASS], U8) for g in range(GROUPS)]
         for g in range(GROUPS):
-            raw = sb("w3_raw%d" % g, [P, PACK, N], F32)
-            nc.sync.dma_start(raw[:], w3[g * PASS:(g + 1) * PASS, :].rearrange("(p j) n -> p j n", j=PACK))
-            w3_raw.append(raw)
+            cols = slice(2 * g * PASS, 2 * (g + 1) * PASS)
+            nc.scalar.copy(
+                wp_codes[g][:].bitcast(U16).rearrange("p (t m) -> p t m", t=PACK),
+                wp_raw[:, cols].bitcast(U16).rearrange("p (m t) -> p t m", t=PACK),
+            )
+
+        wa_raw, w3_raw, v_codes = {}, {}, []
+
+        def load_wa(part):
+            g, c0, width = WA_PARTS[part]
+            wa_raw[part] = sb("wa_raw%d" % part, [P, PACK, width], F32)[:]
+            src = wa[:, g * PASS + c0:g * PASS + c0 + width].rearrange("(p j) c -> p j c", j=PACK)
+            nc.sync.dma_start(wa_raw[part], src)
+
+        def load_w3(g):
             if g == 0:
-                seat_scale_rows(later_planes)
+                w3_raw[g] = placed.tile([P, PACK, N], F32, name="w3_raw0", align_bytes=64, offset=W3_FIRST_AT)
+            else:
+                w3_raw[g] = sb("w3_raw%d" % g, [P, PACK, N], F32)
+            nc.sync.dma_start(w3_raw[g][:], w3[g * PASS:(g + 1) * PASS, :].rearrange("(p j) n -> p j n", j=PACK))
+
+        load_wa(0)
+        load_wa(1)
+        load_wa(2)
+        load_wa(3)
+        load_w3(0)
+        seat_scale_rows(later_planes)
+        load_w3(1)
         w4_codes = sb("w4_codes", [P, N], U32)
         nc.sync.dma_start(w4_codes[:].bitcast(I32), w4_words[0].rearrange("p c i -> p (c i)").bitcast(I32))
-        amp_sb = sb("amp_sb", [P, N // P, 1], F32)
+        amp_sb = sb("amp_sb", [P, BLOCKS, 1], F32)
         with nc.allow_non_contiguous_dma(reason="one value for each partition and row block"):
             nc.sync.dma_start(amp_sb[:, :, 0], amp.rearrange("(i p) -> p i", p=P))
         for half in range(HALVES):
             picked = sb("v_codes%d" % half, [P, SHOTS], U32)
             nc.vector.tensor_copy(picked[:], tab[:].indirect(list_half(half)))
             v_codes.append(picked)
+
+        def shot_range(half):
+            return slice(half * SHOTS, (half + 1) * SHOTS)
 
         def product(out, lhsT, rhs, start=True, stop=True):
             nc.tensor.matmul_mx(
@@ -133,18 +163,21 @@ def tile_list_readout_phase_calibration_kernel(
 
         weight_codes, weight_planes, staged = {}, {}, {}
 
-        def stage(name, index, first=0, width=SHOTS, tag=None):
-            staged[name, index, first] = sb("%s_bf%d_%d" % (name, index, first), [P, PACK * width], BF16, tag=tag)
+        def stage(name, index, first=0, width=SHOTS, tag=None, at=None):
+            label = "%s_bf%d_%d" % (name, index, first)
+            if at is None:
+                staged[name, index, first] = sb(label, [P, PACK * width], BF16, tag=tag)
+            else:
+                staged[name, index, first] = placed.tile(
+                    [P, PACK * width], BF16, name=label, align_bytes=64, offset=at
+                )
 
         def round_wa(part):
             g, c0, width = WA_PARTS[part]
-            if c0 == 0:
-                stage("wa", g)
             dealt = staged["wa", g, 0][:].rearrange("p (t m u w) -> p m u t w", t=PACK, u=2, w=2)
-            copy = nc.scalar.copy if part == 0 else nc.vector.tensor_copy
-            copy(
+            nc.vector.tensor_copy(
                 dealt[:, c0 // PACK:(c0 + width) // PACK],
-                wa_raw[part][:].rearrange("p (u w) (m t) -> p m u t w", w=2, t=PACK),
+                wa_raw[part].rearrange("p (u w) (m t) -> p m u t w", w=2, t=PACK),
             )
 
         def interleave(copy, rounded, rows):
@@ -165,8 +198,10 @@ def tile_list_readout_phase_calibration_kernel(
                 1.0, 1.0, ALU.mult, ALU.mult,
             )
 
+        h_rows = {}
+
         def round_columns(name, index, how, c0=0, c1=SHOTS, first=0):
-            rows = w3_raw[index] if name == "w3" else h_tiles[index]
+            rows = w3_raw[index][:] if name == "w3" else h_rows[index]
             how(staged[name, index, first][:, PACK * (c0 - first):PACK * (c1 - first)], rows[:, :, c0:c1])
 
         def quantise_weight(name, g, c0=0, c1=PASS, first=0):
@@ -184,10 +219,7 @@ def tile_list_readout_phase_calibration_kernel(
 
         h_planes = [sb("h_plane%d" % half, [P, GROUPS, SHOTS], U8) for half in range(HALVES)]
         h_codes = [sb("h_codes%d" % g, [P, S], U32) for g in range(GROUPS)]
-        h_tiles, folded, cosines, pending = {}, {}, {}, {}
-
-        def shot_range(half):
-            return slice(half * SHOTS, (half + 1) * SHOTS)
+        folded, cosines, pending = {}, {}, {}
 
         def phase(u, t):
             half, g = divmod(u, GROUPS)
@@ -195,133 +227,154 @@ def tile_list_readout_phase_calibration_kernel(
             out = bank("phase", PHASE_BANKS[t] if u > 0 else t)
             if t == 0:
                 folded[u] = ring.tile([P, PACK, SHOTS], F32, name="folded", bufs=2)
-            lhsT = wp_codes[:, 2 * col:2 * (col + P)].bitcast(FP4X4), wp_plane[:, col:col + P]
+            lhsT = wp_codes[g][:, 2 * t * P:2 * (t + 1) * P].bitcast(FP4X4), wp_plane[:, col:col + P]
             product(out, lhsT, picked_shots(half))
             nc.scalar.activation(folded[u][:, t, :], out[:], ACT.Abs, bias=phi_sb[:, g, t:t + 1])
 
         def cosine(u, t0, t1):
             if t0 == 0:
-                cosines[u] = ring.tile([P, PACK, SHOTS], F32, name="cos", bufs=3)
+                cosines[u] = placed.tile(
+                    [P, PACK, SHOTS], F32, name="cos%d" % u, align_bytes=64, offset=COS_AT[u]
+                )
             nc.scalar.activation(
                 cosines[u][:, t0:t1, :], folded[u][:, t0:t1, :], ACT.Sin, bias=math.pi / 2, scale=-1.0
             )
 
         def feature(u, t):
             half, g = divmod(u, GROUPS)
-            if t == 0:
-                h_tiles[u] = sb("h%d" % u, [P, PACK, SHOTS], F32, tag="w3_raw0" if u == 1 else None)
+            if t == 0 and u in H_AT:
+                h_rows[u] = placed.tile([P, PACK, SHOTS], F32, name="h%d" % u, align_bytes=64, offset=H_AT[u])[:]
+            elif t == 0:
+                h_rows[u] = sb("h%d" % u, [P, PACK, SHOTS], F32)[:]
             ampl = bank("ampl", AMPL_BANKS[t] if u > 0 else PACK + t)
             product(ampl, stationary("wa", g, t), picked_shots(half))
-            nc.vector.tensor_tensor(h_tiles[u][:, t, :], cosines[u][:, t, :], ampl[:], ALU.mult)
+            nc.vector.tensor_tensor(h_rows[u][:, t, :], cosines[u][:, t, :], ampl[:], ALU.mult)
+            rows = out_1[g * PASS:(g + 1) * PASS, :].rearrange("(p t) j -> p t j", t=PACK)
             per = 1 if u == UNITS - 1 else 2
             if (t + 1) % per == 0:
-                rows = out_1[g * PASS:(g + 1) * PASS, shot_range(half)].rearrange("(p t) j -> p t j", t=PACK)
-                nc.sync.dma_start(rows[:, t + 1 - per:t + 1, :], h_tiles[u][:, t + 1 - per:t + 1, :])
+                nc.sync.dma_start(rows[:, t + 1 - per:t + 1, shot_range(half)], h_rows[u][:, t + 1 - per:t + 1, :])
 
         def step(u, t):
             n = PACK * u + t + 1
             if n < PACK * UNITS:
                 phase(*divmod(n, PACK))
-            if u == 0 or (u % GROUPS == GROUPS - 1 and t >= 2):
+            if u == 0 or (u % 2 == 1 and t >= 2):
                 cosine(u, t, t + 1)
             elif t % 2 == 0:
                 cosine(u, t, t + 2)
             feature(u, t)
 
+        def unit(u):
+            for t in range(PACK):
+                step(u, t)
+
         def quantise_h(u, c0=0, c1=SHOTS):
             half, g = divmod(u, GROUPS)
+            shots = slice(half * SHOTS + c0, half * SHOTS + c1)
             nc.vector.quantize_mx(
-                out=h_codes[g][:, half * SHOTS + c0:half * SHOTS + c1].bitcast(FP8X4),
-                scales=h_planes[half][:, g, c0:c1], in_=staged["h", u, c0][:],
+                out=h_codes[g][:, shots].bitcast(FP8X4), scales=h_planes[half][:, g, c0:c1], in_=staged["h", u, c0][:]
             )
 
-        def store_codes(u):
-            half, g = divmod(u, GROUPS)
+        def store_codes(g, shots):
             words = out_2[g].rearrange("p m t -> p (m t)").bitcast(I32)
-            nc.sync.dma_start(words[:, shot_range(half)], h_codes[g][:, shot_range(half)].bitcast(I32))
-            if g == GROUPS - 1:
-                for r in range(4):
-                    nc.sync.dma_start(
-                        out_3[:, r:16:4, shot_range(half)].rearrange("g q m -> q g m").bitcast(I32),
-                        h_planes[half][r:P:32].bitcast(I32),
-                    )
+            nc.sync.dma_start(words[:, shots], h_codes[g][:, shots].bitcast(I32))
+
+        def store_scale_rows(half):
+            for r in range(4):
+                nc.sync.dma_start(
+                    out_3[:, r:16:4, shot_range(half)].rearrange("g q m -> q g m").bitcast(I32),
+                    h_planes[half][r:P:32].bitcast(I32),
+                )
+
+        y_rows = [sb("y%d" % half, [P, BLOCKS, SHOTS], F32) for half in range(HALVES)]
 
         def response(half, i):
-            resp, lin = bank("resp", PHASE_BANKS[i]), bank("lin", AMPL_BANKS[i])
+            resp = bank("resp", PHASE_BANKS[i])
             for g in range(GROUPS):
                 rhs = h_codes[g][:, shot_range(half)].bitcast(FP8X4), h_planes[half][:, g, :]
                 product(resp, stationary("w3", g, i), rhs, start=(g == 0), stop=(g == GROUPS - 1))
-            cols = slice(i * P, (i + 1) * P)
-            product(lin, (w4_codes[:, cols].bitcast(FP8X4), w4_plane[:, cols]), picked_shots(half))
-            sine = ring.tile([P, SHOTS], F32, name="sine", bufs=HALVES * N // P)
+            sine = ring.tile([P, SHOTS], F32, name="sine", bufs=HALVES * BLOCKS)
             nc.scalar.activation(sine[:], resp[:], ACT.Sin)
-            pending[half, i] = sine, lin
+            pending[half, i] = sine
 
         def result(half, i):
-            sine, lin = pending[half, i]
-            y = sb("y%d_%d" % (half, i), [P, SHOTS], F32)
-            nc.vector.scalar_tensor_tensor(y[:], sine[:], amp_sb[:, i, :], lin[:], ALU.mult, ALU.add)
-            nc.sync.dma_start(out_0[i * P:(i + 1) * P, shot_range(half)], y[:])
+            sine, lin = pending[half, i], bank("lin", AMPL_BANKS[i])
+            cols = slice(i * P, (i + 1) * P)
+            product(lin, (w4_codes[:, cols].bitcast(FP8X4), w4_plane[:, cols]), picked_shots(half))
+            nc.vector.scalar_tensor_tensor(y_rows[half][:, i, :], sine[:], amp_sb[:, i, :], lin[:], ALU.mult, ALU.add)
 
-        for part in range(3):
-            round_wa(part)
+        def store_results(half, i0, i1):
+            rows = out_0[:, shot_range(half)].rearrange("(i p) j -> p i j", p=P)
+            nc.sync.dma_start(rows[:, i0:i1, :], y_rows[half][:, i0:i1, :])
+
+        stage("wa", 0)
+        round_wa(0)
+        round_wa(1)
         quantise_weight("wa", 0, 0, P)
         quantise_weight("wa", 0, P, PASS)
-        round_wa(3)
+        stage("wa", 1)
+        round_wa(2)
         phase(0, 0)
         step(0, 0)
         step(0, 1)
-        round_wa(4)
+        round_wa(3)
         step(0, 2)
         quantise_weight("wa", 1)
         step(0, 3)
 
         stage("w3", 0)
-        round_columns("w3", 0, on_vector)
-        stage("h", 0, 0, MID)
-        round_columns("h", 0, on_vector, 0, MID - SCALAR_SHOTS[0])
-        quantise_weight("w3", 0)
-        round_columns("h", 0, on_scalar, MID - SCALAR_SHOTS[0], MID)
-        stage("h", 0, MID, MID, tag="w3_bf0_0")
-        round_columns("h", 0, on_gpsimd, MID, SHOTS, MID)
-        for t in range(PACK):
-            step(1, t)
+        round_columns("w3", 0, on_vector, 0, MID)
+        stage("h", 0, 0, CUT)
+        round_columns("h", 0, on_vector, 0, CUT)
+        round_columns("w3", 0, on_vector, MID, N)
+        quantise_weight("w3", 0, 0, MID)
+        stage("h", 0, CUT, SHOTS - CUT, at=FIRST_JOB_AT)
+        round_columns("h", 0, on_gpsimd, CUT, SHOTS, CUT)
+        unit(1)
 
-        quantise_h(0, 0, MID)
+        quantise_weight("w3", 0, MID, N)
+        quantise_h(0, 0, CUT)
         stage("h", 1)
         round_columns("h", 1, on_vector)
-        stage("w3", 1, 0, MID)
-        round_columns("w3", 1, on_vector, 0, MID)
-        quantise_h(0, MID, SHOTS)
-        store_codes(0)
-        quantise_weight("w3", 1, 0, MID)
+        stage("w3", 1, 0, CUT)
+        round_columns("w3", 1, on_vector, 0, CUT)
+        quantise_h(0, CUT, SHOTS)
+        store_codes(0, shot_range(0))
         quantise_h(1)
-        store_codes(1)
-        stage("w3", 1, MID, MID, tag="h_bf1_0")
-        round_columns("w3", 1, on_gpsimd, MID, N, MID)
-        for t in range(PACK):
-            step(2, t)
+        store_codes(1, shot_range(0))
+        store_scale_rows(0)
+        stage("w3", 1, CUT, N - CUT, at=SECOND_JOB_AT)
+        round_columns("w3", 1, on_gpsimd, CUT, N, CUT)
+        unit(2)
 
-        quantise_weight("w3", 1, MID, N, MID)
-        stage("h", 2, tag="h_bf1_0")
+        quantise_weight("w3", 1, 0, CUT)
+        quantise_weight("w3", 1, CUT, N, CUT)
+        stage("h", 2, at=SECOND_JOB_AT)
         round_columns("h", 2, on_gpsimd, SCALAR_SHOTS[2], SHOTS)
-        for t in range(PACK):
-            step(3, t)
+        unit(3)
 
-        response(0, 0)
         round_columns("h", 2, on_scalar, 0, SCALAR_SHOTS[2])
-        response(0, 1)
-        result(0, 0)
+        quantise_h(2)
+        store_codes(0, shot_range(1))
+        response(0, 0)
         stage("h", 3)
-        round_columns("h", 3, on_vector, 0, SHOTS - SCALAR_SHOTS[3])
         round_columns("h", 3, on_scalar, SHOTS - SCALAR_SHOTS[3], SHOTS)
-        for u in (2, 3):
-            quantise_h(u)
-            store_codes(u)
+        round_columns("h", 3, on_vector, 0, SHOTS - SCALAR_SHOTS[3])
+        result(0, 0)
+        store_results(0, 0, 1)
+        quantise_h(3)
+        store_codes(1, shot_range(1))
+        store_scale_rows(1)
+        response(0, 1)
         result(0, 1)
-        for job in (response, result):
-            for i in (2, 3):
-                job(0, i)
-        for job in (response, result):
-            for i in range(N // P):
-                job(1, i)
+        store_results(0, 1, 2)
+        for i in (2, 3):
+            response(0, i)
+        for i in (2, 3):
+            result(0, i)
+            store_results(0, i, i + 1)
+        for i in range(BLOCKS):
+            response(1, i)
+        for i in range(BLOCKS):
+            result(1, i)
+            store_results(1, i, i + 1)

@@ -28,14 +28,14 @@ BLOCKS = N // P
 MID = 256
 CUT = 128
 UNIT_BYTES = PACK * SHOTS * 4
-WA_PARTS = [(0, 0, 256), (0, 256, 256), (1, 0, 256), (1, 256, 256)]
-TAB_FIRST = 768
+WA_PARTS = [(0, 0, 128), (0, 128, 192), (0, 320, 192), (1, 0, 256), (1, 256, 256)]
+TAB_FIRST = 640
 SCALAR_SHOTS = {2: 128, 3: 192}
 KB = 1024
 SECOND_JOB_AT = 32 * KB
-FIRST_JOB_AT = 35 * KB - 64
-H_AT = {2: 36 * KB, 1: 44 * KB}
-W3_FIRST_AT = 37 * KB
+H_AT = {2: 36 * KB, 1: 53 * KB}
+FIRST_JOB_AT = 44 * KB
+W3_FIRST_AT = 46 * KB
 COS_AT = [0, UNIT_BYTES, 2 * UNIT_BYTES, 3 * UNIT_BYTES]
 PHASE_BANKS, AMPL_BANKS = (0, 1, 4, 5), (2, 3, 6, 7)
 
@@ -59,13 +59,14 @@ def tile_list_readout_phase_calibration_kernel(
 
         offsets = keep.tile([P, S // 16], U16, name="offsets")
         nc.sync.dma_start(offsets[:], offs)
+        wp_raw = sb("wp_raw", [P, 2 * H], U8)
+        nc.sync.dma_start(wp_raw[:].bitcast(I32), wp_words[0].bitcast(I32))
         tab = sb("tab", [P, T], U32)
         tab_src = tab_words[0].rearrange("p t i -> p (t i)").bitcast(I32)
-        nc.sync.dma_start(tab[:, :TAB_FIRST].bitcast(I32), tab_src[:, :TAB_FIRST])
 
-        def load_scale_rows(rows, src):
+        def load_scale_rows(rows, src, queue=nc.sync):
             nc.vector.memset(rows.bitcast(I32), 0)
-            nc.sync.dma_start(rows[0:P:8, :].bitcast(I32), src[0].bitcast(I32))
+            queue.dma_start(rows[0:P:8, :].bitcast(I32), src[0].bitcast(I32))
 
         def seat_scale_rows(plane):
             for r in range(1, 4):
@@ -75,16 +76,15 @@ def tile_list_readout_phase_calibration_kernel(
         later_planes = sb("later_planes", [P, SHOTS + N], U8)
         wp_plane, w4_plane = first_planes[:, SHOTS:], later_planes[:, SHOTS:]
         v_planes = [first_planes[:, :SHOTS], later_planes[:, :SHOTS]]
+        load_scale_rows(w4_plane, w4_scales, nc.scalar)
+        nc.sync.dma_start(tab[:, :TAB_FIRST].bitcast(I32), tab_src[:, :TAB_FIRST])
         tab_rows = sb("tab_rows", [P, T], U8)
         load_scale_rows(tab_rows[:], tab_scales)
         wp_rows = sb("wp_rows", [P, H], U8)
         load_scale_rows(wp_rows[:], wp_scales)
         nc.sync.dma_start(tab[:, TAB_FIRST:].bitcast(I32), tab_src[:, TAB_FIRST:])
-        wp_raw = sb("wp_raw", [P, 2 * H], U8)
-        nc.sync.dma_start(wp_raw[:].bitcast(I32), wp_words[0].bitcast(I32))
 
         phi_sb = sb("phi_sb", [P, GROUPS, 2 * PACK], F32)
-        nc.scalar.dma_start(phi_sb[:, :, :PACK], phi.rearrange("(g p t) -> p g t", g=GROUPS, t=PACK))
         zero = sb("zero", [P, 1], F32)
         nc.vector.memset(zero[:], 0.0)
         warm = sb("warm", [P, 1], F32)
@@ -107,16 +107,12 @@ def tile_list_readout_phase_calibration_kernel(
             wp_rows[:].rearrange("p (g m t) -> p g t m", g=GROUPS, t=PACK),
         )
         place_scales(0, picked_rows)
-        seat_scale_rows(first_planes)
-        load_scale_rows(w4_plane, w4_scales)
         place_scales(1, look_up_scales(1))
-        wp_codes = [sb("wp_codes%d" % g, [P, 2 * PASS], U8) for g in range(GROUPS)]
-        for g in range(GROUPS):
-            cols = slice(2 * g * PASS, 2 * (g + 1) * PASS)
-            nc.scalar.copy(
-                wp_codes[g][:].bitcast(U16).rearrange("p (t m) -> p t m", t=PACK),
-                wp_raw[:, cols].bitcast(U16).rearrange("p (m t) -> p t m", t=PACK),
-            )
+        wp_codes = sb("wp_codes", [P, 2 * H], U8)
+        nc.vector.tensor_copy(
+            wp_codes[:].bitcast(U16).rearrange("p (g t m) -> p g t m", g=GROUPS, t=PACK),
+            wp_raw[:].bitcast(U16).rearrange("p (g m t) -> p g t m", g=GROUPS, t=PACK),
+        )
 
         wa_raw, w3_raw, v_codes = {}, {}, []
 
@@ -134,9 +130,12 @@ def tile_list_readout_phase_calibration_kernel(
             nc.sync.dma_start(w3_raw[g][:], w3[g * PASS:(g + 1) * PASS, :].rearrange("(p j) n -> p j n", j=PACK))
 
         load_wa(0)
+        seat_scale_rows(first_planes)
+        nc.sync.dma_start(phi_sb[:, :, :PACK], phi.rearrange("(g p t) -> p g t", g=GROUPS, t=PACK))
         load_wa(1)
         load_wa(2)
         load_wa(3)
+        load_wa(4)
         load_w3(0)
         seat_scale_rows(later_planes)
         load_w3(1)
@@ -175,7 +174,7 @@ def tile_list_readout_phase_calibration_kernel(
         def round_wa(part):
             g, c0, width = WA_PARTS[part]
             dealt = staged["wa", g, 0][:].rearrange("p (t m u w) -> p m u t w", t=PACK, u=2, w=2)
-            nc.vector.tensor_copy(
+            (nc.scalar.copy if part == 0 else nc.vector.tensor_copy)(
                 dealt[:, c0 // PACK:(c0 + width) // PACK],
                 wa_raw[part].rearrange("p (u w) (m t) -> p m u t w", w=2, t=PACK),
             )
@@ -227,7 +226,7 @@ def tile_list_readout_phase_calibration_kernel(
             out = bank("phase", PHASE_BANKS[t] if u > 0 else t)
             if t == 0:
                 folded[u] = ring.tile([P, PACK, SHOTS], F32, name="folded", bufs=2)
-            lhsT = wp_codes[g][:, 2 * t * P:2 * (t + 1) * P].bitcast(FP4X4), wp_plane[:, col:col + P]
+            lhsT = wp_codes[:, 2 * col:2 * (col + P)].bitcast(FP4X4), wp_plane[:, col:col + P]
             product(out, lhsT, picked_shots(half))
             nc.scalar.activation(folded[u][:, t, :], out[:], ACT.Abs, bias=phi_sb[:, g, t:t + 1])
 
@@ -310,14 +309,15 @@ def tile_list_readout_phase_calibration_kernel(
         stage("wa", 0)
         round_wa(0)
         round_wa(1)
+        round_wa(2)
         quantise_weight("wa", 0, 0, P)
         quantise_weight("wa", 0, P, PASS)
         stage("wa", 1)
-        round_wa(2)
+        round_wa(3)
         phase(0, 0)
         step(0, 0)
         step(0, 1)
-        round_wa(3)
+        round_wa(4)
         step(0, 2)
         quantise_weight("wa", 1)
         step(0, 3)
@@ -336,18 +336,18 @@ def tile_list_readout_phase_calibration_kernel(
         quantise_h(0, 0, CUT)
         stage("h", 1)
         round_columns("h", 1, on_vector)
-        stage("w3", 1, 0, CUT)
+        stage("w3", 1, 0, CUT, at=H_AT[2] - 512)
         round_columns("w3", 1, on_vector, 0, CUT)
         quantise_h(0, CUT, SHOTS)
         store_codes(0, shot_range(0))
+        quantise_weight("w3", 1, 0, CUT)
         quantise_h(1)
         store_codes(1, shot_range(0))
         store_scale_rows(0)
-        stage("w3", 1, CUT, N - CUT, at=SECOND_JOB_AT)
+        stage("w3", 1, CUT, N - CUT, at=SECOND_JOB_AT + KB)
         round_columns("w3", 1, on_gpsimd, CUT, N, CUT)
         unit(2)
 
-        quantise_weight("w3", 1, 0, CUT)
         quantise_weight("w3", 1, CUT, N, CUT)
         stage("h", 2, at=SECOND_JOB_AT)
         round_columns("h", 2, on_gpsimd, SCALAR_SHOTS[2], SHOTS)

@@ -29,7 +29,7 @@ MID = 256
 CUT = 128
 UNIT_BYTES = PACK * SHOTS * 4
 WA_PARTS = [(0, 0, 128), (0, 128, 192), (0, 320, 192), (1, 0, 256), (1, 256, 256)]
-TAB_FIRST = 640
+TAB_FIRST = 256
 SCALAR_SHOTS = {2: 128, 3: 192}
 KB = 1024
 SECOND_JOB_AT = 32 * KB
@@ -77,11 +77,11 @@ def tile_list_readout_phase_calibration_kernel(
         wp_plane, w4_plane = first_planes[:, SHOTS:], later_planes[:, SHOTS:]
         v_planes = [first_planes[:, :SHOTS], later_planes[:, :SHOTS]]
         load_scale_rows(w4_plane, w4_scales, nc.scalar)
+        wp_rows = sb("wp_rows", [P, H], U8)
+        load_scale_rows(wp_rows[:], wp_scales)
         nc.sync.dma_start(tab[:, :TAB_FIRST].bitcast(I32), tab_src[:, :TAB_FIRST])
         tab_rows = sb("tab_rows", [P, T], U8)
         load_scale_rows(tab_rows[:], tab_scales)
-        wp_rows = sb("wp_rows", [P, H], U8)
-        load_scale_rows(wp_rows[:], wp_scales)
         nc.sync.dma_start(tab[:, TAB_FIRST:].bitcast(I32), tab_src[:, TAB_FIRST:])
 
         phi_sb = sb("phi_sb", [P, GROUPS, 2 * PACK], F32)
@@ -101,12 +101,11 @@ def tile_list_readout_phase_calibration_kernel(
         def place_scales(half, picked):
             nc.vector.tensor_copy(v_planes[half].bitcast(I32), picked[:].bitcast(I32))
 
-        picked_rows = look_up_scales(0)
         nc.vector.tensor_copy(
             wp_plane.rearrange("p (g t m) -> p g t m", g=GROUPS, t=PACK),
             wp_rows[:].rearrange("p (g m t) -> p g t m", g=GROUPS, t=PACK),
         )
-        place_scales(0, picked_rows)
+        place_scales(0, look_up_scales(0))
         place_scales(1, look_up_scales(1))
         wp_codes = sb("wp_codes", [P, 2 * H], U8)
         nc.vector.tensor_copy(

@@ -291,7 +291,12 @@ def tile_list_readout_phase_calibration_kernel(
             for g in range(GROUPS):
                 rhs = h_codes[g][:, shot_range(half)].bitcast(FP8X4), h_planes[half][:, g, :]
                 product(resp, stationary("w3", g, i), rhs, start=(g == 0), stop=(g == GROUPS - 1))
-            sine = ring.tile([P, SHOTS], F32, name="sine", bufs=HALVES * BLOCKS)
+            if half == 0 and i > 0:
+                sine = placed.tile(
+                    [P, SHOTS], F32, name="sine%d" % i, align_bytes=64, offset=COS_AT[UNITS - 1] + i * UNIT_BYTES // PACK
+                )
+            else:
+                sine = ring.tile([P, SHOTS], F32, name="sine", bufs=BLOCKS + 1)
             nc.scalar.activation(sine[:], resp[:], ACT.Sin)
             pending[half, i] = sine
 
@@ -352,15 +357,15 @@ def tile_list_readout_phase_calibration_kernel(
         round_columns("h", 2, on_gpsimd, SCALAR_SHOTS[2], SHOTS)
         unit(3)
 
-        round_columns("h", 2, on_scalar, 0, SCALAR_SHOTS[2])
-        quantise_h(2)
-        store_codes(0, shot_range(1))
         response(0, 0)
+        round_columns("h", 2, on_scalar, 0, SCALAR_SHOTS[2])
+        result(0, 0)
+        store_results(0, 0, 1)
         stage("h", 3)
         round_columns("h", 3, on_scalar, SHOTS - SCALAR_SHOTS[3], SHOTS)
         round_columns("h", 3, on_vector, 0, SHOTS - SCALAR_SHOTS[3])
-        result(0, 0)
-        store_results(0, 0, 1)
+        quantise_h(2)
+        store_codes(0, shot_range(1))
         quantise_h(3)
         store_codes(1, shot_range(1))
         store_scale_rows(1)

@@ -26,16 +26,15 @@ HALVES = S // SHOTS
 UNITS = GROUPS * HALVES
 BLOCKS = N // P
 MID = 256
-CUT = 128
+CUT = 192
 UNIT_BYTES = PACK * SHOTS * 4
 WA_PARTS = [(0, 0, 128), (0, 128, 192), (0, 320, 192), (1, 0, 256), (1, 256, 256)]
 TAB_FIRST = 256
 SCALAR_SHOTS = {2: 128, 3: 192}
 KB = 1024
 SECOND_JOB_AT = 32 * KB
-H_AT = {2: 36 * KB, 1: 53 * KB}
-FIRST_JOB_AT = 44 * KB
-W3_FIRST_AT = 46 * KB
+W3_FIRST_AT = 38 * KB
+H_AT = {1: W3_FIRST_AT}
 COS_AT = [0, UNIT_BYTES, 2 * UNIT_BYTES, 3 * UNIT_BYTES]
 PHASE_BANKS, AMPL_BANKS = (0, 1, 4, 5), (2, 3, 6, 7)
 
@@ -164,15 +163,15 @@ def tile_list_readout_phase_calibration_kernel(
         def stage(name, index, first=0, width=SHOTS, tag=None, at=None):
             label = "%s_bf%d_%d" % (name, index, first)
             if at is None:
-                staged[name, index, first] = sb(label, [P, PACK * width], BF16, tag=tag)
+                staged[name, index, first] = sb(label, [P, PACK * width], BF16, tag=tag)[:]
             else:
                 staged[name, index, first] = placed.tile(
                     [P, PACK * width], BF16, name=label, align_bytes=64, offset=at
-                )
+                )[:]
 
         def round_wa(part):
             g, c0, width = WA_PARTS[part]
-            dealt = staged["wa", g, 0][:].rearrange("p (t m u w) -> p m u t w", t=PACK, u=2, w=2)
+            dealt = staged["wa", g, 0].rearrange("p (t m u w) -> p m u t w", t=PACK, u=2, w=2)
             (nc.scalar.copy if part == 0 else nc.vector.tensor_copy)(
                 dealt[:, c0 // PACK:(c0 + width) // PACK],
                 wa_raw[part].rearrange("p (u w) (m t) -> p m u t w", w=2, t=PACK),
@@ -270,7 +269,8 @@ def tile_list_readout_phase_calibration_kernel(
             half, g = divmod(u, GROUPS)
             shots = slice(half * SHOTS + c0, half * SHOTS + c1)
             nc.vector.quantize_mx(
-                out=h_codes[g][:, shots].bitcast(FP8X4), scales=h_planes[half][:, g, c0:c1], in_=staged["h", u, c0][:]
+                out=h_codes[g][:, shots].bitcast(FP8X4), scales=h_planes[half][:, g, c0:c1],
+                in_=staged["h", u, 0][:, PACK * c0:PACK * c1],
             )
 
         def store_codes(g, shots):
@@ -326,33 +326,35 @@ def tile_list_readout_phase_calibration_kernel(
         quantise_weight("wa", 1)
         step(0, 3)
 
-        stage("w3", 0)
+        first_stage = sb("first_stage", [P, PACK * SHOTS], BF16)
+        staged["h", 0, 0] = first_stage[:]
+        staged["w3", 0, 0] = first_stage[:, PACK * MID:]
         round_columns("w3", 0, on_vector, 0, MID)
-        stage("h", 0, 0, CUT)
         round_columns("h", 0, on_vector, 0, CUT)
-        round_columns("w3", 0, on_vector, MID, N)
+        stage("w3", 0, MID, N - MID)
+        round_columns("w3", 0, on_vector, MID, N, MID)
         quantise_weight("w3", 0, 0, MID)
-        stage("h", 0, CUT, SHOTS - CUT, at=FIRST_JOB_AT)
-        round_columns("h", 0, on_gpsimd, CUT, SHOTS, CUT)
+        quantise_weight("w3", 0, MID, N, MID)
+        round_columns("h", 0, on_gpsimd, CUT, SHOTS)
         unit(1)
 
-        quantise_weight("w3", 0, MID, N)
-        quantise_h(0, 0, CUT)
-        stage("h", 1)
-        round_columns("h", 1, on_vector)
-        stage("w3", 1, 0, CUT, at=H_AT[2] - 512)
-        round_columns("w3", 1, on_vector, 0, CUT)
-        quantise_h(0, CUT, SHOTS)
+        quantise_h(0)
         store_codes(0, shot_range(0))
-        quantise_weight("w3", 1, 0, CUT)
-        quantise_h(1)
+        second_stage = placed.tile(
+            [P, PACK * (MID + SHOTS)], BF16, name="second_stage", align_bytes=64, offset=SECOND_JOB_AT
+        )
+        staged["w3", 1, 0] = second_stage[:, :PACK * N]
+        staged["h", 1, 0] = second_stage[:, PACK * MID:]
+        round_columns("h", 1, on_vector)
+        round_columns("w3", 1, on_vector, 0, CUT)
+        quantise_h(1, 0, MID)
+        quantise_h(1, MID, SHOTS)
         store_codes(1, shot_range(0))
         store_scale_rows(0)
-        stage("w3", 1, CUT, N - CUT, at=SECOND_JOB_AT + KB)
-        round_columns("w3", 1, on_gpsimd, CUT, N, CUT)
+        round_columns("w3", 1, on_gpsimd, CUT, N)
         unit(2)
 
-        quantise_weight("w3", 1, CUT, N, CUT)
+        quantise_weight("w3", 1)
         stage("h", 2, at=SECOND_JOB_AT)
         round_columns("h", 2, on_gpsimd, SCALAR_SHOTS[2], SHOTS)
         unit(3)

@@ -37,6 +37,7 @@ W3_FIRST_AT = 38 * KB
 H_AT = {1: W3_FIRST_AT}
 COS_AT = [0, UNIT_BYTES, 2 * UNIT_BYTES, 3 * UNIT_BYTES]
 PHASE_BANKS, AMPL_BANKS = (0, 1, 4, 5), (2, 3, 6, 7)
+RESP_BANKS, LIN_BANKS = (PHASE_BANKS, (1, 4, 5, 3)), (AMPL_BANKS, (0, 2, 6, 7))
 
 
 def tile_list_readout_phase_calibration_kernel(
@@ -287,7 +288,7 @@ def tile_list_readout_phase_calibration_kernel(
         y_rows = [sb("y%d" % half, [P, BLOCKS, SHOTS], F32) for half in range(HALVES)]
 
         def response(half, i):
-            resp = bank("resp", PHASE_BANKS[i])
+            resp = bank("resp", RESP_BANKS[half][i])
             for g in range(GROUPS):
                 rhs = h_codes[g][:, shot_range(half)].bitcast(FP8X4), h_planes[half][:, g, :]
                 product(resp, stationary("w3", g, i), rhs, start=(g == 0), stop=(g == GROUPS - 1))
@@ -301,7 +302,7 @@ def tile_list_readout_phase_calibration_kernel(
             pending[half, i] = sine
 
         def result(half, i):
-            sine, lin = pending[half, i], bank("lin", AMPL_BANKS[i])
+            sine, lin = pending[half, i], bank("lin", LIN_BANKS[half][i])
             cols = slice(i * P, (i + 1) * P)
             product(lin, (w4_codes[:, cols].bitcast(FP8X4), w4_plane[:, cols]), picked_shots(half))
             nc.vector.scalar_tensor_tensor(y_rows[half][:, i, :], sine[:], amp_sb[:, i, :], lin[:], ALU.mult, ALU.add)

@@ -29,7 +29,7 @@ MID = 256
 CUT = 192
 UNIT_BYTES = PACK * SHOTS * 4
 WA_PARTS = [(0, 0, 128), (0, 128, 192), (0, 320, 192), (1, 0, 256), (1, 256, 256)]
-TAB_FIRST = 256
+TAB_FIRST = 512
 SCALAR_SHOTS = {2: 128, 3: 192}
 KB = 1024
 SECOND_JOB_AT = 32 * KB
@@ -49,6 +49,7 @@ def tile_list_readout_phase_calibration_kernel(
         keep = ctx.enter_context(tc.tile_pool(name="keep", bufs=1))
         psum = ctx.enter_context(tc.psum_pool(name="psum", bufs=1))
         ring = ctx.enter_context(tc.tile_pool(name="ring", bufs=1))
+        head = ctx.enter_context(tc.tile_pool(name="head", bufs=1))
         placed = ctx.enter_context(tc.tile_pool(name="placed", bufs=1))
 
         def sb(name, shape, dtype, tag=None):
@@ -59,8 +60,6 @@ def tile_list_readout_phase_calibration_kernel(
 
         offsets = keep.tile([P, S // 16], U16, name="offsets")
         nc.sync.dma_start(offsets[:], offs)
-        wp_raw = sb("wp_raw", [P, 2 * H], U8)
-        nc.sync.dma_start(wp_raw[:].bitcast(I32), wp_words[0].bitcast(I32))
         tab = sb("tab", [P, T], U32)
         tab_src = tab_words[0].rearrange("p t i -> p (t i)").bitcast(I32)
 
@@ -76,12 +75,14 @@ def tile_list_readout_phase_calibration_kernel(
         later_planes = sb("later_planes", [P, SHOTS + N], U8)
         wp_plane, w4_plane = first_planes[:, SHOTS:], later_planes[:, SHOTS:]
         v_planes = [first_planes[:, :SHOTS], later_planes[:, :SHOTS]]
-        load_scale_rows(w4_plane, w4_scales, nc.scalar)
+        nc.sync.dma_start(tab[:, :TAB_FIRST].bitcast(I32), tab_src[:, :TAB_FIRST])
         wp_rows = sb("wp_rows", [P, H], U8)
         load_scale_rows(wp_rows[:], wp_scales)
-        nc.sync.dma_start(tab[:, :TAB_FIRST].bitcast(I32), tab_src[:, :TAB_FIRST])
         tab_rows = sb("tab_rows", [P, T], U8)
         load_scale_rows(tab_rows[:], tab_scales)
+        load_scale_rows(w4_plane, w4_scales, nc.scalar)
+        wp_raw = sb("wp_raw", [P, 2 * H], U8)
+        nc.sync.dma_start(wp_raw[:].bitcast(I32), wp_words[0].bitcast(I32))
         nc.sync.dma_start(tab[:, TAB_FIRST:].bitcast(I32), tab_src[:, TAB_FIRST:])
 
         phi_sb = sb("phi_sb", [P, GROUPS, 2 * PACK], F32)
@@ -94,7 +95,7 @@ def tile_list_readout_phase_calibration_kernel(
             return offsets[:, half * SHOTS // 16:(half + 1) * SHOTS // 16]
 
         def look_up_scales(half):
-            picked = sb("v_rows%d" % half, [P, SHOTS], U8, tag="v_rows")
+            picked = head.tile([P, SHOTS], U8, name="v_rows%d" % half, align_bytes=64, offset=2 * H - SHOTS // 2 * (1 - half))
             nc.vector.tensor_copy(picked[:], tab_rows[:].indirect(list_half(half)))
             return picked
 
@@ -107,7 +108,7 @@ def tile_list_readout_phase_calibration_kernel(
         )
         place_scales(0, look_up_scales(0))
         place_scales(1, look_up_scales(1))
-        wp_codes = sb("wp_codes", [P, 2 * H], U8)
+        wp_codes = head.tile([P, 2 * H], U8, name="wp_codes", align_bytes=64, offset=0)
         nc.vector.tensor_copy(
             wp_codes[:].bitcast(U16).rearrange("p (g t m) -> p g t m", g=GROUPS, t=PACK),
             wp_raw[:].bitcast(U16).rearrange("p (g m t) -> p g t m", g=GROUPS, t=PACK),

@@ -29,7 +29,7 @@ MID = 256
 CUT = 192
 UNIT_BYTES = PACK * SHOTS * 4
 WA_PARTS = [(0, 0, 128), (0, 128, 192), (0, 320, 192), (1, 0, 256), (1, 256, 256)]
-TAB_FIRST = 512
+TAB_FIRST = 448
 SCALAR_SHOTS = {2: 128, 3: 192}
 KB = 1024
 SECOND_JOB_AT = 32 * KB
@@ -59,7 +59,6 @@ def tile_list_readout_phase_calibration_kernel(
             return psum.tile([P, SHOTS], F32, name=name, tag="bank%d" % number)
 
         offsets = keep.tile([P, S // 16], U16, name="offsets")
-        nc.sync.dma_start(offsets[:], offs)
         tab = sb("tab", [P, T], U32)
         tab_src = tab_words[0].rearrange("p t i -> p (t i)").bitcast(I32)
 
@@ -78,6 +77,7 @@ def tile_list_readout_phase_calibration_kernel(
         nc.sync.dma_start(tab[:, :TAB_FIRST].bitcast(I32), tab_src[:, :TAB_FIRST])
         wp_rows = sb("wp_rows", [P, H], U8)
         load_scale_rows(wp_rows[:], wp_scales)
+        nc.sync.dma_start(offsets[:], offs)
         tab_rows = sb("tab_rows", [P, T], U8)
         load_scale_rows(tab_rows[:], tab_scales)
         load_scale_rows(w4_plane, w4_scales, nc.scalar)

import math
from contextlib import ExitStack

import concourse.mybir as mybir

K, T, S, H, N = 512, 4096, 1024, 1024, 512
FLOPS = 2 * S * (2 * K * H + H * N + K * N)

F32 = mybir.dt.float32
BF16 = mybir.dt.bfloat16
I32 = mybir.dt.int32
U32 = mybir.dt.uint32
U16 = mybir.dt.uint16
U8 = mybir.dt.uint8
FP8X4 = mybir.dt.float8_e4m3fn_x4
FP4X4 = mybir.dt.float4_e2m1fn_x4
ACT = mybir.ActivationFunctionType
ALU = mybir.AluOpType

P = 128
PACK = 4
PASS = P * PACK
GROUPS = H // PASS
SHOTS = 512
HALVES = S // SHOTS
UNITS = GROUPS * HALVES
BLOCKS = N // P
MID = 256
CUT = 192
UNIT_BYTES = PACK * SHOTS * 4
WA_PARTS = [(0, 0, 128), (0, 128, 192), (0, 320, 192), (1, 0, 256), (1, 256, 256)]
TAB_FIRST = 448
SCALAR_SHOTS = {2: 128, 3: 192}
KB = 1024
SECOND_JOB_AT = 32 * KB
W3_FIRST_AT = 38 * KB
H_AT = {1: W3_FIRST_AT}
COS_AT = [0, UNIT_BYTES, 2 * UNIT_BYTES, 3 * UNIT_BYTES]
PHASE_BANKS, AMPL_BANKS = (0, 1, 4, 5), (2, 3, 6, 7)
RESP_BANKS, LIN_BANKS = (PHASE_BANKS, (1, 4, 5, 3)), (AMPL_BANKS, (0, 2, 6, 7))


def tile_list_readout_phase_calibration_kernel(
    tc, tab_words, tab_scales, offs, wp_words, wp_scales, phi, wa, w3, amp, w4_words, w4_scales,
    out_0, out_1, out_2, out_3,
):
    nc = tc.nc
    with ExitStack() as ctx:
        keep = ctx.enter_context(tc.tile_pool(name="keep", bufs=1))
        psum = ctx.enter_context(tc.psum_pool(name="psum", bufs=1))
        ring = ctx.enter_context(tc.tile_pool(name="ring", bufs=1))
        head = ctx.enter_context(tc.tile_pool(name="head", bufs=1))
        placed = ctx.enter_context(tc.tile_pool(name="placed", bufs=1))

        def sb(name, shape, dtype, tag=None):
            return keep.tile(shape, dtype, name=name, tag=tag or name, align_bytes=64)

        def bank(name, number):
            return psum.tile([P, SHOTS], F32, name=name, tag="bank%d" % number)

        offsets = keep.tile([P, S // 16], U16, name="offsets")
        tab = sb("tab", [P, T], U32)
        tab_src = tab_words[0].rearrange("p t i -> p (t i)").bitcast(I32)

        def load_scale_rows(rows, src, queue=nc.sync):
            nc.vector.memset(rows.bitcast(I32), 0)
            queue.dma_start(rows[0:P:8, :].bitcast(I32), src[0].bitcast(I32))

        def seat_scale_rows(plane):
            for r in range(1, 4):
                nc.sync.dma_start(plane[r:P:32, :].bitcast(I32), plane[8 * r:P:32, :].bitcast(I32))

        first_planes = sb("first_planes", [P, SHOTS + H], U8)
        later_planes = sb("later_planes", [P, SHOTS + N], U8)
        wp_plane, w4_plane = first_planes[:, SHOTS:], later_planes[:, SHOTS:]
        v_planes = [first_planes[:, :SHOTS], later_planes[:, :SHOTS]]
        nc.sync.dma_start(tab[:, :TAB_FIRST].bitcast(I32), tab_src[:, :TAB_FIRST])
        wp_rows = sb("wp_rows", [P, H], U8)
        load_scale_rows(wp_rows[:], wp_scales)
        nc.sync.dma_start(offsets[:], offs)
        tab_rows = sb("tab_rows", [P, T], U8)
        load_scale_rows(tab_rows[:], tab_scales)
        load_scale_rows(w4_plane, w4_scales, nc.scalar)
        wp_raw = sb("wp_raw", [P, 2 * H], U8)
        nc.sync.dma_start(wp_raw[:].bitcast(I32), wp_words[0].bitcast(I32))
        nc.sync.dma_start(tab[:, TAB_FIRST:].bitcast(I32), tab_src[:, TAB_FIRST:])

        phi_sb = sb("phi_sb", [P, GROUPS, 2 * PACK], F32)
        zero = sb("zero", [P, 1], F32)
        nc.vector.memset(zero[:], 0.0)
        warm = sb("warm", [P, 1], F32)
        nc.scalar.activation(warm[:], zero[:], ACT.Sin)

        def list_half(half):
            return offsets[:, half * SHOTS // 16:(half + 1) * SHOTS // 16]

        def look_up_scales(half):
            picked = head.tile([P, SHOTS], U8, name="v_rows%d" % half, align_bytes=64, offset=2 * H - SHOTS // 2 * (1 - half))
            nc.vector.tensor_copy(picked[:], tab_rows[:].indirect(list_half(half)))
            return picked

        def place_scales(half, picked):
            nc.vector.tensor_copy(v_planes[half].bitcast(I32), picked[:].bitcast(I32))

        nc.vector.tensor_copy(
            wp_plane.rearrange("p (g t m) -> p g t m", g=GROUPS, t=PACK),
            wp_rows[:].rearrange("p (g m t) -> p g t m", g=GROUPS, t=PACK),
        )
        place_scales(0, look_up_scales(0))
        place_scales(1, look_up_scales(1))
        wp_codes = head.tile([P, 2 * H], U8, name="wp_codes", align_bytes=64, offset=0)
        nc.vector.tensor_copy(
            wp_codes[:].bitcast(U16).rearrange("p (g t m) -> p g t m", g=GROUPS, t=PACK),
            wp_raw[:].bitcast(U16).rearrange("p (g m t) -> p g t m", g=GROUPS, t=PACK),
        )

        wa_raw, w3_raw, v_codes = {}, {}, []

        def load_wa(part):
            g, c0, width = WA_PARTS[part]
            wa_raw[part] = sb("wa_raw%d" % part, [P, PACK, width], F32)[:]
            src = wa[:, g * PASS + c0:g * PASS + c0 + width].rearrange("(p j) c -> p j c", j=PACK)
            nc.sync.dma_start(wa_raw[part], src)

        def load_w3(g):
            if g == 0:
                w3_raw[g] = placed.tile([P, PACK, N], F32, name="w3_raw0", align_bytes=64, offset=W3_FIRST_AT)
            else:
                w3_raw[g] = sb("w3_raw%d" % g, [P, PACK, N], F32)
            nc.sync.dma_start(w3_raw[g][:], w3[g * PASS:(g + 1) * PASS, :].rearrange("(p j) n -> p j n", j=PACK))

        load_wa(0)
        seat_scale_rows(first_planes)
        nc.sync.dma_start(phi_sb[:, :, :PACK], phi.rearrange("(g p t) -> p g t", g=GROUPS, t=PACK))
        load_wa(1)
        load_wa(2)
        load_wa(3)
        load_wa(4)
        load_w3(0)
        seat_scale_rows(later_planes)
        load_w3(1)
        w4_codes = sb("w4_codes", [P, N], U32)
        nc.sync.dma_start(w4_codes[:].bitcast(I32), w4_words[0].rearrange("p c i -> p (c i)").bitcast(I32))
        amp_sb = sb("amp_sb", [P, BLOCKS, 1], F32)
        with nc.allow_non_contiguous_dma(reason="one value for each partition and row block"):
            nc.sync.dma_start(amp_sb[:, :, 0], amp.rearrange("(i p) -> p i", p=P))
        for half in range(HALVES):
            picked = sb("v_codes%d" % half, [P, SHOTS], U32)
            nc.vector.tensor_copy(picked[:], tab[:].indirect(list_half(half)))
            v_codes.append(picked)

        def shot_range(half):
            return slice(half * SHOTS, (half + 1) * SHOTS)

        def product(out, lhsT, rhs, start=True, stop=True):
            nc.tensor.matmul_mx(
                out=out[:], lhsT=lhsT[0], lhsT_scale=lhsT[1], rhs=rhs[0], rhs_scale=rhs[1], start=start, stop=stop
            )

        def picked_shots(half):
            return v_codes[half][:].bitcast(FP8X4), v_planes[half]

        weight_codes, weight_planes, staged = {}, {}, {}

        def stage(name, index, first=0, width=SHOTS, tag=None, at=None):
            label = "%s_bf%d_%d" % (name, index, first)
            if at is None:
                staged[name, index, first] = sb(label, [P, PACK * width], BF16, tag=tag)[:]
            else:
                staged[name, index, first] = placed.tile(
                    [P, PACK * width], BF16, name=label, align_bytes=64, offset=at
                )[:]

        def round_wa(part):
            g, c0, width = WA_PARTS[part]
            dealt = staged["wa", g, 0].rearrange("p (t m u w) -> p m u t w", t=PACK, u=2, w=2)
            (nc.scalar.copy if part == 0 else nc.vector.tensor_copy)(
                dealt[:, c0 // PACK:(c0 + width) // PACK],
                wa_raw[part].rearrange("p (u w) (m t) -> p m u t w", w=2, t=PACK),
            )

        def interleave(copy, rounded, rows):
            copy(
                rounded.rearrange("p (c i u w) -> p c u i w", i=2, u=2, w=2),
                rows.rearrange("p (u w) (c i) -> p c u i w", i=2, w=2),
            )

        def on_vector(rounded, rows):
            interleave(nc.vector.tensor_copy, rounded, rows)

        def on_scalar(rounded, rows):
            interleave(nc.scalar.copy, rounded, rows)

        def on_gpsimd(rounded, rows):
            nc.gpsimd.tensor_scalar(
                rounded.rearrange("p (c t) -> p c t", t=PACK), rows.rearrange("p t c -> p c t"),
                1.0, 1.0, ALU.mult, ALU.mult,
            )

        h_rows = {}

        def round_columns(name, index, how, c0=0, c1=SHOTS, first=0):
            rows = w3_raw[index][:] if name == "w3" else h_rows[index]
            how(staged[name, index, first][:, PACK * (c0 - first):PACK * (c1 - first)], rows[:, :, c0:c1])

        def quantise_weight(name, g, c0=0, c1=PASS, first=0):
            if (name, g) not in weight_codes:
                weight_codes[name, g] = sb("%s_codes%d" % (name, g), [P, PASS], U32)
                weight_planes[name, g] = sb("%s_plane%d" % (name, g), [P, PASS], U8)
            nc.vector.quantize_mx(
                out=weight_codes[name, g][:, c0:c1].bitcast(FP8X4), scales=weight_planes[name, g][:, c0:c1],
                in_=staged[name, g, first][:, PACK * (c0 - first):PACK * (c1 - first)],
            )

        def stationary(name, g, block):
            cols = slice(block * P, (block + 1) * P)
            return weight_codes[name, g][:, cols].bitcast(FP8X4), weight_planes[name, g][:, cols]

        h_planes = [sb("h_plane%d" % half, [P, GROUPS, SHOTS], U8) for half in range(HALVES)]
        h_codes = [sb("h_codes%d" % g, [P, S], U32) for g in range(GROUPS)]
        folded, cosines, pending = {}, {}, {}

        def phase(u, t):
            half, g = divmod(u, GROUPS)
            col = g * PASS + t * P
            out = bank("phase", PHASE_BANKS[t] if u > 0 else t)
            if t == 0:
                folded[u] = ring.tile([P, PACK, SHOTS], F32, name="folded", bufs=2)
            lhsT = wp_codes[:, 2 * col:2 * (col + P)].bitcast(FP4X4), wp_plane[:, col:col + P]
            product(out, lhsT, picked_shots(half))
            nc.scalar.activation(folded[u][:, t, :], out[:], ACT.Abs, bias=phi_sb[:, g, t:t + 1])

        def cosine(u, t0, t1):
            if t0 == 0:
                cosines[u] = placed.tile(
                    [P, PACK, SHOTS], F32, name="cos%d" % u, align_bytes=64, offset=COS_AT[u]
                )
            nc.scalar.activation(
                cosines[u][:, t0:t1, :], folded[u][:, t0:t1, :], ACT.Sin, bias=math.pi / 2, scale=-1.0
            )

        def feature(u, t):
            half, g = divmod(u, GROUPS)
            if t == 0 and u in H_AT:
                h_rows[u] = placed.tile([P, PACK, SHOTS], F32, name="h%d" % u, align_bytes=64, offset=H_AT[u])[:]
            elif t == 0:
                h_rows[u] = sb("h%d" % u, [P, PACK, SHOTS], F32)[:]
            ampl = bank("ampl", AMPL_BANKS[t] if u > 0 else PACK + t)
            product(ampl, stationary("wa", g, t), picked_shots(half))
            nc.vector.tensor_tensor(h_rows[u][:, t, :], cosines[u][:, t, :], ampl[:], ALU.mult)
            rows = out_1[g * PASS:(g + 1) * PASS, :].rearrange("(p t) j -> p t j", t=PACK)
            per = 1 if u == UNITS - 1 else 2
            if (t + 1) % per == 0:
                nc.sync.dma_start(rows[:, t + 1 - per:t + 1, shot_range(half)], h_rows[u][:, t + 1 - per:t + 1, :])

        def step(u, t):
            n = PACK * u + t + 1
            if n < PACK * UNITS:
                phase(*divmod(n, PACK))
            if u == 0 or (u % 2 == 1 and t >= 2):
                cosine(u, t, t + 1)
            elif t % 2 == 0:
                cosine(u, t, t + 2)
            feature(u, t)

        def unit(u):
            for t in range(PACK):
                step(u, t)

        def quantise_h(u, c0=0, c1=SHOTS):
            half, g = divmod(u, GROUPS)
            shots = slice(half * SHOTS + c0, half * SHOTS + c1)
            nc.vector.quantize_mx(
                out=h_codes[g][:, shots].bitcast(FP8X4), scales=h_planes[half][:, g, c0:c1],
                in_=staged["h", u, 0][:, PACK * c0:PACK * c1],
            )

        def store_codes(g, shots):
            words = out_2[g].rearrange("p m t -> p (m t)").bitcast(I32)
            nc.sync.dma_start(words[:, shots], h_codes[g][:, shots].bitcast(I32))

        def store_scale_rows(half):
            for r in range(4):
                nc.sync.dma_start(
                    out_3[:, r:16:4, shot_range(half)].rearrange("g q m -> q g m").bitcast(I32),
                    h_planes[half][r:P:32].bitcast(I32),
                )

        y_rows = [sb("y%d" % half, [P, BLOCKS, SHOTS], F32) for half in range(HALVES)]

        def response(half, i):
            resp = bank("resp", RESP_BANKS[half][i])
            for g in range(GROUPS):
                rhs = h_codes[g][:, shot_range(half)].bitcast(FP8X4), h_planes[half][:, g, :]
                product(resp, stationary("w3", g, i), rhs, start=(g == 0), stop=(g == GROUPS - 1))
            if half == 0 and i > 0:
                sine = placed.tile(
                    [P, SHOTS], F32, name="sine%d" % i, align_bytes=64, offset=COS_AT[UNITS - 1] + i * UNIT_BYTES // PACK
                )
            else:
                sine = ring.tile([P, SHOTS], F32, name="sine", bufs=BLOCKS + 1)
            nc.scalar.activation(sine[:], resp[:], ACT.Sin)
            pending[half, i] = sine

        def result(half, i):
            sine, lin = pending[half, i], bank("lin", LIN_BANKS[half][i])
            cols = slice(i * P, (i + 1) * P)
            product(lin, (w4_codes[:, cols].bitcast(FP8X4), w4_plane[:, cols]), picked_shots(half))
            nc.vector.scalar_tensor_tensor(y_rows[half][:, i, :], sine[:], amp_sb[:, i, :], lin[:], ALU.mult, ALU.add)

        def store_results(half, i0, i1):
            rows = out_0[:, shot_range(half)].rearrange("(i p) j -> p i j", p=P)
            nc.sync.dma_start(rows[:, i0:i1, :], y_rows[half][:, i0:i1, :])

        stage("wa", 0)
        round_wa(0)
        round_wa(1)
        round_wa(2)
        quantise_weight("wa", 0, 0, P)
        quantise_weight("wa", 0, P, PASS)
        stage("wa", 1)
        round_wa(3)
        phase(0, 0)
        step(0, 0)
        step(0, 1)
        round_wa(4)
        step(0, 2)
        quantise_weight("wa", 1)
        step(0, 3)

        first_stage = sb("first_stage", [P, PACK * SHOTS], BF16)
        staged["h", 0, 0] = first_stage[:]
        staged["w3", 0, 0] = first_stage[:, PACK * MID:]
        round_columns("w3", 0, on_vector, 0, MID)
        round_columns("h", 0, on_vector, 0, CUT)
        stage("w3", 0, MID, N - MID)
        round_columns("w3", 0, on_vector, MID, N, MID)
        quantise_weight("w3", 0, 0, MID)
        quantise_weight("w3", 0, MID, N, MID)
        round_columns("h", 0, on_gpsimd, CUT, SHOTS)
        unit(1)

        quantise_h(0)
        store_codes(0, shot_range(0))
        second_stage = placed.tile(
            [P, PACK * (MID + SHOTS)], BF16, name="second_stage", align_bytes=64, offset=SECOND_JOB_AT
        )
        staged["w3", 1, 0] = second_stage[:, :PACK * N]
        staged["h", 1, 0] = second_stage[:, PACK * MID:]
        round_columns("h", 1, on_vector)
        round_columns("w3", 1, on_vector, 0, CUT)
        quantise_h(1, 0, MID)
        quantise_h(1, MID, SHOTS)
        store_codes(1, shot_range(0))
        store_scale_rows(0)
        round_columns("w3", 1, on_gpsimd, CUT, N)
        unit(2)

        quantise_weight("w3", 1)
        stage("h", 2, at=SECOND_JOB_AT)
        round_columns("h", 2, on_gpsimd, SCALAR_SHOTS[2], SHOTS)
        unit(3)

        response(0, 0)
        round_columns("h", 2, on_scalar, 0, SCALAR_SHOTS[2])
        result(0, 0)
        store_results(0, 0, 1)
        stage("h", 3)
        round_columns("h", 3, on_scalar, SHOTS - SCALAR_SHOTS[3], SHOTS)
        round_columns("h", 3, on_vector, 0, SHOTS - SCALAR_SHOTS[3])
        quantise_h(2)
        store_codes(0, shot_range(1))
        quantise_h(3)
        store_codes(1, shot_range(1))
        store_scale_rows(1)
        response(0, 1)
        result(0, 1)
        store_results(0, 1, 2)
        for i in (2, 3):
            response(0, i)
        for i in (2, 3):
            result(0, i)
            store_results(0, i, i + 1)
        for i in range(BLOCKS):
            response(1, i)
        for i in range(BLOCKS):
            result(1, i)
            store_results(1, i, i + 1)
